import numpy as np, ml_dtypes
CORES = [10,34,74,98]
N = 4
BF = ml_dtypes.bfloat16
def gentries(a):
    return np.ascontiguousarray(a.reshape(8, 16, -1).transpose(0, 2, 1)).reshape(8, -1)
def gtable(e):
    e = np.asarray(e); return np.ascontiguousarray(e.reshape(8, -1, 16).transpose(0, 2, 1)).reshape(128, -1).astype(np.int32)
R0, P0, S, L, RO = 6144, 416, 32, 14, 3
P = P0 + RO * S; R = R0 + RO * (N - 1) * S
def counts(rng, share):
    return np.where(rng.random((N, 8, P0)) < share, rng.integers(L, 17, (N, 8, P0)), rng.integers(1, L, (N, 8, P0)))
def world(rng, cnt):
    post = rng.integers(0, R0, (N, 8, P0, 16)); home = np.full((N, 8, R0), 65535)
    on = np.argsort(rng.random((N, 8, P0, 16)), axis=-1) < cnt[..., None]
    for q in range(N):
        for g in range(8):
            ix = np.flatnonzero(on[q, g])[:R0]; c = rng.permutation(R0); n = len(ix)
            post[q, g].reshape(-1)[ix] = c[:n]; home[q, g, c[:n]] = ix
            if n: home[q, g, c[n:]] = np.where(rng.random(R0 - n) < 0.5, 65535, ix[rng.integers(0, n, R0 - n)])
    cl = rng.integers(0, 24, (N, 8, P0)); pr = rng.integers(40, 200, (8, 24, 14)); gi = np.arange(8)[None, :, None]
    at = np.minimum(home >> 4, P0 - 1)
    kc = np.where(home == 65535, rng.integers(0, 24, home.shape), np.take_along_axis(cl, at, 2))
    x = np.clip(pr[gi, kc] + rng.integers(-40, 41, (N, 8, R0, 14)), 0, 255)
    cen = rng.integers(0, 256, (N, 8, P0, 16)); cen[..., :14] = pr[gi, cl] + rng.integers(-16, 17, (N, 8, P0, 14))
    m = N * P0; w = m // 24; od = np.argsort(cl.transpose(1, 0, 2).reshape(8, m) + rng.random((8, m)), axis=1); pos = np.argsort(od, axis=1)
    z = np.take_along_axis(od, ((pos[:, :, None] + rng.integers(-w, w + 1, (8, m, 16))) % m).reshape(8, 16 * m), 1)
    near = (P * (z // P0) + z % P0).reshape(8, N, P0, 16).transpose(1, 0, 2, 3)
    near = np.where(rng.random(near.shape) < 0.15, rng.integers(0, N * P, near.shape), near)
    sl = 16 * at[:, :, None, :] + rng.integers(0, 16, (N, 8, RO, R0))
    ab = np.take_along_axis(post.reshape(N, 8, 16 * P0), sl.reshape(N, 8, RO * R0), 2).reshape(N, 8, RO, R0); u = rng.random(ab.shape)
    ab = np.where(u < 0.3, np.arange(R0), np.where(u < 0.5, rng.integers(0, R, ab.shape), ab))
    return {"x": x, "home": home, "cen": cen, "post": post, "near": near, "ab": ab}
def pack(d):
    h = d["home"][..., None]; v = np.concatenate([d["x"], h >> 8, h & 255], axis=-1).astype(np.float32)
    def turn(a): return np.ascontiguousarray(a.transpose(0, 1, 3, 2)).reshape(N, 128, -1)
    return {"rec": turn(v).astype(BF), "post": turn(d["post"]).astype(np.int32), "cen": turn(d["cen"].astype(np.float32)).astype(BF), "near": turn(d["near"]).astype(np.int32),
            "absorb": np.stack([gtable(a.reshape(8, -1)) for a in d["ab"]])}
def setup_inputs(rng):
    return pack(world(rng, counts(rng, rng.choice(np.array([0.2, 0.4, 0.6]), (N, 8, 1)))))
def setup_inputs_room(rng):
    nf = rng.choice(np.array([0, 1, S - 1, S, S + 1, 3 * S]), (N, 8)); nf[0] = (S, S + 1, S - 1, 0, 1, 3 * S, S, 2 * S); nf[1, 0] = S
    fm = np.argsort(rng.random((N, 8, P0)), axis=-1) < nf[..., None]
    cnt = np.where(fm, rng.choice(np.array([L, 16]), fm.shape), np.where(rng.random(fm.shape) < 0.5, L - 1, rng.integers(1, L, fm.shape)))
    d = world(rng, cnt); d["x"][:, 0] = rng.integers(128, 256, (N, R0, 14)); d["cen"][:, 0, :, :14] = 0
    fp = np.flatnonzero(fm[1, 0]); fq = np.flatnonzero(~fm[0, 0])
    d["near"][0, 0, fq] = (P + fp[np.arange(len(fq)) % S])[:, None]
    return pack(d)
def setup_inputs_ties(rng):
    cnt = counts(rng, 0.5); cnt[:, :, :6] = 16
    d = world(rng, cnt); d["x"] = rng.integers(0, 3, (N, 8, R0, 14)); d["cen"][..., :14] = rng.integers(0, 3, (N, 8, P0, 14))
    d["x"][:, 0] = 7; d["cen"][:, 0, :, :14] = np.where(rng.random((N, P0, 1)) < 0.5, 7, rng.integers(5, 9, (N, P0, 14)))
    d["x"][:, 2] *= rng.random((N, R0, 1)) < 0.5; d["cen"][:, 2, :, :14] = rng.integers(5, 9, (N, P0, 14))
    d["ab"][:, :4] = np.arange(R0)
    d["near"][:, 1::2] = P * rng.integers(0, N, (N, 4, P0, 16)) + rng.integers(0, 6, (N, 4, P0, 16))
    return pack(d)
def setup_inputs_ends(rng):
    q = rng.permutation(N); cnt = counts(rng, 0.3); cnt[q[0]] = rng.integers(0, L, (8, P0)); cnt[q[1]] = L
    ch = rng.permutation(P0)[:5]; cnt[:, 3] = rng.integers(1, L, (N, P0)); cnt[:, 3, ch] = 16
    cnt[:, 4] = rng.integers(1, L, (N, P0)); cnt[:, 4, 0] = 16; cnt[:, 4, P0 - 1] = L
    d = world(rng, cnt); ab = d["ab"]; near = d["near"]; d["cen"][:, 3, :, :14] = 0
    ab[:, 1] = rng.choice(np.array([0, R0 - 1]), (N, RO, R0)); ab[:, 2] = rng.integers(R0, R, (N, RO, R0)); ab[:, 5] = rng.integers(0, R0, (N, 1, 1)); ab[:, 3] = np.arange(R0)
    near[:, 4] = P * rng.integers(0, N, (N, P0, 16)) + rng.choice(np.array([0, P0 - 1, P0, P - 1]), (N, P0, 16))
    near[:, 3] = P * rng.integers(0, N, (N, P0, 16)) + np.where(rng.random((N, P0, 16)) < 0.5, P0 + rng.integers(0, 5, (N, P0, 16)), ch[rng.integers(0, 5, (N, P0, 16))])
    for a in range(N):
        s = d["post"][a, 3, ch]; d["x"][a, 3, s[:, 0]] = 0; d["x"][a, 3, s[:, 1:].reshape(-1)] = rng.integers(200, 256, (75, 14))
    return pack(d)
def setup_inputs_sharp(rng):
    d = world(rng, counts(rng, 0.4)); E = N * S - 32; n = P0 - S; i = np.arange(n)
    tg = np.where(i < n - 32, i % E, E + i - (n - 32))
    for g in range(0, 8, 2):
        fs = [np.sort(rng.permutation(P0)[:S]) for q in range(N)]; to = np.concatenate([P * q + fs[q] for q in range(N)])
        for q in range(N):
            fp = fs[q]; fq = np.setdiff1d(np.arange(P0), fp); po = d["post"][q, g]
            dull = (rng.random(n) < 0.5) & ((i < E) | ((i >= 2 * E) & (i < n - 32)))
            z = int(np.flatnonzero(tg == q * S)[0]); dull[z] = False
            cnt = np.zeros(P0, np.int64); cnt[fp] = rng.integers(L, 16, S); cnt[fq] = rng.integers(1, 5, n); cnt[fq[z]] = 1
            key = rng.random((P0, 16)); key[fp, 0] = 2
            on = np.argsort(np.argsort(key, axis=1), axis=1) < cnt[:, None]
            ix = np.flatnonzero(on); m = len(ix); c = 1 + rng.permutation(R0 - 1); dead = c[m:]; low = dead[:len(dead) // 2]; high = dead[len(dead) // 2:]
            po[fp] = rng.choice(high, (S, 16)); po[fq] = rng.choice(low, (n, 16))
            po[on] = c[:m]; po[fq[z], int(np.argmax(on[fq[z]]))] = 0
            h = np.where(rng.random(R0) < 0.5, 65535, ix[rng.integers(0, m, R0)]); h[po[on]] = ix; d["home"][q, g] = h
            x = rng.integers(130, 201, (R0, 14)); x[low] = 0; x[high] = 255
            e = fp[::2]; x[po[e][on[e]]] = 0
            e = fp[1::2]; s = po[e][on[e]]; x[s] = rng.integers(0, 3, (len(s), 14))
            e = fq[~dull]; x[po[e][on[e]]] = 127
            d["x"][q, g] = x; d["cen"][q, g, fq, :14] = 255; d["ab"][q, g, 0] = np.arange(R0)
            d["near"][q, g, fq] = np.where(np.arange(16) < rng.integers(0, 15, (n, 1)), (P * q + fq)[:, None], to[tg][:, None])
    return pack(d)
def setup_inputs_spread(rng):
    d = world(rng, counts(rng, rng.random((N, 8, 1))))
    d["x"] = np.minimum((np.exp2(8 * rng.random((N, 8, R0, 1))) * rng.random((N, 8, R0, 14))).astype(np.int64), 255)
    d["cen"] = rng.integers(0, 256, (N, 8, P0, 16)) >> rng.integers(0, 8, (N, 8, P0, 1))
    d["near"] = rng.integers(0, N * P, (N, 8, P0, 16)); d["ab"] = rng.integers(0, R, (N, 8, RO, R0))
    return pack(d)
def check_inputs(d):
    bad = []
    for k, hi in (("rec", 255), ("cen", 255), ("post", R0 - 1), ("near", N * P - 1), ("absorb", R - 1)):
        v = np.asarray(d[k]).astype(np.float64)
        if not (np.min(v) >= 0 and np.max(v) <= hi) or np.any(v != np.floor(v)): bad.append("range of " + k)
    v = np.asarray(d["rec"]).astype(np.float64).reshape(N, 8, 16, R0); h = v[:, :, 14] * 256 + v[:, :, 15]
    if np.any((h >= 16 * P0) & (h != 65535)): bad.append("homes of rec")
    return bad
def reference(rec, post, cen, near, absorb):
    w = rec.astype(np.float32).astype(np.int32).reshape(N, 8, 16, R0)
    x = np.zeros((N, 8, 14, R), np.int32); x[..., :R0] = w[:, :, :14]
    home = np.full((N, 8, R), 65535, np.int64); home[..., :R0] = w[:, :, 14] * 256 + w[:, :, 15]
    po = np.zeros((N, 8, P, 16), np.int64); po[:, :, :P0] = post.reshape(N, 8, 16, P0).transpose(0, 1, 3, 2)
    ne = np.zeros((N, 8, P, 16), np.int64); ne[:, :, :P0] = near.reshape(N, 8, 16, P0).transpose(0, 1, 3, 2)
    ce = np.zeros((N, 8, 14, P), np.int32); ce[..., :P0] = cen.astype(np.float32).astype(np.int32).reshape(N, 8, 16, P0)[:, :, :14]
    al = np.stack([gentries(a) for a in absorb]).astype(np.int64).reshape(N, 8, RO, R0)
    for t in range(RO):
        new = P0 + S * t
        for q in range(N): x[q, :, :, :R0] = np.maximum(x[q, :, :, :R0], np.take_along_axis(x[q], al[q, :, t][:, None, :], 2))
        live = (np.take_along_axis(home, po.reshape(N, 8, 16 * P), 2) == np.arange(16 * P)).reshape(N, 8, P, 16)
        full = (np.add.reduce(live.astype(np.int64), axis=3) >= L).astype(np.int64)
        num = np.add.accumulate(full, axis=2) - full; sp = (full == 1) & (num < S)
        b = np.zeros((N, 8, S, 14), np.int32); row = np.zeros((N, 8, S), np.int64)
        for q in range(N):
            for g in range(8):
                for k, p in enumerate(np.flatnonzero(sp[q, g])):
                    f = new + k; ix = po[q, g, p].copy(); v = x[q, g][:, ix]; on = live[q, g, p]
                    va = v[:, np.argmax(on)]; da = np.add.reduce(np.abs(v - va[:, None]), axis=0)
                    vb = v[:, np.argmax(np.where(on, da, -1))]; db = np.add.reduce(np.abs(v - vb[:, None]), axis=0)
                    go = on & (db < da)
                    po[q, g, f] = ix; ne[q, g, f] = ne[q, g, p]; ce[q, g, :, p] = va; ce[q, g, :, f] = vb
                    home[q, g, ix[go]] = 16 * f + np.flatnonzero(go)
                    b[q, g, k] = vb; row[q, g, k] = np.argmin(go)
        tab = np.where(sp, num + S * np.arange(N)[:, None, None], -1).transpose(1, 0, 2).reshape(8, N * P)
        mov = np.full((N, 8, N * S), -1, np.int64)
        for q in range(N):
            tj = np.take_along_axis(tab, ne[q].reshape(8, 16 * P), 1).reshape(8, P, 16)
            tg = np.take_along_axis(tj, np.argmax(tj >= 0, axis=2)[:, :, None], 2)[:, :, 0]
            for g in range(8):
                Q = np.flatnonzero((tg[g] >= 0) & ~sp[q, g]); v = x[q, g][:, po[q, g, Q]]
                vb = b[:, g].reshape(N * S, 14).T[:, tg[g, Q]]
                gain = np.add.reduce(np.abs(v - ce[q, g][:, Q][:, :, None]), axis=0) - np.add.reduce(np.abs(v - vb[:, :, None]), axis=0)
                gain = np.where(live[q, g, Q], gain, 0); m = np.argmax(gain, axis=1); ok = np.any(gain > 0, axis=1)
                Q = Q[ok]; m = m[ok]; u, i = np.unique(tg[g, Q], return_index=True)
                mov[q, g, u] = po[q, g, Q[i], m[i]]
        for r in range(N):
            win = mov[r, :, r * S:(r + 1) * S].copy()
            for o, q in enumerate([a for a in range(N) if a != r]):
                c = mov[q, :, r * S:(r + 1) * S]; e = R0 + ((N - 1) * t + o) * S
                x[r, :, :, e:e + S] = np.where((c >= 0)[:, None, :], np.take_along_axis(x[q], np.maximum(c, 0)[:, None, :], 2), 0)
                gg, kk = np.nonzero(c >= 0); home[q, gg, c[gg, kk]] = 65535
                win = np.where((win < 0) & (c >= 0), e + np.arange(S), win)
            gg, kk = np.nonzero(win >= 0); m = row[r, gg, kk]
            home[r, gg, win[gg, kk]] = 16 * (new + kk) + m; po[r, gg, new + kk, m] = win[gg, kk]
    hh = np.stack([home >> 8, home & 255], axis=2)
    ya = np.concatenate([x[..., R0:], hh[..., R0:].astype(np.int32)], axis=2).reshape(N, 128, R - R0)
    return {"ypost": np.ascontiguousarray(po.transpose(0, 1, 3, 2)).reshape(N, 128, P).astype(np.float32),
            "yh": hh[..., :R0].reshape(N, 16, R0).astype(np.float32).astype(BF), "ya": ya.astype(np.float32).astype(BF)}

@@ -1,0 +1,747 @@
+from concourse.bass import DstId, RemoteDMATransfer
+from concourse.mybir import AluOpType as Op, AxisListType as Ax, ActivationFunctionType as Fn
+
+R0, P0, SP, RO = 6144, 416, 32, 3
+R = R0 + 96 * RO
+PD = 512
+MD = 544
+WP = 672
+XW = 16 * WP
+TS = 544
+BIG = 262144.0
+SU1, SU2 = 15, 12
+LEAD, LAG = 5, 4
+HQ = (112, 224)
+VQ = (64, 128)
+AB = [128, 192, 64]
+
+SCRATCH = {}
+ALIAS = {}
+OWN = ("plr", "pls", "bw", "bs", "mf", "arr", "p0", "p1", "p2", "p3", "p4", "p5", "p6", "p7")
+
+
+def _b(names, w, dt="bfloat16", where="sbuf"):
+    for name in names.split():
+        if w > 100 or name.startswith(OWN):
+            SCRATCH[name] = (where, [128, w], dt)
+        else:
+            pool = "small_" + dt
+            o = SCRATCH.get(pool, ("", [0, 0]))[1][1]
+            ALIAS[name] = (pool, o, w)
+            SCRATCH[pool] = ("sbuf", [128, o + (w + 15) // 16 * 16], dt)
+
+
+F, I, U = "float32", "int32", "uint16"
+_b("x1 x2", R)
+_b("hh", R + 512)
+_b("xd", R0)
+_b("xg", XW)
+_b("ng mc md", 16 * 480)
+_b("e16 rmp rx nm hm vnm", 2048)
+_b("e16f", 2048, F)
+_b("postI nearI nsh", P0, I)
+_b("abI", 1152, I)
+_b("ab16", 1152, U)
+_b("post16 near16", 512, U)
+_b("postf nearf", WP, F)
+_b("slot", P0, F)
+_b("ctr live", WP)
+for _t in range(RO):
+    _b("tab%d" % _t, 4 * TS)
+    _b("plr%d" % _t, 6, U)
+    _b("pls%d" % _t, 2, U)
+    _b("bw%d" % _t, 144)
+    _b("bs%d" % _t, 32)
+    _b("mf%d" % _t, 128)
+    _b("arr%d" % _t, 96)
+    _b("atab%d" % _t, 96, F)
+    _b("vst%d" % _t, 512)
+_b("full scan sd1 junk", TS)
+_b("cmpv", TS + 2)
+_b("cidx", TS, F)
+_b("ident nid ibig bo bo14c bo14b bo14p bo14n px mw mw15 one0 lga u128 w128 w128b vm oh lgt lut dat", 128)
+_b("bof zx pg pgm", 128, F)
+_b("lg", 1024)
+_b("ones n15 ck cka ckb wt tq ff xs xs2 ma mb vhi vlo", 512)
+_b("bt", 480)
+_b("kt k1", 256, F)
+_b("k2", 128, F)
+_b("k3", 64, F)
+_b("fc", 64, F)
+_b("km kmf i32k dg tr whi postp nearp laf lbf ktk spa spb ownv ra wv wb wd hd fo", 32, F)
+_b("kmi kma wi wr", 32, I)
+_b("k16 lp oa obt ob go nog rw rwf wf ac lpn hw z32", 32)
+_b("g8 rgp rgn", 8)
+_b("miw", 16)
+_b("pcol pr", 2, I)
+_b("i16 r16", 16, F)
+_b("i8 cs ms", 8, F)
+_b("acc lac_f lbc_f kmx", 2, F)
+_b("pl16 lac lbc", 2, U)
+_b("la16 ps16 lb16 spl16 tgl", 32, U)
+_b("ls16 lq16 lm16 rl16", 8, U)
+_b("lsi lqi lmi", 8, I)
+_b("fa eq", 96, F)
+_b("ya1 ya2 ya3", 288)
+for _i in range(8):
+    _b("p%d" % _i, 512, F, "psum")
+
+NDMA = 16
+SEMAPHORES = ["qv", "qs", "qp", "qg", "sent"] + ["d%d" % i for i in range(NDMA)] + \
+    ["%s%d" % (a, t) for a in ("rp", "rb", "rm") for t in range(RO)]
+
+
+def rank_program(g, core, T, topo):
+    r = T.rank_of(core)
+    if r is None:
+        return
+    Q = {"v": g.vector, "s": g.scalar, "p": g.tensor, "g": g, "y": g.sync}
+    cnt = {"qv": 0, "qs": 0, "qp": 0, "qg": 0}
+    total = {}
+    known = {q: {} for q in Q}
+    acc = {}
+    dn = [0]
+
+    def waits(q, toks):
+        need = {}
+        for (sem, val, q2, snap) in toks:
+            if known[q].get(sem, 0) < val and (sem not in need or need[sem][1] < val):
+                need[sem] = (sem, val, q2, snap)
+        lst = list(need.values())
+        for tk in lst:
+            if any(o is not tk and o[3].get(tk[0], 0) >= tk[1] for o in lst):
+                continue
+            Q[q].wait_ge(T.sem[tk[0]], tk[1])
+        for tk in lst:
+            k = known[q]
+            k[tk[0]] = max(k.get(tk[0], 0), tk[1])
+            for s2, v2 in tk[3].items():
+                if k.get(s2, 0) < v2:
+                    k[s2] = v2
+
+    def deps(q, reads, writes):
+        toks = []
+        for is_w, regs in ((False, reads), (True, writes)):
+            for (b, c0, c1) in regs:
+                ps = SCRATCH.get(b, ("",))[0] == "psum"
+                for (d0, d1, w2, tok) in acc.get(b, ()):
+                    if ps:
+                        if tok[2] == q and (q == "p" or not (is_w or w2)):
+                            continue
+                        toks.append(tok)
+                    elif d0 < c1 and c0 < d1 and (is_w or w2):
+                        toks.append(tok)
+        return toks
+
+    def note(reads, writes, tok):
+        for (b, c0, c1) in writes:
+            ps = SCRATCH.get(b, ("",))[0] == "psum"
+            old = acc.get(b, [])
+            acc[b] = [o for o in old if not (ps or (c0 <= o[0] and o[1] <= c1))] + [(c0, c1, True, tok)]
+        for (b, c0, c1) in reads:
+            old = acc.get(b, [])
+            acc[b] = [o for o in old if not (not o[2] and o[3][2] == tok[2] and o[3][0] == tok[0] and c0 <= o[0] and o[1] <= c1)] + [(c0, c1, False, tok)]
+
+    def run(q, fn, reads, writes):
+        waits(q, deps(q, reads, writes))
+        sem = "q" + q
+        cnt[sem] += 1
+        total[sem] = cnt[sem]
+        fn().then_inc(T.sem[sem], 1)
+        note(reads, writes, (sem, cnt[sem], q, dict(known[q])))
+
+    def dma(q, out, in_):
+        waits(q, deps(q, in_[1], out[1]))
+        sem = "d%d" % dn[0]
+        dn[0] += 1
+        Q[q].dma_start(out[0], in_[0]).then_inc(T.sem[sem], 16)
+        total[sem] = 16
+        note(in_[1], out[1], (sem, 16, "dma", dict(known[q])))
+
+    def v(b, c0=0, c1=None, s=1):
+        if b in ALIAS:
+            b, o, w = ALIAS[b]
+            c0, c1 = o + c0, o + (w if c1 is None else c1)
+        c1 = SCRATCH[b][1][1] if c1 is None else c1
+        return (T[b][:, c0:c1] if s == 1 else T[b][:, c0:c1:s], [(b, c0, c1)])
+
+    def part(b, n, c0, c1, s):
+        return (T[b][0:n, c0:c1] if s == 1 else T[b][0:n, c0:c1:s], [(b, c0, c1)])
+
+    def ind(win, off):
+        return (win[0].indirect(off[0]), win[1] + off[1])
+
+    def col(i):
+        return v("fc", i, i + 1)
+
+    def fam(b, m):
+        return v(b, 128 * m, 128 * m + 128)
+
+    def tt(out, a, b, op):
+        run("v", lambda: g.vector.tensor_tensor(out[0], a[0], b[0], op), a[1] + b[1], out[1])
+
+    def ts(out, a, s1, o1, s2=None, o2=None):
+        regs = list(a[1])
+        x1, x2 = s1, s2
+        if isinstance(s1, tuple):
+            regs += s1[1]
+            x1 = s1[0]
+        if isinstance(s2, tuple):
+            regs += s2[1]
+            x2 = s2[0]
+        if o2 is None:
+            run("v", lambda: g.vector.tensor_scalar(out[0], a[0], x1, None, o1), regs, out[1])
+        else:
+            run("v", lambda: g.vector.tensor_scalar(out[0], a[0], x1, x2, o1, o2), regs, out[1])
+
+    def cp(out, a):
+        run("v", lambda: g.vector.tensor_copy(out[0], a[0]), a[1], out[1])
+
+    def scat(win, off, a):
+        run("v", lambda: g.vector.tensor_copy(win[0].indirect(off[0]), a[0]), a[1] + off[1] + win[1], win[1])
+
+    def red(out, a, op, ab=False):
+        kw = {"apply_absolute_value": True} if ab else {}
+        run("v", lambda: g.vector.tensor_reduce(out[0], a[0], Ax.X, op, **kw), a[1], out[1])
+
+    def tr(out, a):
+        run("v", lambda: g.vector.transpose(out[0], a[0]), a[1], out[1])
+
+    def fill(out, c):
+        run("v", lambda: g.vector.memset(out[0], c), [], out[1])
+
+    def act(out, a, fn=Fn.Copy, bias=None, scale=None, accum=None):
+        kw = {}
+        regs = list(a[1])
+        w = list(out[1])
+        if bias is not None:
+            kw["bias"] = bias[0]
+            regs += bias[1]
+        if isinstance(scale, tuple):
+            kw["scale"] = scale[0]
+            regs += scale[1]
+        elif scale is not None:
+            kw["scale"] = scale
+        if accum is not None:
+            kw["accum_out"] = accum[0]
+            w += accum[1]
+        run("s", lambda: g.scalar.activation(out[0], a[0], fn, **kw), regs, w)
+
+    def mm(out, lhsT, rhs, start, stop):
+        run("p", lambda: g.tensor.matmul(out[0], lhsT[0], rhs[0], start, stop), lhsT[1] + rhs[1], out[1])
+
+    def iota(out, pat, base=0, cm=0, flag=True):
+        kw = {"allow_small_or_imprecise_dtypes": True} if flag else {}
+        run("g", lambda: g.iota(out[0], pat, base, cm, **kw), [], out[1])
+
+    others = [q for q in range(len(T.cores)) if q != r]
+    NE = 2
+
+    def send(bufs, dsts, sem):
+        trs = []
+        regs = []
+        for i, q in enumerate(others):
+            dst = T.cores[q]
+            rid, pid, _ = topo.addr(dst)
+            eng = topo.engines(core, dst)[NE * i:NE * i + NE]
+            trs.append(RemoteDMATransfer(dst_ids=[DstId(rid=rid, pnc=pid)], dma_engine_mask=sum(1 << e for e in eng),
+                                         remote_sem=T.sem[sem], srcs=[bufs[i][0]], dsts=[dsts[i][0]]))
+            regs += bufs[i][1]
+        waits("g", deps("g", regs, []))
+        g.remote_dma_fused(trs, local_sem=T.sem["sent"])
+        total["sent"] = total.get("sent", 0) + NE * len(others)
+
+    def arrives(regs, sem):
+        n = NE * len(others)
+        total[sem] = n
+        note([], regs, (sem, n, "remote", {}))
+
+    def place(q):
+        return r - (1 if r > q else 0)
+
+    half = R0 // 2
+    dma("y", v("postI"), (T.post[:, :], []))
+    dma("s", v("hh", 0, half), (T.rec[:, 0:half], []))
+    dma("y", v("hh", half, R0), (T.rec[:, half:R0], []))
+    dma("s", v("abI"), (T.absorb[:, :], []))
+    dma("y", v("nearI"), (T.near[:, :], []))
+    dma("s", v("xd", 0, half), (T.rec[:, 0:half], []))
+    dma("y", v("xd", half, R0), (T.rec[:, half:R0], []))
+    dma("y", v("ctr", 0, P0), (T.cen[:, :], []))
+
+    pI, p15 = v("pcol", 0, 1), v("pcol", 1, 2)
+    NI = v("vnm", 0, 128)
+    R1 = v("md", 0, 2048)
+    iota(pI, [[0, 1]], 0, 1, False)
+    iota(v("vnm"), [[-1, 16], [1, 128]])
+    iota(v("i32k"), [[16, 32]])
+    iota(v("w128"), [[-1, 128]], 128)
+    iota(v("slot"), [[16, P0]])
+    iota(v("whi"), [[8, 4], [0, 8]])
+    iota(v("n15"), [[0, 32], [1, 16]])
+    iota(v("i16"), [[1, 16]])
+    iota(v("i8"), [[16, 8]])
+    iota(v("cidx"), [[1, TS]])
+    iota(v("dg"), [[0, 2], [1, 16]])
+    iota(v("postf", MD, WP), [[1, 128]], R)
+    iota(v("postf", PD, MD), [[0, 32]])
+    iota(v("tab0"), [[0, 4 * TS]])
+    fill(v("hh", R0, R), 0.0)
+    fill(v("live", P0, WP), 0.0)
+    fill(v("full", P0, TS), 0.0)
+    fill(v("cmpv", TS, TS + 2), -544.0)
+    fill(v("ctr", P0, WP), 0.0)
+    fill(v("nearf", P0, WP), 0.0)
+    fill(v("wt"), 0.0)
+    fill(v("ff", P0, 512), 0.0)
+    fill(v("ones"), 1.0)
+    fill(v("z32"), 0.0)
+    PF, MF_, PB = col(0), col(1), col(2)
+    ts(p15, pI, 15, Op.bitwise_and)
+    cp(PF, pI)
+    cp(MF_, p15)
+    tt(PB, PF, MF_, Op.subtract)
+    for i in range(7):
+        ts(col(8 + i), MF_, float(i), Op.is_equal)
+    C14, C15, N14, CF = col(16), col(17), col(18), col(19)
+    ts(C14, MF_, 14.0, Op.is_equal)
+    ts(C15, MF_, 15.0, Op.is_equal)
+    ts(CF, MF_, 13.5, Op.is_le)
+    ts(N14, MF_, 13.5, Op.is_gt)
+    ts(col(20), C14, 256.0, Op.mult, C15, Op.add)
+    K32, KN32, KN16, K16c = col(21), col(22), col(23), col(24)
+    ts(K32, CF, 32.0, Op.mult)
+    ts(KN32, CF, -32.0, Op.mult)
+    ts(KN16, CF, -16.0, Op.mult)
+    ts(K16c, CF, 16.0, Op.mult)
+    HB, HB1 = col(26), col(27)
+    ts(HB, MF_, 0.5, Op.add)
+    ts(HB1, MF_, 16.5, Op.add)
+    ts(v("e16"), v("vnm"), PB, Op.is_equal)
+    act(v("hm"), v("e16"), scale=col(20))
+    cp(v("post16", 0, P0), v("postI"))
+
+    X = v("hh", 0, R)
+    ts(col(37), PF, 0.0, Op.mult, -256.0, Op.add)
+    act(v("slot"), v("slot"), Fn.Identity, bias=MF_)
+    act(R1, v("e16"), Fn.Identity, scale=0.0, bias=col(37))
+    home_parts = ((0, HQ[0], "p5"), (HQ[0], HQ[1], "p2"), (HQ[1], P0, "p6"))
+    for (a, b, pb) in home_parts[0:2]:
+        act(v("xg", 16 * a, 16 * b), ind(X, v("post16", a, b)))
+    ts(v("u128"), NI, PB, Op.subtract)
+    ts(v("px"), v("u128"), 0.0, Op.is_ge)
+    ts(v("w128b"), v("u128"), 15.5, Op.is_le)
+    tt(v("bo"), v("px"), v("w128b"), Op.mult)
+    cp(v("postf", 0, P0), v("postI"))
+    ts(v("g8"), v("i8"), PB, Op.is_equal)
+    act(v("rgp"), v("g8"), scale=K32)
+    act(v("rgn"), v("g8"), scale=KN32)
+    act(v("bo14p"), v("bo"), scale=K16c)
+    act(v("bo14n"), v("bo"), scale=KN16)
+    A, B = col(33), col(34)
+    ts(A, col(12), 32768.0, Op.mult)
+    ts(A, col(14), 16.0, Op.mult, A, Op.add)
+    ts(B, col(8), 32768.0, Op.mult, col(9), Op.add)
+    for (i, w) in ((10, -256.0), (11, -16.0), (12, -32768.0 * 128), (13, -15.0)):
+        ts(B, col(i), w, Op.mult, B, Op.add)
+    ts(v("lga"), NI, A, Op.mult, B, Op.add)
+    for k in range(8):
+        ts(col(40 + k), PB, 16.0 * k, Op.is_equal)
+    for k in range(8):
+        act(v("lg", 128 * k, 128 * k + 128), v("lga"), scale=col(40 + k))
+    cp(v("xg", 16 * HQ[1], 16 * P0), ind(X, v("post16", HQ[1], P0)))
+    for (a, b, pb) in (home_parts[0], home_parts[2], home_parts[1]):
+        for m in range(16):
+            mm(v(pb, a, b), fam("hm", m), v("xg", 16 * a + m, 16 * b, 16), m == 0, m == 15)
+    ts(col(28), MF_, 512.0, Op.add)
+    ts(col(29), MF_, 528.0, Op.add)
+    ts(v("scan"), v("cidx"), col(28), Op.is_ge, 16.0, Op.mult)
+    ts(v("sd1"), v("cidx"), col(29), Op.is_ge, 84.0, Op.mult)
+    tt(v("sd1"), v("sd1"), v("scan"), Op.add)
+    ts(v("ident"), NI, PF, Op.is_equal)
+    ts(v("ibig"), v("ident"), BIG, Op.mult)
+    ts(v("nid"), v("ident"), -1.0, Op.mult)
+    ts(v("w128b"), NI, PF, Op.is_gt, -32.0, Op.mult)
+    tt(v("w128b"), v("w128b"), v("bo"), Op.mult)
+    tt(v("px"), v("w128b"), v("ident"), Op.add)
+    ts(v("mw"), v("bo"), MF_, Op.mult)
+    ts(col(30), PF, 0.0, Op.is_equal)
+    ts(col(31), PF, 1.0, Op.is_equal)
+    ts(col(32), col(30), -BIG, Op.mult)
+    ts(v("one0"), NI, 0.0, Op.mult, col(30), Op.add)
+    cp(v("k16"), v("i32k"))
+    ts(v("dat"), v("w128"), col(8), Op.mult, col(9), Op.add)
+    ts(v("ckb"), v("n15"), -1.0, Op.mult, 15.0, Op.add)
+    ts(v("ckb"), v("ckb"), col(31), Op.mult)
+    ts(v("cka"), v("n15"), 0.0, Op.mult, col(32), Op.add)
+    ts(v("ck"), v("ckb"), col(32), Op.add)
+    ts(v("dg"), v("dg"), MF_, Op.is_equal)
+    for (a, b, pb) in (home_parts[0], home_parts[2], home_parts[1]):
+        tt(v("live", a, b), v("slot", a, b), v(pb, a, b), Op.is_equal)
+
+    def constants_b():
+        ts(v("nsh"), v("nearI"), 4, Op.arith_shift_right, 96, Op.bitwise_and)
+        tt(v("nearf", 0, P0), v("nsh"), v("nearI"), Op.add)
+        cp(v("near16", 0, P0), v("nearf", 0, P0))
+        cp(v("ab16"), v("abI"))
+        act(v("rx"), v("e16"), scale=KN16)
+        act(v("rmp"), v("e16"), scale=K32)
+        act(v("nm"), v("e16"), scale=col(8))
+        run("g", lambda: g.affine_select(R1[0], R1[0], [[-1, 16], [1, 128]], Op.is_gt, 0.0, 1, -1), R1[1], R1[1])
+        run("g", lambda: g.affine_select(R1[0], R1[0], [[0, 16], [-1, 128]], Op.is_gt, 0.0, 15, 1), R1[1], R1[1])
+        dma("y", (T["nm"][1:128:16, :], [("nm", 0, 2048)]), (T["md"][1:128:16, 0:2048], R1[1]))
+
+    def constants_c():
+        ts(v("u128"), v("n15", 0, 128), SU1 - 0.5, Op.is_ge, -2.0, Op.mult)
+        ts(v("u128"), v("u128"), 1.0, Op.add)
+        tt(v("bo14c"), v("u128"), v("bo14n"), Op.mult)
+        ts(v("u128"), v("n15", 0, 128), SU2 - 0.5, Op.is_ge, -2.0, Op.mult)
+        ts(v("u128"), v("u128"), 1.0, Op.add)
+        tt(v("bo14b"), v("u128"), v("bo14p"), Op.mult)
+        ts(v("pr", 0, 1), pI, 4, Op.arith_shift_right)
+        cp(col(35), v("pr", 0, 1))
+        ts(v("wt", 2, 512, 16), v("whi"), col(35), Op.add)
+        ts(v("wt", 3, 512, 16), v("whi"), 0.0, Op.mult, MF_, Op.add)
+        for k in (4, 5):
+            ts(v("wt", k, 512, 16), v("whi"), 0.0, Op.mult, 1.0, Op.add)
+        ts(col(36), col(10), -34.0, Op.mult, col(14), Op.add)
+        cp(v("tq", 31, 32), col(36))
+        ts(v("r16"), v("i16"), MF_, Op.is_equal)
+        ts(v("cs"), v("i8"), PB, Op.is_equal)
+        ts(v("miw"), v("i16"), MF_, Op.is_equal)
+
+    def constants_d():
+        act(v("e16f"), v("e16"))
+        iota(v("vhi"), [[1, 2], [0, 256]], 26)
+        iota(v("vlo"), [[0, 2], [1, 256]])
+        for k in range(RO):
+            iota(v("atab%d" % k), [[32 - 8192, 3], [1, 32]], 3 * 8192 + R0 + 96 * k)
+        for k in range(1, RO):
+            iota(v("tab%d" % k), [[0, 4 * TS]])
+        ts(v("w128b"), v("n15", 0, 128), 15.0, Op.is_equal)
+        tt(v("mw15"), v("mw"), v("w128b"), Op.mult)
+        cp(v("bof"), v("bo"))
+        ts(v("tr"), v("i32k"), MF_, Op.add, float(R), Op.add)
+        fill(v("vm"), 255.0)
+        ts(v("vst0"), v("vhi"), C14, Op.mult)
+        ts(v("vlo"), v("vlo"), C15, Op.mult)
+        tt(v("vst0"), v("vst0"), v("vlo"), Op.add)
+        for t in range(1, RO):
+            ts(col(36 + t), C14, 2.0 * t, Op.mult)
+            act(v("vst%d" % t), v("vst0"), Fn.Identity, bias=col(36 + t))
+
+    deferred = []
+
+    for t in range(RO):
+        nq = P0 + SP * t
+        nc = nq // 16
+        last = t == RO - 1
+        xa = ["hh", "x1", "x2"][t]
+        xb = ["x1", "x2", "x1"][t]
+        Xa = v(xa, 0, R)
+        Xb = v(xb, 0, R)
+        tab, plr, pls, bw, bs, mf, arr = [n + str(t) for n in ("tab", "plr", "pls", "bw", "bs", "mf", "arr")]
+        p0 = lambda a=0, b=512: v("p0", a, b)
+        p1 = lambda a=0, b=512: v("p1", a, b)
+
+        mm(p0(0, nq), v("bo"), v("live", 0, nq), True, True)
+        ts(v("full", 0, nq), p0(0, nq), 13.5, Op.is_ge)
+        run("v", lambda: g.vector.tensor_tensor_scan(v("scan")[0], v("full")[0], v("sd1")[0], 0.0, Op.add, Op.max),
+            v("full")[1] + v("sd1")[1], v("scan")[1])
+        act(v("junk"), v("scan"), Fn.Sign, bias=HB, scale=-1.0, accum=v("acc", 0, 1))
+        ts(v("cmpv", 0, TS), v("scan"), HB1, Op.is_le, 2.0, Op.mult)
+        red(v("acc", 1, 2), v("cmpv", 0, TS + 1), Op.add)
+        ts(v(pls), v("acc"), 0.5, Op.mult, 272.0 + TS * r, Op.add)
+        send([v(pls)] * 3, [v("plr%d" % t, 2 * place(q), 2 * place(q) + 2) for q in others], "rp%d" % t)
+        arrives([(plr, 0, 6)], "rp%d" % t)
+        if t > 0:
+            deferred[0]()
+        ts(v("pl16"), v("acc"), 0.5, Op.mult, 272.0, Op.add)
+        scat(v(tab), v(pls), v("dat", 32 * r, 32 * r + 32))
+        cp(v("lp"), ind(v("live"), v("pl16")))
+        cp(v("postp"), ind(v("postf"), v("pl16")))
+        cp(v("ps16"), v("postp"))
+        mm(p1(0, 32), v("px"), v("lp"), True, True)
+        scat(v("live"), v("pl16"), v("z32"))
+        if t == 0:
+            constants_b()
+        pieces = []
+        a = 384 * t
+        o = 0
+        for w in AB:
+            pieces.append((a, a + w, 16 * o))
+            a += w
+            o += w
+
+        def absorb(i):
+            a, b, c = pieces[i]
+            w = 16 * (b - a)
+            tt(v(xb, c, c + w), ind(Xa, v("ab16", a, b)), v("xd", c, c + w), Op.max)
+
+        absorb(0)
+        act(v(xb, R0, R), v(xa, R0, R))
+        ts(v("oa"), p1(0, 32), 0.0, Op.max)
+        mm(p0(0, 32), v("mw"), v("oa"), True, False)
+        mm(p0(0, 32), v("one0"), v("k16"), False, True)
+        cp(v("la16"), p0(0, 32))
+        tt(v("laf"), v("dg"), p0(0, 32), Op.mult)
+        for (c0, c1, d0, d1) in ((0, 2 * r, 0, 32 * r), (2 * r, 6, 32 * r + 32, 128)):
+            if c1 > c0:
+                scat(v(tab), v(plr, c0, c1), v("dat", d0, d1))
+        qh = (nq // 2) // 16 * 16
+        halves = ((0, qh, "p2"), (qh, nq, "p6"))
+        for (qa, qb, pn) in halves:
+            act(v("ng", 16 * qa, 16 * qb), ind(v(tab), v("near16", qa, qb)))
+        for i in range(1, len(pieces)):
+            absorb(i)
+        XS = v("xs")
+        cp(XS, ind(Xb, v("ps16")))
+        cp(v("xs2"), XS)
+        tt(v("ma"), ind(XS, v("la16")), v("xs2"), Op.max)
+        cp(v("xg", 0, 16 * VQ[0]), ind(Xb, v("post16", 0, VQ[0])))
+        mm(p1(0, 32), v("ck", 0, 128), v("ones", 0, 32), True, False)
+        mm(p1(0, 32), v("ibig"), v("lp"), False, False)
+        for m in range(16):
+            mm(p1(0, 32), fam("rx", m), v("xs", m, 512, 16), False, False)
+        for m in range(16):
+            mm(p1(0, 32), fam("rmp", m), v("ma", m, 512, 16), False, m == 15)
+        tr(v("ktk"), p1(0, 32))
+        for h in range(2):
+            red(v("kmx", h, h + 1), v("ktk", 16 * h, 16 * h + 16), Op.max)
+        for h in range(2):
+            ts(v("obt", 16 * h, 16 * h + 16), v("ktk", 16 * h, 16 * h + 16), v("kmx", h, h + 1), Op.is_equal)
+        tr(v("ob"), v("obt"))
+        mm(p0(0, 32), v("mw"), v("ob"), True, False)
+        mm(p0(0, 32), v("one0"), v("k16"), False, True)
+        tt(v("lbf"), v("dg"), p0(0, 32), Op.mult)
+        for h in range(2):
+            red(v("lbc_f", h, h + 1), v("lbf", 16 * h, 16 * h + 16), Op.add)
+        cp(v("lbc"), v("lbc_f"))
+        cp(v(bs), ind(XS, v("lbc")))
+        send([v(bs)] * 3, [v("bw%d" % t, 32 * r, 32 * r + 32)] * 3, "rb%d" % t)
+        if not last:
+            dma("y", v("xd"), v(xb, 0, R0))
+        cp(v("lb16"), p0(0, 32))
+        cp(v(bw, 32 * r, 32 * r + 32), v(bs))
+        fill(v(bw, 128, 144), 8192.0)
+        for q in others:
+            arrives([(bw, 32 * q, 32 * q + 32)], "rb%d" % t)
+
+        if t == 0:
+            act(v("hm"), v("e16"), scale=KN32)
+            iota(v("xg", 16 * P0, XW), [[0, XW - 16 * P0]], -1)
+        for (a, b) in ((VQ[1], 256), (256, nq)):
+            act(v("xg", 16 * a, 16 * b), ind(Xb, v("post16", a, b)))
+        if t > 0:
+            deferred[1]()
+        for (qa, qb, pn) in halves:
+            for j in range(16):
+                mm(v(pn, qa, qb), fam("nm", j), v("ng", 16 * qa + j, 16 * qb, 16), j == 0, j == 15)
+            act(v("ff", qa, qb), v(pn, qa, qb), Fn.Relu)
+        cp(v("xg", 16 * VQ[0], 16 * VQ[1]), ind(Xb, v("post16", VQ[0], VQ[1])))
+        if t == 0:
+            constants_c()
+        mm(v("p3", 0, nq), v("ident"), v("ctr", 0, nq), True, True)
+
+        chunks = [(c, min(nq, 128 * c + 128) - 128 * c) for c in range(4)]
+        mm(v("p5"), v("ones", 0, 128), v("cka"), True, False)
+        for c in range(4):
+            gc = v("p5", 128 * c, 128 * c + 128)
+            mm(gc, v("live", 128 * c, 128 * c + 128), v("ibig"), False, False)
+            mm(gc, v("ctr", 128 * c, 128 * c + 128), v("bo14c"), False, False)
+        flip = [0]
+        pend = []
+
+        def xm(m, a=0, b=nq):
+            return v("xg", 16 * a + m, 16 * b, 16)
+
+        def s_unit(m, other, dst, sums):
+            pb = ("p6", "p7", "p1")[flip[0] % 3]
+            flip[0] += 1
+            mm(v(pb, 0, nq), v("ident"), xm(m), True, False)
+            mm(v(pb, 0, nq), v("nid"), other, False, True)
+            act(v(dst, m * 480, m * 480 + nq), v(pb, 0, nq), Fn.Relu)
+            return (sums, m, dst, chunks)
+
+        def add(u):
+            sums, m, dst, cs = u
+            for c, n in cs:
+                mm(part("p5", n, 128 * c + m, 128 * c + 128, 16), v(dst, m * 480 + 128 * c, m * 480 + 128 * c + n), v(sums), False, False)
+
+        def pipe(u):
+            pend.append(u)
+            if len(pend) > LAG:
+                add(pend.pop(0))
+
+        def v_unit(m, pb, dst, sums, a, b):
+            tt(v(dst, m * 480 + a, m * 480 + b), xm(m, a, b), v(pb, a, b), Op.max)
+            pipe((sums, m, dst, [x for x in chunks if a <= 128 * x[0] < b]))
+
+        def distances(other, pb, dst, sums, su, a):
+            vm_ = list(range(su))
+            sm_ = list(range(su, 16))
+            while vm_ or sm_:
+                if sm_ and (not vm_ or len(sm_) * su >= (len(vm_) - LEAD) * (16 - su)):
+                    pipe(s_unit(sm_.pop(0), other, dst, sums))
+                else:
+                    v_unit(vm_.pop(0), pb, dst, sums, a, nq)
+
+        for m in range(SU1):
+            v_unit(m, "p3", "mc", "rgp", 0, 256)
+        for k in range(16):
+            mm(p0(0, nc), fam("e16", k), v("ff", k, nq, 16), k == 0, k == 15)
+        for c in range(4):
+            mm(v("p2", 8 * c, 8 * c + 8), v("ff", 128 * c, 128 * c + 128), v("g8"), True, True)
+        ts(v("tgl", 0, nc), p0(0, nc), -1.0, Op.mult, 128.0, Op.add)
+        act(v("bt", 0, nq), ind(v(bw, 0, 144), v("tgl", 0, nc)))
+        mm(v("p4", 0, nq), v("ident"), v("bt", 0, nq), True, True)
+        for c, n in chunks:
+            mm(part("p5", n, 128 * c, 128 * c + 128, 1), v("bt", 128 * c, 128 * c + n), v("bo14b"), False, False)
+        distances(v("ctr", 0, nq), "p3", "mc", "rgp", SU1, 256)
+        distances(v("bt", 0, nq), "p4", "md", "rgn", SU2, 0)
+        while pend:
+            add(pend.pop(0))
+        mm(v("p5"), v("ones", 0, 128), v("ckb"), False, True)
+
+        cp(v("kt"), v("p5", 1, 512, 2))
+        tt(v("k1"), v("p5", 0, 512, 2), v("kt"), Op.max)
+        prev, w = "k1", 256
+        for nxt in ("k2", "k3", "km"):
+            w //= 2
+            tt(v(nxt), v(prev, 0, 2 * w, 2), v(prev, 1, 2 * w, 2), Op.max)
+            prev = nxt
+        cp(v("kmi"), v("km"))
+        ts(v("kmf"), v("km"), 15.5, Op.is_ge)
+        ts(v("kma"), v("kmi"), 15, Op.bitwise_and)
+        tt(v("wt", 0, 512, 16), v("kmf"), v("p2", 0, 32), Op.mult)
+        cp(v("wt", 1, 512, 16), v("kma"))
+        for c in range(4):
+            mm(v("p%d" % (c // 2), 128 * (c % 2), 128 * (c % 2) + 128), v("wt", 128 * c, 128 * c + 128), v("ident"), True, True)
+        cp(v("tq", 32, 288), v("p0", 0, 256))
+        act(v("tq", 288, 32 + nq), v("p1", 0, nq - 256))
+        banks = ["p3", "p4", "p2", "p6", "p7", "p0", "p1", "p5"]
+        for k in range(8):
+            mm(v(banks[k], 0, nq + 1), v("lg", 128 * k, 128 * k + 128), v("tq", 31, 32 + nq), True, True)
+        for k in range(8):
+            red(v("ms", k, k + 1), v(banks[k], 0, nq + 1), Op.min, True)
+            act(v("zx", 16 * k, 16 * k + 16), v("r16"), scale=v("ms", k, k + 1))
+        mm(p0(0, 8), v("zx"), v("cs"), True, True)
+        cp(v("ls16"), p0(0, 8))
+        cp(v(mf), ind(v("xg"), v("ls16")))
+        send([v(mf, 32 * q, 32 * q + 32) for q in others],
+             [v("arr%d" % t, 32 * place(q), 32 * place(q) + 32) for q in others], "rm%d" % t)
+        arrives([(arr, 0, 96)], "rm%d" % t)
+
+        tt(v("mb"), ind(XS, v("lb16")), v("xs2"), Op.max)
+        cp(v("lsi"), p0(0, 8))
+        ts(v("lqi"), v("lsi"), 4, Op.arith_shift_right)
+        ts(v("lmi"), v("lsi"), 15, Op.bitwise_and)
+        cp(v("lq16"), v("lqi"))
+        cp(v("lm16"), v("lmi"))
+        if t == 0:
+            constants_d()
+        for h in range(2):
+            red(v("lac_f", h, h + 1), v("laf", 16 * h, 16 * h + 16), Op.add)
+        cp(v("lac"), v("lac_f"))
+        act(v("ac"), ind(XS, v("lac")))
+        if not last:
+            act(v("lgt"), ind(v("live"), v("lq16")))
+        act(v("oh"), ind(v("miw"), v("lm16")))
+        act(v("pg"), ind(v("postf"), v("lq16")))
+        mm(p1(0, 32), v("ck", 0, 128), v("ones", 0, 32), True, False)
+        mm(p1(0, 32), v("ibig"), v("lp"), False, False)
+        for m in range(16):
+            mm(p1(0, 32), fam("rmp", m), v("ma", m, 512, 16), False, False)
+        for m in range(16):
+            mm(p1(0, 32), fam("hm", m), v("mb", m, 512, 16), False, False)
+        mm(p1(0, 32), v("bo14p"), v(bs), False, False)
+        mm(p1(0, 32), v("bo14n"), v("ac"), False, True)
+        if not last:
+            tt(v("lut"), v("lgt"), v("oh"), Op.subtract)
+            scat(v("live"), v("lq16"), v("lut"))
+        ts(v("go"), p1(0, 32), 15.5, Op.is_ge)
+        ts(v("nog"), p1(0, 32), 15.5, Op.is_lt)
+        mm(p0(0, 32), v("px"), v("nog"), True, True)
+        tt(v("pgm"), v("pg"), v("oh"), Op.mult)
+        mm(v("p4", 0, 32), v("bof"), v("pgm", 32 * r, 32 * r + 32), True, True)
+        if not last:
+            tt(v("lpn"), v("lp"), v("go"), Op.subtract)
+            scat(v("live"), v("pl16"), v("lpn"))
+        ts(v("rw"), p0(0, 32), 0.0, Op.max)
+        ts(v("fo"), v(mf, 32 * r, 32 * r + 32), 0.0, Op.is_ge, 2.0 ** -17, Op.max)
+        ts(v("ra"), v("p4", 0, 32), 32768.0, Op.add)
+        tt(v("ownv"), v("ra"), v("fo"), Op.mult)
+        mm(v("p7", 0, 32), v("mw15"), v("rw"), True, True)
+        for k in range(16):
+            mm(v("p6", 0, 8), fam("e16f", k), v("pgm", k, 128, 16), k == 0, k == 15)
+
+        def split_list():
+            tt(v("spa"), v("postp"), v("tr"), Op.subtract)
+            tt(v("spb"), v("spa"), v("go"), Op.mult)
+            tt(v("spa"), v("spb"), v("tr"), Op.add)
+            cp(v("spl16"), v("spa"))
+
+        def split_homes(t=t):
+            tt(v("hw"), v("vst%d" % t, 0, 512, 16), v("p7", 0, 32), Op.add)
+            cp(v("rl16"), v("p6", 0, 8))
+            cp(v("vm", 32 * r, 32 * r + 32), v("hw"))
+            scat(v("hh"), v("spl16"), v("vst%d" % t))
+            scat(v("hh"), v("rl16"), v("vm"))
+
+        def arrival_homes(t=t):
+            ts(v("hd"), v("hw"), -255.0, Op.add)
+            for k in range(3):
+                tt(v("eq", 32 * k, 32 * k + 32), v("fa", 32 * k, 32 * k + 32), v("wv"), Op.is_equal)
+            for k in range(3):
+                tt(v("fa", 32 * k, 32 * k + 32), v("eq", 32 * k, 32 * k + 32), v("hd"), Op.mult)
+            ts(v("hh", R0 + 96 * t, R0 + 96 * t + 96), v("fa"), 255.0, Op.add)
+
+        def homes(t=t):
+            split_homes(t)
+            arrival_homes(t)
+
+        def rest(t=t, nq=nq):
+            cp(v("wi"), v("wv"))
+            ts(v("wr"), v("wi"), 8191, Op.bitwise_and)
+            cp(v("wd"), v("wr"))
+            tt(v("wb"), v("wd"), v("postp"), Op.subtract)
+            tt(v("wd"), v("wb"), v("rwf"), Op.mult)
+            tt(v("postf", nq, nq + 32), v("wd"), v("postp"), Op.add)
+            if t < RO - 1:
+                cp(v("post16", nq, nq + 32), v("postf", nq, nq + 32))
+                act(v("nearp"), ind(v("nearf"), v("pl16")))
+                cp(v("near16", nq, nq + 32), v("nearp"))
+                act(v("nearf", nq, nq + 32), v("nearp"))
+                scat(v("ctr"), v("pl16"), v("ac"))
+                act(v("ctr", nq, nq + 32), v("bs%d" % t))
+                split_list()
+
+        if last:
+            split_list()
+            split_homes()
+            dma("y", (T.yh[0:16:2, :], []), (T["hh"][14:128:16, 0:R0], [("hh", 0, R0)]))
+            dma("s", (T.yh[1:16:2, :], []), (T["hh"][15:128:16, 0:R0], [("hh", 0, R0)]))
+
+        ts(v("eq"), v(arr), 0.0, Op.is_ge)
+        tt(v("fa"), v("eq"), v("atab%d" % t), Op.mult)
+        tt(v("wv"), v("fa", 0, 32), v("ownv"), Op.max)
+        tt(v("wb"), v("fa", 32, 64), v("fa", 64, 96), Op.max)
+        tt(v("wv"), v("wv"), v("wb"), Op.max)
+        ts(v("wf"), v("wv"), 8191.5, Op.is_ge)
+        tt(v("rwf"), v("rw"), v("wf"), Op.mult)
+        if not last:
+            tt(v("live", nq, nq + 32), v("go"), v("rwf"), Op.add)
+        ts(v(xb, R0 + 96 * t, R0 + 96 * t + 96), v(arr), 0.0, Op.max)
+        if last:
+            rest()
+            arrival_homes()
+        else:
+            deferred = [rest, homes]
+
+    dma("y", (T.ypost[:, :], []), v("postf", 0, 512))
+    ts(v("ya1"), v("x1", R0, R), CF, Op.mult)
+    ts(v("ya2"), v("hh", R0, R), N14, Op.mult)
+    tt(v("ya3"), v("ya1"), v("ya2"), Op.add)
+    dma("y", (T.ya[:, :], []), v("ya3"))
+    for sem, val in total.items():
+        g.wait_ge(T.sem[sem], val)

@@ -9,20 +9,26 @@ WP = 672
 XW = 16 * WP
 TS = 544
 BIG = 262144.0
-SU1, SU2 = 15, 12
-LEAD, LAG = 5, 4
-HQ = (112, 224)
-VQ = (64, 128)
-AB = [128, 192, 64]
+HOME = "svsssss"
+SLOT = ["vvvvsss", "vvvvvss", "vvvvvsss"]
+NEAR = ["ssss", "ssss", "ssss"]
+HELP = [4, 7, 7]
+PARTS = [(0, 2), (2, 4)]
+SU = [[(16, 16), (6, 6)]] * 3
+CYCLE, GATHER, SCATTER, WAKE, LOOK, HOP = 0.00087, 1.56, 3.8, 0.13, 0.15, 4.5
+FIXED = {"v": 0.0, "s": 0.15, "p": 0.0, "g": 0.15}
+START, RATE, PASSES = 1.8, 2e5, 4
+EARLY = {"tab": 8, "near0": 2, "near1": 4, "near2": 4, "first0": 4, "offer0": 3, "offer1": 3, "slot1": 8, "dist11": 3}
+HOOK = []
 
 SCRATCH = {}
 ALIAS = {}
-OWN = ("plr", "pls", "bw", "bs", "mf", "arr", "p0", "p1", "p2", "p3", "p4", "p5", "p6", "p7")
+OWN = ("plr", "pls", "bw", "mf", "arr", "p0", "p1", "p2", "p3", "p4", "p5", "p6", "p7")
 
 
 def _b(names, w, dt="bfloat16", where="sbuf"):
     for name in names.split():
-        if w > 100 or name.startswith(OWN):
+        if w > 256 or name.startswith(OWN):
             SCRATCH[name] = (where, [128, w], dt)
         else:
             pool = "small_" + dt
@@ -37,7 +43,7 @@ _b("hh", R + 512)
 _b("xd", R0)
 _b("xg", XW)
 _b("ng mc md", 16 * 480)
-_b("e16 rmp rx nm hm vnm", 2048)
+_b("e16 rmp rx nm hm em", 2048)
 _b("e16f", 2048, F)
 _b("postI nearI nsh", P0, I)
 _b("abI", 1152, I)
@@ -50,43 +56,44 @@ for _t in range(RO):
     _b("tab%d" % _t, 4 * TS)
     _b("plr%d" % _t, 6, U)
     _b("pls%d" % _t, 2, U)
+    _b("lst%d" % _t, 10, U)
     _b("bw%d" % _t, 144)
-    _b("bs%d" % _t, 32)
     _b("mf%d" % _t, 128)
     _b("arr%d" % _t, 96)
     _b("atab%d" % _t, 96, F)
     _b("vst%d" % _t, 512)
-_b("full scan sd1 junk", TS)
-_b("cmpv", TS + 2)
+_b("full scan sd1 sd2 junk0 junk1", TS)
+_b("cm0 cm1", 130, F)
 _b("cidx", TS, F)
-_b("ident nid ibig bo bo14c bo14b bo14p bo14n px mw mw15 one0 lga u128 w128 w128b vm oh lgt lut dat", 128)
+_b("ident nid ibig bo bo14p bo14n px mw mw15 lga ni u128 w128 wa128 wb128 wc128 bou nsp vm oh lgt dat", 128)
+_b(" ".join("su%dp su%dn su%da su%db" % (i, i, i, i) for i in (range(1, 16) if HOOK else sorted({x for a in SU for b in a for x in b} - {0, 16}))), 128)
+_b("lval", 160)
 _b("bof zx pg pgm", 128, F)
 _b("lg", 1024)
-_b("ones n15 ck cka ckb wt tq ff xs xs2 ma mb vhi vlo", 512)
-_b("bt", 480)
-_b("kt k1", 256, F)
-_b("k2", 128, F)
-_b("k3", 64, F)
+_b("ones n15 ck cka ckb rst", 256)
+_b("kt0 kt1", 256, F)
+_b("wt ff xs ma mb vhi vlo bt", 512)
+_b("tq", 512)
 _b("fc", 64, F)
-_b("km kmf i32k dg tr whi postp nearp laf lbf ktk spa spb ownv ra wv wb wd hd fo", 32, F)
-_b("kmi kma wi wr", 32, I)
-_b("k16 lp oa obt ob go nog rw rwf wf ac lpn hw z32", 32)
-_b("g8 rgp rgn", 8)
+_b("i32k i32 tr whi postp nearp ktk kts spa spb spc ownv ra wv wb wc wd we hd thr", 32, F)
+_b("kmi0 kmi1 kma0 kma1", 16, I)
+_b("lp oa obt ob go nog rw rwf wf wfa wfb wfm ac hw", 32)
+_b("g8 rgp rgn kd", 8)
 _b("miw", 16)
 _b("pcol pr", 2, I)
 _b("i16 r16", 16, F)
-_b("i8 cs ms", 8, F)
-_b("acc lac_f lbc_f kmx", 2, F)
-_b("pl16 lac lbc", 2, U)
-_b("la16 ps16 lb16 spl16 tgl", 32, U)
-_b("ls16 lq16 lm16 rl16", 8, U)
+_b("i8 cs ms0 ms1 ms2 ms3 mt1 mt2", 8, F)
+_b("acc", 2, F)
+_b("lac lbc", 2, U)
+_b("ps16 spl16 tgl kx16", 32, U)
+_b("ls16 lm16 rl16", 8, U)
 _b("lsi lqi lmi", 8, I)
-_b("fa eq", 96, F)
+_b("fa fb eq eh", 96, F)
 _b("ya1 ya2 ya3", 288)
 for _i in range(8):
     _b("p%d" % _i, 512, F, "psum")
 
-NDMA = 16
+NDMA = 28
 SEMAPHORES = ["qv", "qs", "qp", "qg", "sent"] + ["d%d" % i for i in range(NDMA)] + \
     ["%s%d" % (a, t) for a in ("rp", "rb", "rm") for t in range(RO)]
 
@@ -96,80 +103,145 @@ def rank_program(g, core, T, topo):
     if r is None:
         return
     Q = {"v": g.vector, "s": g.scalar, "p": g.tensor, "g": g, "y": g.sync}
-    cnt = {"qv": 0, "qs": 0, "qp": 0, "qg": 0}
-    total = {}
-    known = {q: {} for q in Q}
+    ops = []
     acc = {}
     dn = [0]
+    stage = [""]
 
-    def waits(q, toks):
-        need = {}
-        for (sem, val, q2, snap) in toks:
-            if known[q].get(sem, 0) < val and (sem not in need or need[sem][1] < val):
-                need[sem] = (sem, val, q2, snap)
-        lst = list(need.values())
-        for tk in lst:
-            if any(o is not tk and o[3].get(tk[0], 0) >= tk[1] for o in lst):
-                continue
-            Q[q].wait_ge(T.sem[tk[0]], tk[1])
-        for tk in lst:
-            k = known[q]
-            k[tk[0]] = max(k.get(tk[0], 0), tk[1])
-            for s2, v2 in tk[3].items():
-                if k.get(s2, 0) < v2:
-                    k[s2] = v2
+    def meet(a, b):
+        if a[0] >= b[1] or b[0] >= a[1]:
+            return False
+        return a[2] == 1 or a[2] != b[2] or (a[0] - b[0]) % a[2] == 0
 
-    def deps(q, reads, writes):
-        toks = []
+    def note(q, fn, time, lag, reads, writes, adds=False, after=(), sem=None, mine=0):
+        me = len(ops)
+        dep = {d: True for d in after}
         for is_w, regs in ((False, reads), (True, writes)):
-            for (b, c0, c1) in regs:
-                ps = SCRATCH.get(b, ("",))[0] == "psum"
-                for (d0, d1, w2, tok) in acc.get(b, ()):
+            for reg in regs:
+                ps = SCRATCH[reg[0]][0] == "psum"
+                for (o, w2, d, adds2) in acc.get(reg[0], ()):
                     if ps:
-                        if tok[2] == q and (q == "p" or not (is_w or w2)):
-                            continue
-                        toks.append(tok)
-                    elif d0 < c1 and c0 < d1 and (is_w or w2):
-                        toks.append(tok)
-        return toks
+                        if ops[d]["q"] != q:
+                            dep[d] = True
+                        elif q == "p":
+                            if not (adds and adds2):
+                                dep.setdefault(d, False)
+                        elif is_w or w2:
+                            dep[d] = True
+                    elif (is_w or w2) and meet(reg[1:], o):
+                        dep[d] = True
+        ops.append({"q": q, "fn": fn, "time": time, "lag": lag, "dep": dep, "sem": sem, "early": EARLY.get(stage[0], 0.0), "tag": HOOK[0]() if HOOK else None})
+        me += mine
+        for reg in writes:
+            ps = SCRATCH[reg[0]][0] == "psum"
+            old = acc.get(reg[0], [])
+            if not adds:
+                old = [o for o in old if not (ps or (reg[3] == 1 and reg[1] <= o[0][0] and o[0][1] <= reg[2]) or reg[1:] == o[0])]
+            acc[reg[0]] = old + [(reg[1:], True, me, adds)]
+        for reg in reads:
+            acc.setdefault(reg[0], []).append((reg[1:], False, me, False))
+        return me - mine
 
-    def note(reads, writes, tok):
-        for (b, c0, c1) in writes:
-            ps = SCRATCH.get(b, ("",))[0] == "psum"
-            old = acc.get(b, [])
-            acc[b] = [o for o in old if not (ps or (c0 <= o[0] and o[1] <= c1))] + [(c0, c1, True, tok)]
-        for (b, c0, c1) in reads:
-            old = acc.get(b, [])
-            acc[b] = [o for o in old if not (not o[2] and o[3][2] == tok[2] and o[3][0] == tok[0] and c0 <= o[0] and o[1] <= c1)] + [(c0, c1, False, tok)]
+    def run(q, fn, cycles, reads, writes, adds=False):
+        note(q, fn, cycles * CYCLE + FIXED[q], 0.0, reads, writes, adds)
 
-    def run(q, fn, reads, writes):
-        waits(q, deps(q, reads, writes))
-        sem = "q" + q
-        cnt[sem] += 1
-        total[sem] = cnt[sem]
-        fn().then_inc(T.sem[sem], 1)
-        note(reads, writes, (sem, cnt[sem], q, dict(known[q])))
-
-    def dma(q, out, in_):
-        waits(q, deps(q, in_[1], out[1]))
+    def dma(q, out, in_, nbytes, turn=False):
         sem = "d%d" % dn[0]
         dn[0] += 1
-        Q[q].dma_start(out[0], in_[0]).then_inc(T.sem[sem], 16)
-        total[sem] = 16
-        note(in_[1], out[1], (sem, 16, "dma", dict(known[q])))
+        me = note(q, lambda: Q[q].dma_start(out[0], in_[0]).then_inc(T.sem[sem], 16), 0.1, START, in_[1], out[1], sem=(sem, 0), mine=1)
+        note("d", None, nbytes / RATE, 0.0, [], [], after=[me], sem=(sem, 16))
+        if turn:
+            ops[me]["dep"][me - 2] = False
+            ops[me + 1]["dep"][me - 1] = False
 
-    def v(b, c0=0, c1=None, s=1):
+    def emit():
+        n = len(ops)
+        before = [[(d, ops[d]["lag"] if o["q"] in "dr" else WAKE if w else 0.0) for d, w in o["dep"].items()] for o in ops]
+        behind = [[] for _ in ops]
+        for i in range(n):
+            for d, gap in before[i]:
+                behind[d].append((i, gap))
+
+        def lay(turn, edges):
+            end = [0.0] * n
+            busy = {q: [] for q in "vspgydr"}
+            for i in turn:
+                at = max([end[d] + gap for d, gap in edges[i]] + [0.0])
+                time, b = ops[i]["time"], busy[ops[i]["q"]]
+                lo, hi = 0, len(b)
+                while lo < hi:
+                    mid = (lo + hi) // 2
+                    lo, hi = (mid + 1, hi) if b[mid][1] <= at else (lo, mid)
+                while lo < len(b) and b[lo][0] < at + time:
+                    at = max(at, b[lo][1])
+                    lo += 1
+                b.insert(lo, (at, at + time))
+                end[i] = at + time
+            return end
+
+        way = [0.0] * n
+        for i in range(n - 1, -1, -1):
+            way[i] = ops[i]["time"] + max([way[j] + gap for j, gap in behind[i]] + [0.0])
+        turn = sorted(range(n), key=lambda i: (-way[i], i))
+        best = None
+        for _ in range(PASSES):
+            end = lay(turn, before)
+            turn = [turn[k] for k in sorted(range(n), key=lambda k: (end[turn[k]] - ops[turn[k]]["time"], k))]
+            if best is None or max(end) < best[0]:
+                best = (max(end), turn)
+            turn = [turn[k] for k in sorted(range(n), key=lambda k: (-end[turn[k]], -k))]
+            end = lay(turn, behind)
+            key = [-end[i] - ops[i]["early"] for i in range(n)]
+            for i in range(n - 1, -1, -1):
+                key[i] = min([key[i]] + [key[j] - ops[i]["time"] for j, gap in behind[i]])
+            turn = sorted(range(n), key=lambda i: (key[i], i))
+        order = best[1]
+        if HOOK:
+            HOOK.append(best[0])
+        cnt = {}
+        known = {q: {} for q in Q}
+        tok = {}
+        for i in order:
+            o = ops[i]
+            q = o["q"]
+            if q in "dr":
+                tok[i] = (o["sem"][0], o["sem"][1], {})
+                cnt[o["sem"][0]] = o["sem"][1]
+                continue
+            need = {}
+            for d, w in o["dep"].items():
+                if w and known[q].get(tok[d][0], 0) < tok[d][1] and need.get(tok[d][0], ("", 0))[1] < tok[d][1]:
+                    need[tok[d][0]] = tok[d]
+            for tk in need.values():
+                if not any(x is not tk and x[2].get(tk[0], 0) >= tk[1] for x in need.values()):
+                    Q[q].wait_ge(T.sem[tk[0]], tk[1])
+            for tk in need.values():
+                for s2, v2 in list(tk[2].items()) + [tk[:2]]:
+                    known[q][s2] = max(known[q].get(s2, 0), v2)
+            if HOOK:
+                HOOK[1](o["tag"])
+            if o["sem"] is None:
+                sem = "q" + q
+                cnt[sem] = cnt.get(sem, 0) + 1
+                o["fn"]().then_inc(T.sem[sem], 1)
+            else:
+                o["fn"]()
+                sem = o["sem"][0]
+                cnt[sem] = cnt.get(sem, 0) + o["sem"][1]
+            tok[i] = (sem, cnt[sem], dict(known[q]))
+        for sem, val in cnt.items():
+            g.wait_ge(T.sem[sem], val)
+
+    def v(b, c0=0, c1=None, s=1, n=128):
         if b in ALIAS:
             b, o, w = ALIAS[b]
             c0, c1 = o + c0, o + (w if c1 is None else c1)
         c1 = SCRATCH[b][1][1] if c1 is None else c1
-        return (T[b][:, c0:c1] if s == 1 else T[b][:, c0:c1:s], [(b, c0, c1)])
-
-    def part(b, n, c0, c1, s):
-        return (T[b][0:n, c0:c1] if s == 1 else T[b][0:n, c0:c1:s], [(b, c0, c1)])
+        kind = "psum" if SCRATCH[b][0] == "psum" else "two" if SCRATCH[b][2] in (U, "bfloat16") else "four"
+        return (T[b][0:n, c0:c1] if s == 1 else T[b][0:n, c0:c1:s], [(b, c0, c1, s)], len(range(c0, c1, s)), kind)
 
     def ind(win, off):
-        return (win[0].indirect(off[0]), win[1] + off[1])
+        return (win[0].indirect(off[0]), win[1] + off[1], 16 * off[2], "ind")
 
     def col(i):
         return v("fc", i, i + 1)
@@ -177,8 +249,12 @@ def rank_program(g, core, T, topo):
     def fam(b, m):
         return v(b, 128 * m, 128 * m + 128)
 
+    def cyc(out, a):
+        return max(64, a[2] * (GATHER if a[3] == "ind" else 0.5 if out[3] == a[3] == "two" else 1))
+
     def tt(out, a, b, op):
-        run("v", lambda: g.vector.tensor_tensor(out[0], a[0], b[0], op), a[1] + b[1], out[1])
+        c = cyc(out, a) if a[3] == "ind" else max(64, a[2] * (1 if "psum" in (a[3], b[3]) else 2))
+        run("v", lambda: g.vector.tensor_tensor(out[0], a[0], b[0], op), c, a[1] + b[1], out[1])
 
     def ts(out, a, s1, o1, s2=None, o2=None):
         regs = list(a[1])
@@ -190,25 +266,30 @@ def rank_program(g, core, T, topo):
             regs += s2[1]
             x2 = s2[0]
         if o2 is None:
-            run("v", lambda: g.vector.tensor_scalar(out[0], a[0], x1, None, o1), regs, out[1])
+            run("v", lambda: g.vector.tensor_scalar(out[0], a[0], x1, None, o1), cyc(out, a), regs, out[1])
         else:
-            run("v", lambda: g.vector.tensor_scalar(out[0], a[0], x1, x2, o1, o2), regs, out[1])
+            run("v", lambda: g.vector.tensor_scalar(out[0], a[0], x1, x2, o1, o2), cyc(out, a), regs, out[1])
 
     def cp(out, a):
-        run("v", lambda: g.vector.tensor_copy(out[0], a[0]), a[1], out[1])
+        run("v", lambda: g.vector.tensor_copy(out[0], a[0]), cyc(out, a), a[1], out[1])
 
     def scat(win, off, a):
-        run("v", lambda: g.vector.tensor_copy(win[0].indirect(off[0]), a[0]), a[1] + off[1] + win[1], win[1])
+        run("v", lambda: g.vector.tensor_copy(win[0].indirect(off[0]), a[0]), max(64, SCATTER * a[2]), a[1] + off[1], win[1])
 
     def red(out, a, op, ab=False):
         kw = {"apply_absolute_value": True} if ab else {}
-        run("v", lambda: g.vector.tensor_reduce(out[0], a[0], Ax.X, op, **kw), a[1], out[1])
+        run("v", lambda: g.vector.tensor_reduce(out[0], a[0], Ax.X, op, **kw), max(64, a[2]), a[1], out[1])
+
+    def scan(out, a, b, init, o0, o1):
+        regs = a[1] + b[1] + (init[1] if isinstance(init, tuple) else [])
+        x = init[0] if isinstance(init, tuple) else init
+        run("v", lambda: g.vector.tensor_tensor_scan(out[0], a[0], b[0], x, o0, o1), cyc(out, b), regs, out[1])
 
     def tr(out, a):
-        run("v", lambda: g.vector.transpose(out[0], a[0]), a[1], out[1])
+        run("v", lambda: g.vector.transpose(out[0], a[0]), 64, a[1], out[1])
 
     def fill(out, c):
-        run("v", lambda: g.vector.memset(out[0], c), [], out[1])
+        run("v", lambda: g.vector.memset(out[0], c), cyc(out, out), [], out[1])
 
     def act(out, a, fn=Fn.Copy, bias=None, scale=None, accum=None):
         kw = {}
@@ -225,19 +306,23 @@ def rank_program(g, core, T, topo):
         if accum is not None:
             kw["accum_out"] = accum[0]
             w += accum[1]
-        run("s", lambda: g.scalar.activation(out[0], a[0], fn, **kw), regs, w)
+        run("s", lambda: g.scalar.activation(out[0], a[0], fn, **kw), a[2] * (GATHER if a[3] == "ind" else 1), regs, w)
+
+    def copy(q, out, a):
+        (cp if q == "v" else act)(out, a)
 
     def mm(out, lhsT, rhs, start, stop):
-        run("p", lambda: g.tensor.matmul(out[0], lhsT[0], rhs[0], start, stop), lhsT[1] + rhs[1], out[1])
+        c = max(min(64, lhsT[2]), rhs[2]) * (2 if rhs[3] == "four" else 0.5)
+        run("p", lambda: g.tensor.matmul(out[0], lhsT[0], rhs[0], start, stop), c, lhsT[1] + rhs[1], out[1], not (start or stop))
 
     def iota(out, pat, base=0, cm=0, flag=True):
         kw = {"allow_small_or_imprecise_dtypes": True} if flag else {}
-        run("g", lambda: g.iota(out[0], pat, base, cm, **kw), [], out[1])
+        run("g", lambda: g.iota(out[0], pat, base, cm, **kw), 2 * out[2], [], out[1])
 
     others = [q for q in range(len(T.cores)) if q != r]
     NE = 2
 
-    def send(bufs, dsts, sem):
+    def send(bufs, dsts, lands, sem):
         trs = []
         regs = []
         for i, q in enumerate(others):
@@ -247,61 +332,62 @@ def rank_program(g, core, T, topo):
             trs.append(RemoteDMATransfer(dst_ids=[DstId(rid=rid, pnc=pid)], dma_engine_mask=sum(1 << e for e in eng),
                                          remote_sem=T.sem[sem], srcs=[bufs[i][0]], dsts=[dsts[i][0]]))
             regs += bufs[i][1]
-        waits("g", deps("g", regs, []))
-        g.remote_dma_fused(trs, local_sem=T.sem["sent"])
-        total["sent"] = total.get("sent", 0) + NE * len(others)
-
-    def arrives(regs, sem):
         n = NE * len(others)
-        total[sem] = n
-        note([], regs, (sem, n, "remote", {}))
+        me = note("g", lambda: g.remote_dma_fused(trs, local_sem=T.sem["sent"]), 0.6, HOP, regs, [], sem=("sent", n))
+        note("r", None, 0.001, 0.0, [], [reg for x in lands for reg in x[1]], after=[me], sem=(sem, n))
 
     def place(q):
         return r - (1 if r > q else 0)
 
-    half = R0 // 2
-    dma("y", v("postI"), (T.post[:, :], []))
-    dma("s", v("hh", 0, half), (T.rec[:, 0:half], []))
-    dma("y", v("hh", half, R0), (T.rec[:, half:R0], []))
-    dma("s", v("abI"), (T.absorb[:, :], []))
-    dma("y", v("nearI"), (T.near[:, :], []))
-    dma("s", v("xd", 0, half), (T.rec[:, 0:half], []))
-    dma("y", v("xd", half, R0), (T.rec[:, half:R0], []))
-    dma("y", v("ctr", 0, P0), (T.cen[:, :], []))
+    third = R0 // 3
+    fill(v("tab0"), 0.0)
+    dma("y", v("postI"), (T.post[:, :], []), 2e5)
+    for i in range(3):
+        dma("y", v("hh", third * i, third * i + third), (T.rec[:, third * i:third * i + third], []), 5e5, True)
+    dma("y", v("abI", 0, 384), (T.absorb[:, 0:384], []), 2e5, True)
+    dma("y", v("nearI"), (T.near[:, :], []), 2e5, True)
+    dma("y", v("ctr", 0, P0), (T.cen[:, :], []), 1e5, True)
+    dma("y", v("abI", 384, 1152), (T.absorb[:, 384:1152], []), 4e5, True)
+    for k in range(1, RO):
+        dma("y", v("tab%d" % k), v("tab0"), 5e5, True)
 
     pI, p15 = v("pcol", 0, 1), v("pcol", 1, 2)
-    NI = v("vnm", 0, 128)
-    R1 = v("md", 0, 2048)
+    NI = v("ni")
     iota(pI, [[0, 1]], 0, 1, False)
-    iota(v("vnm"), [[-1, 16], [1, 128]])
+    iota(NI, [[1, 128]])
     iota(v("i32k"), [[16, 32]])
+    iota(v("i32"), [[1, 32]])
     iota(v("w128"), [[-1, 128]], 128)
     iota(v("slot"), [[16, P0]])
     iota(v("whi"), [[8, 4], [0, 8]])
-    iota(v("n15"), [[0, 32], [1, 16]])
+    iota(v("n15"), [[0, 16], [1, 16]])
     iota(v("i16"), [[1, 16]])
     iota(v("i8"), [[16, 8]])
     iota(v("cidx"), [[1, TS]])
-    iota(v("dg"), [[0, 2], [1, 16]])
     iota(v("postf", MD, WP), [[1, 128]], R)
     iota(v("postf", PD, MD), [[0, 32]])
-    iota(v("tab0"), [[0, 4 * TS]])
-    fill(v("hh", R0, R), 0.0)
+    iota(v("vhi"), [[1, 2], [0, 256]], 26)
+    iota(v("vlo"), [[0, 2], [1, 256]])
+    for k in range(RO):
+        iota(v("atab%d" % k), [[1, 96]], R0 + 96 * k)
+        iota(v("bw%d" % k, 128, 144), [[0, 16]], 8192)
+    iota(v("vm"), [[0, 128]], 255)
+    iota(v("wt"), [[0, 512]])
+    iota(v("ones"), [[0, 256]], 1)
+    iota(v("nearf", P0, WP), [[0, WP - P0]])
+    iota(v("ctr", P0, WP), [[0, WP - P0]])
+    iota(v("xg", 16 * MD, XW, 16), [[0, 128]], -1)
+    for b in ("hh", "x1", "x2"):
+        fill(v(b, R0, R), 0.0)
     fill(v("live", P0, WP), 0.0)
     fill(v("full", P0, TS), 0.0)
-    fill(v("cmpv", TS, TS + 2), -544.0)
-    fill(v("ctr", P0, WP), 0.0)
-    fill(v("nearf", P0, WP), 0.0)
-    fill(v("wt"), 0.0)
     fill(v("ff", P0, 512), 0.0)
-    fill(v("ones"), 1.0)
-    fill(v("z32"), 0.0)
     PF, MF_, PB = col(0), col(1), col(2)
     ts(p15, pI, 15, Op.bitwise_and)
     cp(PF, pI)
     cp(MF_, p15)
     tt(PB, PF, MF_, Op.subtract)
-    for i in range(7):
+    for i in range(8):
         ts(col(8 + i), MF_, float(i), Op.is_equal)
     C14, C15, N14, CF = col(16), col(17), col(18), col(19)
     ts(C14, MF_, 14.0, Op.is_equal)
@@ -309,439 +395,397 @@ def rank_program(g, core, T, topo):
     ts(CF, MF_, 13.5, Op.is_le)
     ts(N14, MF_, 13.5, Op.is_gt)
     ts(col(20), C14, 256.0, Op.mult, C15, Op.add)
-    K32, KN32, KN16, K16c = col(21), col(22), col(23), col(24)
+    K32, KN32, KN16, K16c, N255 = col(21), col(22), col(23), col(24), col(25)
     ts(K32, CF, 32.0, Op.mult)
     ts(KN32, CF, -32.0, Op.mult)
     ts(KN16, CF, -16.0, Op.mult)
     ts(K16c, CF, 16.0, Op.mult)
-    HB, HB1 = col(26), col(27)
-    ts(HB, MF_, 0.5, Op.add)
-    ts(HB1, MF_, 16.5, Op.add)
-    ts(v("e16"), v("vnm"), PB, Op.is_equal)
-    act(v("hm"), v("e16"), scale=col(20))
-    cp(v("post16", 0, P0), v("postI"))
-
-    X = v("hh", 0, R)
-    ts(col(37), PF, 0.0, Op.mult, -256.0, Op.add)
-    act(v("slot"), v("slot"), Fn.Identity, bias=MF_)
-    act(R1, v("e16"), Fn.Identity, scale=0.0, bias=col(37))
-    home_parts = ((0, HQ[0], "p5"), (HQ[0], HQ[1], "p2"), (HQ[1], P0, "p6"))
-    for (a, b, pb) in home_parts[0:2]:
-        act(v("xg", 16 * a, 16 * b), ind(X, v("post16", a, b)))
+    ts(N255, N14, 255.0, Op.mult)
+    HB = (col(26), col(27))
+    ts(HB[0], MF_, 0.5, Op.add)
+    ts(HB[1], MF_, 16.5, Op.add)
     ts(v("u128"), NI, PB, Op.subtract)
-    ts(v("px"), v("u128"), 0.0, Op.is_ge)
-    ts(v("w128b"), v("u128"), 15.5, Op.is_le)
-    tt(v("bo"), v("px"), v("w128b"), Op.mult)
+    for m in range(16):
+        ts(fam("hm", m), v("u128"), float(m), Op.is_equal, col(20), Op.mult)
+    for m in range(16):
+        ts(fam("e16", m), v("u128"), float(m), Op.is_equal)
+    act(v("em"), v("e16"), scale=MF_)
+    act(v("rx"), v("e16"), scale=KN16)
+    act(v("rmp"), v("e16"), scale=K32)
+    act(v("e16f"), v("e16"))
+    cp(v("post16", 0, P0), v("postI"))
     cp(v("postf", 0, P0), v("postI"))
+    act(v("slot"), v("slot"), Fn.Identity, bias=MF_)
+    ts(v("wa128"), v("u128"), 0.0, Op.is_ge)
+    ts(v("wb128"), v("u128"), 15.5, Op.is_le)
+    tt(v("bo"), v("wa128"), v("wb128"), Op.mult)
     ts(v("g8"), v("i8"), PB, Op.is_equal)
-    act(v("rgp"), v("g8"), scale=K32)
-    act(v("rgn"), v("g8"), scale=KN32)
-    act(v("bo14p"), v("bo"), scale=K16c)
-    act(v("bo14n"), v("bo"), scale=KN16)
-    A, B = col(33), col(34)
-    ts(A, col(12), 32768.0, Op.mult)
-    ts(A, col(14), 16.0, Op.mult, A, Op.add)
-    ts(B, col(8), 32768.0, Op.mult, col(9), Op.add)
-    for (i, w) in ((10, -256.0), (11, -16.0), (12, -32768.0 * 128), (13, -15.0)):
-        ts(B, col(i), w, Op.mult, B, Op.add)
-    ts(v("lga"), NI, A, Op.mult, B, Op.add)
+    ts(v("rgp"), v("g8"), K32, Op.mult)
+    ts(v("rgn"), v("g8"), KN32, Op.mult)
+    ts(v("bo14p"), v("bo"), K16c, Op.mult)
+    ts(v("bo14n"), v("bo"), KN16, Op.mult)
+    ts(v("wc128"), v("u128"), col(8), Op.add)
+    tt(v("bou"), v("wc128"), v("bo"), Op.mult)
+    ts(col(37), col(9), -256.0, Op.mult, col(8), Op.add)
+    ts(col(38), col(9), -256.0, Op.mult)
+    for j in range(16):
+        ts(fam("nm", j), v("bou"), float(j), Op.is_gt, col(37), Op.mult)
+    ts(v("nsp"), v("bo"), col(38), Op.mult)
+    A0, A1, B = col(33), col(34), [col(48 + i) for i in range(6)]
+    ts(A0, col(12), 32768.0, Op.mult)
+    ts(A1, col(14), 16.0, Op.mult, A0, Op.add)
+    ts(B[0], col(8), 32768.0, Op.mult, col(9), Op.add)
+    for n, (i, w) in enumerate(((10, -256.0), (11, -16.0), (12, -32768.0 * 128), (13, -15.0), (15, 2.0 ** 23))):
+        ts(B[n + 1], col(i), w, Op.mult, B[n], Op.add)
+    ts(v("lga"), NI, A1, Op.mult, B[5], Op.add)
     for k in range(8):
         ts(col(40 + k), PB, 16.0 * k, Op.is_equal)
-    for k in range(8):
-        act(v("lg", 128 * k, 128 * k + 128), v("lga"), scale=col(40 + k))
-    cp(v("xg", 16 * HQ[1], 16 * P0), ind(X, v("post16", HQ[1], P0)))
-    for (a, b, pb) in (home_parts[0], home_parts[2], home_parts[1]):
-        for m in range(16):
-            mm(v(pb, a, b), fam("hm", m), v("xg", 16 * a + m, 16 * b, 16), m == 0, m == 15)
+        ts(fam("lg", k), v("lga"), col(40 + k), Op.mult)
     ts(col(28), MF_, 512.0, Op.add)
     ts(col(29), MF_, 528.0, Op.add)
-    ts(v("scan"), v("cidx"), col(28), Op.is_ge, 16.0, Op.mult)
+    ts(v("sd2"), v("cidx"), col(28), Op.is_ge, 16.0, Op.mult)
     ts(v("sd1"), v("cidx"), col(29), Op.is_ge, 84.0, Op.mult)
-    tt(v("sd1"), v("sd1"), v("scan"), Op.add)
+    tt(v("sd1", PD, TS), v("sd1", PD, TS), v("sd2", PD, TS), Op.add)
     ts(v("ident"), NI, PF, Op.is_equal)
     ts(v("ibig"), v("ident"), BIG, Op.mult)
     ts(v("nid"), v("ident"), -1.0, Op.mult)
-    ts(v("w128b"), NI, PF, Op.is_gt, -32.0, Op.mult)
-    tt(v("w128b"), v("w128b"), v("bo"), Op.mult)
-    tt(v("px"), v("w128b"), v("ident"), Op.add)
+    ts(v("wa128"), NI, PF, Op.is_gt, -32.0, Op.mult)
+    tt(v("wb128"), v("wa128"), v("bo"), Op.mult)
+    tt(v("px"), v("wb128"), v("ident"), Op.add)
     ts(v("mw"), v("bo"), MF_, Op.mult)
     ts(col(30), PF, 0.0, Op.is_equal)
     ts(col(31), PF, 1.0, Op.is_equal)
     ts(col(32), col(30), -BIG, Op.mult)
-    ts(v("one0"), NI, 0.0, Op.mult, col(30), Op.add)
-    cp(v("k16"), v("i32k"))
+    ts(v("kd", 0, 1), MF_, 16.0, Op.mult)
+    ts(v("kd", 1, 2), MF_, 16.0, Op.mult, 256.0, Op.add)
+    cp(v("kx16"), v("i32"))
     ts(v("dat"), v("w128"), col(8), Op.mult, col(9), Op.add)
-    ts(v("ckb"), v("n15"), -1.0, Op.mult, 15.0, Op.add)
-    ts(v("ckb"), v("ckb"), col(31), Op.mult)
+    ts(v("ck"), v("n15"), -1.0, Op.mult, 15.0, Op.add)
+    ts(v("ckb"), v("ck"), col(31), Op.mult)
     ts(v("cka"), v("n15"), 0.0, Op.mult, col(32), Op.add)
     ts(v("ck"), v("ckb"), col(32), Op.add)
-    ts(v("dg"), v("dg"), MF_, Op.is_equal)
-    for (a, b, pb) in (home_parts[0], home_parts[2], home_parts[1]):
-        tt(v("live", a, b), v("slot", a, b), v(pb, a, b), Op.is_equal)
+    ts(v("rst"), v("n15"), 0.0, Op.is_equal, -2.0 ** 22, Op.mult)
+    ts(v("nsh"), v("nearI"), 4, Op.arith_shift_right, 96, Op.bitwise_and)
+    tt(v("nearf", 0, P0), v("nsh"), v("nearI"), Op.add)
+    cp(v("near16", 0, P0), v("nearf", 0, P0))
+    for t in range(RO):
+        cp(v("ab16", 384 * t, 384 * t + 384), v("abI", 384 * t, 384 * t + 384))
+    made = {16: ("bo14p", "bo14n"), 0: ("bo14n", "bo14p")}
 
-    def constants_b():
-        ts(v("nsh"), v("nearI"), 4, Op.arith_shift_right, 96, Op.bitwise_and)
-        tt(v("nearf", 0, P0), v("nsh"), v("nearI"), Op.add)
-        cp(v("near16", 0, P0), v("nearf", 0, P0))
-        cp(v("ab16"), v("abI"))
-        act(v("rx"), v("e16"), scale=KN16)
-        act(v("rmp"), v("e16"), scale=K32)
-        act(v("nm"), v("e16"), scale=col(8))
-        run("g", lambda: g.affine_select(R1[0], R1[0], [[-1, 16], [1, 128]], Op.is_gt, 0.0, 1, -1), R1[1], R1[1])
-        run("g", lambda: g.affine_select(R1[0], R1[0], [[0, 16], [-1, 128]], Op.is_gt, 0.0, 15, 1), R1[1], R1[1])
-        dma("y", (T["nm"][1:128:16, :], [("nm", 0, 2048)]), (T["md"][1:128:16, 0:2048], R1[1]))
+    def signs(su):
+        if su not in made:
+            made[su] = ("su%dp" % su, "su%dn" % su)
+            ts(v("su%da" % su), v("n15", 0, 128), su - 0.5, Op.is_ge, -2.0, Op.mult)
+            ts(v("su%db" % su), v("su%da" % su), 1.0, Op.add)
+            tt(v(made[su][0]), v("su%db" % su), v("bo14p"), Op.mult)
+            ts(v(made[su][1]), v(made[su][0]), -1.0, Op.mult)
+        return made[su]
 
-    def constants_c():
-        ts(v("u128"), v("n15", 0, 128), SU1 - 0.5, Op.is_ge, -2.0, Op.mult)
-        ts(v("u128"), v("u128"), 1.0, Op.add)
-        tt(v("bo14c"), v("u128"), v("bo14n"), Op.mult)
-        ts(v("u128"), v("n15", 0, 128), SU2 - 0.5, Op.is_ge, -2.0, Op.mult)
-        ts(v("u128"), v("u128"), 1.0, Op.add)
-        tt(v("bo14b"), v("u128"), v("bo14p"), Op.mult)
-        ts(v("pr", 0, 1), pI, 4, Op.arith_shift_right)
-        cp(col(35), v("pr", 0, 1))
-        ts(v("wt", 2, 512, 16), v("whi"), col(35), Op.add)
-        ts(v("wt", 3, 512, 16), v("whi"), 0.0, Op.mult, MF_, Op.add)
-        for k in (4, 5):
-            ts(v("wt", k, 512, 16), v("whi"), 0.0, Op.mult, 1.0, Op.add)
-        ts(col(36), col(10), -34.0, Op.mult, col(14), Op.add)
-        cp(v("tq", 31, 32), col(36))
-        ts(v("r16"), v("i16"), MF_, Op.is_equal)
-        ts(v("cs"), v("i8"), PB, Op.is_equal)
-        ts(v("miw"), v("i16"), MF_, Op.is_equal)
+    ts(v("pr", 0, 1), pI, 4, Op.arith_shift_right)
+    cp(col(35), v("pr", 0, 1))
+    ts(v("wt", 2, 512, 16), v("whi"), col(35), Op.add)
+    ts(v("wt", 3, 512, 16), v("whi"), 0.0, Op.mult, MF_, Op.add)
+    for k in (4, 5):
+        ts(v("wt", k, 512, 16), v("whi"), 0.0, Op.mult, 1.0, Op.add)
+    ts(v("tq", 128 * PARTS[-1][0] + 15, 128 * PARTS[-1][0] + 16), col(10), -34.0, Op.mult, col(14), Op.add)
+    ts(v("r16"), v("i16"), MF_, Op.is_equal)
+    ts(v("cs"), v("i8"), PB, Op.is_equal)
+    ts(v("miw"), v("i16"), MF_, Op.is_equal)
+    ts(v("wc128"), v("n15", 0, 128), 15.0, Op.is_equal)
+    tt(v("mw15"), v("mw"), v("wc128"), Op.mult)
+    cp(v("bof"), v("bo"))
+    ts(v("tr"), v("i32k"), MF_, Op.add, float(R), Op.add)
+    ts(v("vhi"), v("vhi"), C14, Op.mult)
+    ts(v("vlo"), v("vlo"), C15, Op.mult)
+    tt(v("vst0"), v("vhi"), v("vlo"), Op.add)
+    for t in range(1, RO):
+        ts(col(56 + t), C14, 2.0 * t, Op.mult)
+        ts(v("vst%d" % t), v("vst0"), col(56 + t), Op.add)
 
-    def constants_d():
-        act(v("e16f"), v("e16"))
-        iota(v("vhi"), [[1, 2], [0, 256]], 26)
-        iota(v("vlo"), [[0, 2], [1, 256]])
-        for k in range(RO):
-            iota(v("atab%d" % k), [[32 - 8192, 3], [1, 32]], 3 * 8192 + R0 + 96 * k)
-        for k in range(1, RO):
-            iota(v("tab%d" % k), [[0, 4 * TS]])
-        ts(v("w128b"), v("n15", 0, 128), 15.0, Op.is_equal)
-        tt(v("mw15"), v("mw"), v("w128b"), Op.mult)
-        cp(v("bof"), v("bo"))
-        ts(v("tr"), v("i32k"), MF_, Op.add, float(R), Op.add)
-        fill(v("vm"), 255.0)
-        ts(v("vst0"), v("vhi"), C14, Op.mult)
-        ts(v("vlo"), v("vlo"), C15, Op.mult)
-        tt(v("vst0"), v("vst0"), v("vlo"), Op.add)
-        for t in range(1, RO):
-            ts(col(36 + t), C14, 2.0 * t, Op.mult)
-            act(v("vst%d" % t), v("vst0"), Fn.Identity, bias=col(36 + t))
+    X = v("hh", 0, R)
+    for i, q in enumerate(HOME):
+        a, b = 64 * i, min(P0, 64 * i + 64)
+        copy(q, v("xg", 16 * a, 16 * b), ind(X, v("post16", a, b)))
+    for c in range(4):
+        a, b = 128 * c, min(P0, 128 * c + 128)
+        for m in range(16):
+            mm(v("p%d" % (2 + c), a, b), fam("hm", m), v("xg", 16 * a + m, 16 * b, 16), m == 0, m == 15)
+        tt(v("live", a, b), v("slot", a, b), v("p%d" % (2 + c), a, b), Op.is_equal)
 
-    deferred = []
+    def count_full(n):
+        mm(v("p0", 0, n), v("bo"), v("live", 0, n), True, True)
+        ts(v("full", 0, n), v("p0", 0, n), 13.5, Op.is_ge)
+        scan(v("scan", 0, n), v("full", 0, n), v("sd1", 0, n), 0.0, Op.add, Op.max)
+        for h in range(2):
+            act(v("junk%d" % h, 0, n), v("scan", 0, n), Fn.Sign, bias=HB[h], scale=-1.0, accum=v("cm%d" % h, 0, 1))
 
+    count_full(P0)
     for t in range(RO):
         nq = P0 + SP * t
-        nc = nq // 16
+        ne = max(P0, nq - SP)
         last = t == RO - 1
         xa = ["hh", "x1", "x2"][t]
         xb = ["x1", "x2", "x1"][t]
         Xa = v(xa, 0, R)
         Xb = v(xb, 0, R)
-        tab, plr, pls, bw, bs, mf, arr = [n + str(t) for n in ("tab", "plr", "pls", "bw", "bs", "mf", "arr")]
+        tab, plr, pls, lst, bw, mf, arr = [n + str(t) for n in ("tab", "plr", "pls", "lst", "bw", "mf", "arr")]
+        pl16, lq16 = v(lst, 8, 10), v(lst, 0, 8)
+        bs = v(bw, 32 * r, 32 * r + 32)
         p0 = lambda a=0, b=512: v("p0", a, b)
         p1 = lambda a=0, b=512: v("p1", a, b)
 
-        mm(p0(0, nq), v("bo"), v("live", 0, nq), True, True)
-        ts(v("full", 0, nq), p0(0, nq), 13.5, Op.is_ge)
-        run("v", lambda: g.vector.tensor_tensor_scan(v("scan")[0], v("full")[0], v("sd1")[0], 0.0, Op.add, Op.max),
-            v("full")[1] + v("sd1")[1], v("scan")[1])
-        act(v("junk"), v("scan"), Fn.Sign, bias=HB, scale=-1.0, accum=v("acc", 0, 1))
-        ts(v("cmpv", 0, TS), v("scan"), HB1, Op.is_le, 2.0, Op.mult)
-        red(v("acc", 1, 2), v("cmpv", 0, TS + 1), Op.add)
-        ts(v(pls), v("acc"), 0.5, Op.mult, 272.0 + TS * r, Op.add)
-        send([v(pls)] * 3, [v("plr%d" % t, 2 * place(q), 2 * place(q) + 2) for q in others], "rp%d" % t)
-        arrives([(plr, 0, 6)], "rp%d" % t)
-        if t > 0:
-            deferred[0]()
-        ts(v("pl16"), v("acc"), 0.5, Op.mult, 272.0, Op.add)
+        stage[0] = "list"
+        scan(v("scan", ne, TS), v("full", ne, TS), v("sd1", ne, TS), v("scan", ne - 1, ne), Op.add, Op.max)
+        for h in range(2):
+            ts(v("cm%d" % h, 1, 1 + TS - ne), v("scan", ne, TS), HB[h], Op.is_le, 2.0, Op.mult)
+            red(v("acc", h, h + 1), v("cm%d" % h, 0, 1 + TS - ne), Op.add)
+        ts(v(pls), v("acc"), 0.5, Op.mult, ne / 2 + TS * r, Op.add)
+        send([v(pls)] * 3, [v(plr, 2 * place(q), 2 * place(q) + 2) for q in others], [v(plr)], "rp%d" % t)
+        ts(pl16, v("acc"), 0.5, Op.mult, ne / 2, Op.add)
         scat(v(tab), v(pls), v("dat", 32 * r, 32 * r + 32))
-        cp(v("lp"), ind(v("live"), v("pl16")))
-        cp(v("postp"), ind(v("postf"), v("pl16")))
+        stage[0] = "rows"
+        cp(v("lp"), ind(v("live"), pl16))
+        cp(v("postp"), ind(v("postf"), pl16))
         cp(v("ps16"), v("postp"))
-        mm(p1(0, 32), v("px"), v("lp"), True, True)
-        scat(v("live"), v("pl16"), v("z32"))
+        mm(p0(0, 32), v("px"), v("lp"), True, True)
+        ts(v("oa"), p0(0, 32), 0.0, Op.max)
+
+        def row_list(out, one):
+            mm(p0(0, 2), v("ident"), v("kd", 0, 2), True, False)
+            for j in range(16):
+                mm(p0(0, 2), fam("em", j), v(one, j, 32, 16), False, j == 15)
+            cp(v(out), p0(0, 2))
+
+        row_list("lac", "oa")
+        stage[0] = "absorb"
+        nh = HELP[t]
+        own = R0 - 512 * nh
         if t == 0:
-            constants_b()
-        pieces = []
-        a = 384 * t
-        o = 0
-        for w in AB:
-            pieces.append((a, a + w, 16 * o))
-            a += w
-            o += w
-
-        def absorb(i):
-            a, b, c = pieces[i]
-            w = 16 * (b - a)
-            tt(v(xb, c, c + w), ind(Xa, v("ab16", a, b)), v("xd", c, c + w), Op.max)
-
-        absorb(0)
-        act(v(xb, R0, R), v(xa, R0, R))
-        ts(v("oa"), p1(0, 32), 0.0, Op.max)
-        mm(p0(0, 32), v("mw"), v("oa"), True, False)
-        mm(p0(0, 32), v("one0"), v("k16"), False, True)
-        cp(v("la16"), p0(0, 32))
-        tt(v("laf"), v("dg"), p0(0, 32), Op.mult)
+            for i in range(3):
+                a, b = third * i, min(own, third * i + third)
+                if a < b:
+                    cp(v("xd", a, b), v("hh", a, b))
+        for a in range(0, own, 1024):
+            b = min(own, a + 1024)
+            tt(v(xb, a, b), ind(Xa, v("ab16", 384 * t + a // 16, 384 * t + b // 16)), v("xd", a, b), Op.max)
+        for i, a in enumerate(range(own, R0, 512)):
+            act(v("md", a - own, a - own + 512), ind(Xa, v("ab16", 384 * t + a // 16, 384 * t + a // 16 + 32)))
+            pb = v("p%d" % (6 + i % 2))
+            mm(pb, v("ident"), v(xa, a, a + 512), True, True)
+            tt(v(xb, a, a + 512), v("md", a - own, a - own + 512), pb, Op.max)
+        if not last and HELP[t + 1] < 12:
+            dma("y", v("xd", 0, R0 - 512 * HELP[t + 1]), v(xb, 0, R0 - 512 * HELP[t + 1]), 16e5)
+        stage[0] = "tab"
         for (c0, c1, d0, d1) in ((0, 2 * r, 0, 32 * r), (2 * r, 6, 32 * r + 32, 128)):
             if c1 > c0:
                 scat(v(tab), v(plr, c0, c1), v("dat", d0, d1))
-        qh = (nq // 2) // 16 * 16
-        halves = ((0, qh, "p2"), (qh, nq, "p6"))
-        for (qa, qb, pn) in halves:
-            act(v("ng", 16 * qa, 16 * qb), ind(v(tab), v("near16", qa, qb)))
-        for i in range(1, len(pieces)):
-            absorb(i)
+        chunks = [(c, 128 * c, min(nq, 128 * c + 128)) for c in range(4)]
+        parts = [(h, chunks[a][1], chunks[b - 1][2], chunks[a:b]) for h, (a, b) in enumerate(PARTS)]
+        for c, a, b in chunks:
+            stage[0] = "near%d" % c
+            copy(NEAR[t][c], v("ng", 16 * a, 16 * b), ind(v(tab), v("near16", a, b)))
+        stage[0] = "split"
         XS = v("xs")
         cp(XS, ind(Xb, v("ps16")))
-        cp(v("xs2"), XS)
-        tt(v("ma"), ind(XS, v("la16")), v("xs2"), Op.max)
-        cp(v("xg", 0, 16 * VQ[0]), ind(Xb, v("post16", 0, VQ[0])))
-        mm(p1(0, 32), v("ck", 0, 128), v("ones", 0, 32), True, False)
-        mm(p1(0, 32), v("ibig"), v("lp"), False, False)
+        cp(v("ac"), ind(XS, v("lac")))
+        tt(v("ma"), ind(v("ac"), v("kx16")), XS, Op.max)
+        mm(p0(0, 32), v("ck", 0, 128), v("ones", 0, 32), True, False)
+        mm(p0(0, 32), v("ibig"), v("lp"), False, False)
         for m in range(16):
-            mm(p1(0, 32), fam("rx", m), v("xs", m, 512, 16), False, False)
+            mm(p0(0, 32), fam("rx", m), v("xs", m, 512, 16), False, False)
         for m in range(16):
-            mm(p1(0, 32), fam("rmp", m), v("ma", m, 512, 16), False, m == 15)
-        tr(v("ktk"), p1(0, 32))
+            mm(p0(0, 32), fam("rmp", m), v("ma", m, 512, 16), False, m == 15)
+        tr(v("ktk"), p0(0, 32))
+        scan(v("kts"), v("rst", 0, 32), v("ktk"), 0.0, Op.add, Op.max)
         for h in range(2):
-            red(v("kmx", h, h + 1), v("ktk", 16 * h, 16 * h + 16), Op.max)
-        for h in range(2):
-            ts(v("obt", 16 * h, 16 * h + 16), v("ktk", 16 * h, 16 * h + 16), v("kmx", h, h + 1), Op.is_equal)
+            ts(v("obt", 16 * h, 16 * h + 16), v("ktk", 16 * h, 16 * h + 16), v("kts", 16 * h + 15, 16 * h + 16), Op.is_equal)
         tr(v("ob"), v("obt"))
-        mm(p0(0, 32), v("mw"), v("ob"), True, False)
-        mm(p0(0, 32), v("one0"), v("k16"), False, True)
-        tt(v("lbf"), v("dg"), p0(0, 32), Op.mult)
-        for h in range(2):
-            red(v("lbc_f", h, h + 1), v("lbf", 16 * h, 16 * h + 16), Op.add)
-        cp(v("lbc"), v("lbc_f"))
-        cp(v(bs), ind(XS, v("lbc")))
-        send([v(bs)] * 3, [v("bw%d" % t, 32 * r, 32 * r + 32)] * 3, "rb%d" % t)
-        if not last:
-            dma("y", v("xd"), v(xb, 0, R0))
-        cp(v("lb16"), p0(0, 32))
-        cp(v(bw, 32 * r, 32 * r + 32), v(bs))
-        fill(v(bw, 128, 144), 8192.0)
-        for q in others:
-            arrives([(bw, 32 * q, 32 * q + 32)], "rb%d" % t)
+        row_list("lbc", "ob")
+        cp(bs, ind(XS, v("lbc")))
+        send([bs] * 3, [bs] * 3, [v(bw, 32 * q, 32 * q + 32) for q in others], "rb%d" % t)
 
-        if t == 0:
-            act(v("hm"), v("e16"), scale=KN32)
-            iota(v("xg", 16 * P0, XW), [[0, XW - 16 * P0]], -1)
-        for (a, b) in ((VQ[1], 256), (256, nq)):
-            act(v("xg", 16 * a, 16 * b), ind(Xb, v("post16", a, b)))
-        if t > 0:
-            deferred[1]()
-        for (qa, qb, pn) in halves:
-            for j in range(16):
-                mm(v(pn, qa, qb), fam("nm", j), v("ng", 16 * qa + j, 16 * qb, 16), j == 0, j == 15)
-            act(v("ff", qa, qb), v(pn, qa, qb), Fn.Relu)
-        cp(v("xg", 16 * VQ[0], 16 * VQ[1]), ind(Xb, v("post16", VQ[0], VQ[1])))
-        if t == 0:
-            constants_c()
-        mm(v("p3", 0, nq), v("ident"), v("ctr", 0, nq), True, True)
+        for i, q in enumerate(SLOT[t]):
+            a, b = 64 * i, min(nq, 64 * i + 64)
+            stage[0] = "slot%d" % (i // 2)
+            copy(q, v("xg", 16 * a, 16 * b), ind(Xb, v("post16", a, b)))
 
-        chunks = [(c, min(nq, 128 * c + 128) - 128 * c) for c in range(4)]
-        mm(v("p5"), v("ones", 0, 128), v("cka"), True, False)
-        for c in range(4):
-            gc = v("p5", 128 * c, 128 * c + 128)
-            mm(gc, v("live", 128 * c, 128 * c + 128), v("ibig"), False, False)
-            mm(gc, v("ctr", 128 * c, 128 * c + 128), v("bo14c"), False, False)
-        flip = [0]
-        pend = []
+        for h, qa, qb, cs in parts:
+            stage[0] = "first%d" % h
+            for c, a, b in cs:
+                mm(p1(a - qa, b - qa), v("nsp"), v(tab, TS * r + a, TS * r + b), True, False)
+                for j in range(16):
+                    mm(p1(a - qa, b - qa), fam("nm", j), v("ng", 16 * a + j, 16 * b, 16), False, j == 15)
+            act(v("ff", qa, qb), p1(0, qb - qa), Fn.Relu)
+            nl = (qb - qa) // 16
+            for k in range(16):
+                mm(p1(0, nl), fam("e16", k), v("ff", qa + k, qb, 16), k == 0, k == 15)
+            for i, (c, a, b) in enumerate(cs):
+                mm(p1(32 + 8 * i, 40 + 8 * i), v("ff", a, a + 128), v("g8"), True, True)
+            ts(v("tgl", qa // 16, qa // 16 + nl), p1(0, nl), -1.0, Op.mult, 128.0, Op.add)
+            cp(v("wt", qa, qa + 128 * len(cs), 16), p1(32, 32 + 8 * len(cs)))
+            act(v("bt", qa, qb), ind(v(bw, 0, 144), v("tgl", qa // 16, qa // 16 + nl)))
 
-        def xm(m, a=0, b=nq):
-            return v("xg", 16 * a + m, 16 * b, 16)
-
-        def s_unit(m, other, dst, sums):
-            pb = ("p6", "p7", "p1")[flip[0] % 3]
-            flip[0] += 1
-            mm(v(pb, 0, nq), v("ident"), xm(m), True, False)
-            mm(v(pb, 0, nq), v("nid"), other, False, True)
-            act(v(dst, m * 480, m * 480 + nq), v(pb, 0, nq), Fn.Relu)
-            return (sums, m, dst, chunks)
-
-        def add(u):
-            sums, m, dst, cs = u
-            for c, n in cs:
-                mm(part("p5", n, 128 * c + m, 128 * c + 128, 16), v(dst, m * 480 + 128 * c, m * 480 + 128 * c + n), v(sums), False, False)
-
-        def pipe(u):
-            pend.append(u)
-            if len(pend) > LAG:
-                add(pend.pop(0))
-
-        def v_unit(m, pb, dst, sums, a, b):
-            tt(v(dst, m * 480 + a, m * 480 + b), xm(m, a, b), v(pb, a, b), Op.max)
-            pipe((sums, m, dst, [x for x in chunks if a <= 128 * x[0] < b]))
-
-        def distances(other, pb, dst, sums, su, a):
-            vm_ = list(range(su))
-            sm_ = list(range(su, 16))
-            while vm_ or sm_:
-                if sm_ and (not vm_ or len(sm_) * su >= (len(vm_) - LEAD) * (16 - su)):
-                    pipe(s_unit(sm_.pop(0), other, dst, sums))
-                else:
-                    v_unit(vm_.pop(0), pb, dst, sums, a, nq)
-
-        for m in range(SU1):
-            v_unit(m, "p3", "mc", "rgp", 0, 256)
-        for k in range(16):
-            mm(p0(0, nc), fam("e16", k), v("ff", k, nq, 16), k == 0, k == 15)
-        for c in range(4):
-            mm(v("p2", 8 * c, 8 * c + 8), v("ff", 128 * c, 128 * c + 128), v("g8"), True, True)
-        ts(v("tgl", 0, nc), p0(0, nc), -1.0, Op.mult, 128.0, Op.add)
-        act(v("bt", 0, nq), ind(v(bw, 0, 144), v("tgl", 0, nc)))
-        mm(v("p4", 0, nq), v("ident"), v("bt", 0, nq), True, True)
-        for c, n in chunks:
-            mm(part("p5", n, 128 * c, 128 * c + 128, 1), v("bt", 128 * c, 128 * c + n), v("bo14b"), False, False)
-        distances(v("ctr", 0, nq), "p3", "mc", "rgp", SU1, 256)
-        distances(v("bt", 0, nq), "p4", "md", "rgn", SU2, 0)
-        while pend:
-            add(pend.pop(0))
-        mm(v("p5"), v("ones", 0, 128), v("ckb"), False, True)
-
-        cp(v("kt"), v("p5", 1, 512, 2))
-        tt(v("k1"), v("p5", 0, 512, 2), v("kt"), Op.max)
-        prev, w = "k1", 256
-        for nxt in ("k2", "k3", "km"):
-            w //= 2
-            tt(v(nxt), v(prev, 0, 2 * w, 2), v(prev, 1, 2 * w, 2), Op.max)
-            prev = nxt
-        cp(v("kmi"), v("km"))
-        ts(v("kmf"), v("km"), 15.5, Op.is_ge)
-        ts(v("kma"), v("kmi"), 15, Op.bitwise_and)
-        tt(v("wt", 0, 512, 16), v("kmf"), v("p2", 0, 32), Op.mult)
-        cp(v("wt", 1, 512, 16), v("kma"))
-        for c in range(4):
-            mm(v("p%d" % (c // 2), 128 * (c % 2), 128 * (c % 2) + 128), v("wt", 128 * c, 128 * c + 128), v("ident"), True, True)
-        cp(v("tq", 32, 288), v("p0", 0, 256))
-        act(v("tq", 288, 32 + nq), v("p1", 0, nq - 256))
-        banks = ["p3", "p4", "p2", "p6", "p7", "p0", "p1", "p5"]
-        for k in range(8):
-            mm(v(banks[k], 0, nq + 1), v("lg", 128 * k, 128 * k + 128), v("tq", 31, 32 + nq), True, True)
-        for k in range(8):
-            red(v("ms", k, k + 1), v(banks[k], 0, nq + 1), Op.min, True)
-            act(v("zx", 16 * k, 16 * k + 16), v("r16"), scale=v("ms", k, k + 1))
-        mm(p0(0, 8), v("zx"), v("cs"), True, True)
-        cp(v("ls16"), p0(0, 8))
-        cp(v(mf), ind(v("xg"), v("ls16")))
-        send([v(mf, 32 * q, 32 * q + 32) for q in others],
-             [v("arr%d" % t, 32 * place(q), 32 * place(q) + 32) for q in others], "rm%d" % t)
-        arrives([(arr, 0, 96)], "rm%d" % t)
-
-        tt(v("mb"), ind(XS, v("lb16")), v("xs2"), Op.max)
-        cp(v("lsi"), p0(0, 8))
-        ts(v("lqi"), v("lsi"), 4, Op.arith_shift_right)
-        ts(v("lmi"), v("lsi"), 15, Op.bitwise_and)
-        cp(v("lq16"), v("lqi"))
-        cp(v("lm16"), v("lmi"))
-        if t == 0:
-            constants_d()
-        for h in range(2):
-            red(v("lac_f", h, h + 1), v("laf", 16 * h, 16 * h + 16), Op.add)
-        cp(v("lac"), v("lac_f"))
-        act(v("ac"), ind(XS, v("lac")))
-        if not last:
-            act(v("lgt"), ind(v("live"), v("lq16")))
-        act(v("oh"), ind(v("miw"), v("lm16")))
-        act(v("pg"), ind(v("postf"), v("lq16")))
+        stage[0] = "go"
+        tt(v("mb"), ind(bs, v("kx16")), XS, Op.max)
         mm(p1(0, 32), v("ck", 0, 128), v("ones", 0, 32), True, False)
         mm(p1(0, 32), v("ibig"), v("lp"), False, False)
         for m in range(16):
             mm(p1(0, 32), fam("rmp", m), v("ma", m, 512, 16), False, False)
-        for m in range(16):
-            mm(p1(0, 32), fam("hm", m), v("mb", m, 512, 16), False, False)
-        mm(p1(0, 32), v("bo14p"), v(bs), False, False)
+        for m in range(32):
+            mm(p1(0, 32), fam("rx", m // 2), v("mb", m // 2, 512, 16), False, False)
+        mm(p1(0, 32), v("bo14p"), bs, False, False)
         mm(p1(0, 32), v("bo14n"), v("ac"), False, True)
-        if not last:
-            tt(v("lut"), v("lgt"), v("oh"), Op.subtract)
-            scat(v("live"), v("lq16"), v("lut"))
         ts(v("go"), p1(0, 32), 15.5, Op.is_ge)
         ts(v("nog"), p1(0, 32), 15.5, Op.is_lt)
-        mm(p0(0, 32), v("px"), v("nog"), True, True)
-        tt(v("pgm"), v("pg"), v("oh"), Op.mult)
-        mm(v("p4", 0, 32), v("bof"), v("pgm", 32 * r, 32 * r + 32), True, True)
+        mm(p1(0, 32), v("px"), v("nog"), True, True)
         if not last:
-            tt(v("lpn"), v("lp"), v("go"), Op.subtract)
-            scat(v("live"), v("pl16"), v("lpn"))
-        ts(v("rw"), p0(0, 32), 0.0, Op.max)
-        ts(v("fo"), v(mf, 32 * r, 32 * r + 32), 0.0, Op.is_ge, 2.0 ** -17, Op.max)
-        ts(v("ra"), v("p4", 0, 32), 32768.0, Op.add)
-        tt(v("ownv"), v("ra"), v("fo"), Op.mult)
-        mm(v("p7", 0, 32), v("mw15"), v("rw"), True, True)
+            mm(p1(32, 64), v("bo"), v("go"), True, True)
+            ts(v("thr"), p1(32, 64), -301.0, Op.mult, 13 * 301 - 0.5, Op.add)
+            tt(v("lval", 128, 160), v("lp"), v("go"), Op.subtract)
+        ts(v("rw"), p1(0, 32), 0.0, Op.max)
+        mm(p1(0, 32), v("mw15"), v("rw"), True, True)
+        tt(v("hw"), v("vst%d" % t, 0, 512, 16), p1(0, 32), Op.add)
+        stage[0] = "homes"
+        tt(v("spa"), v("postp"), v("tr"), Op.subtract)
+        tt(v("spb"), v("spa"), v("go"), Op.mult)
+        tt(v("spc"), v("spb"), v("tr"), Op.add)
+        cp(v("spl16"), v("spc"))
+        for a in range(0, 32, 8):
+            scat(v("hh"), v("spl16", a, a + 8), v("vst%d" % t, 16 * a, 16 * a + 128))
+        cp(v("vm", 32 * r, 32 * r + 32), v("hw"))
+        if not last:
+            act(v("nearp"), ind(v("nearf"), pl16))
+            cp(v("near16", nq, nq + 32), v("nearp"))
+            act(v("nearf", nq, nq + 32), v("nearp"))
+
+        flip = [0]
+        for h, qa, qb, cs in parts:
+            w, wg = qb - qa, 128 * len(cs)
+            ph, pg_ = "p%d" % (2 + h % 2), "p%d" % (4 + h % 2)
+            mm(v(pg_, 0, wg), v("ones", 0, 128), v("cka", 0, wg), True, False)
+            for c, a, b in cs:
+                mm(v(pg_, a - qa, a - qa + 128), v("live", a, a + 128), v("ibig"), False, False)
+            for d, (other, dst, sums) in enumerate((("ctr", "mc", "rgp"), ("bt", "md", "rgn"))):
+                su = SU[t][h][d]
+                stage[0] = "dist%d%d" % (h, d)
+                if su:
+                    mm(v(ph, 256 * d, 256 * d + w), v("ident"), v(other, qa, qb), True, True)
+                for c, a, b in cs:
+                    mm(v(pg_, a - qa, a - qa + 128, 1, b - a), v(other, a, b), v(signs(su)[1 - d]), False, False)
+                o = 16 * qa
+                step = 512 // w
+                for m0, m1 in [(m, m + 1) for m in range(su)] + [(m, min(16, m + step)) for m in range(su, 16, step)]:
+                    if m0 < su:
+                        tt(v(dst, o + m0 * w, o + m1 * w), v("xg", o + m0, 16 * qb, 16), v(ph, 256 * d, 256 * d + w), Op.max)
+                    else:
+                        pb = "p%d" % (6 + flip[0] % 2)
+                        flip[0] += 1
+                        for m in range(m0, m1):
+                            e = m - m0
+                            mm(v(pb, e * w, e * w + w), v("ident"), v("xg", o + m, 16 * qb, 16), True, False)
+                            mm(v(pb, e * w, e * w + w), v("nid"), v(other, qa, qb), False, True)
+                        act(v(dst, o + m0 * w, o + m1 * w), v(pb, 0, (m1 - m0) * w), Fn.Relu)
+                    for k in range(m0, m1):
+                        for c, a, b in cs:
+                            mm(v(pg_, a - qa + k, a - qa + 128, 16, b - a), v(dst, o + k * w + a - qa, o + k * w + b - qa), v(sums), False, False)
+            mm(v(pg_, 0, wg), v("ones", 0, 128), v("ckb", 0, wg), False, True)
+
+            kt, kmi, kma = "kt%d" % (h % 2), "kmi%d" % (h % 2), "kma%d" % (h % 2)
+            end = h == len(parts) - 1
+            stage[0] = "offer%d" % h
+            scan(v(kt, 0, wg), v("rst", 0, wg), v(pg_, 0, wg), 0.0, Op.add, Op.max)
+            cp(v(kmi, 0, wg // 16), v(kt, 15, wg, 16))
+            ts(v("wt", qa + 7, qa + wg, 16), v(kt, 15, wg, 16), 15.5, Op.is_lt)
+            ts(v(kma, 0, wg // 16), v(kmi, 0, wg // 16), 15, Op.bitwise_and)
+            cp(v("wt", qa + 1, qa + wg, 16), v(kma, 0, wg // 16))
+            for c, a, b in cs:
+                mm(v(ph, a - qa, b - qa), v("wt", a, a + 128), v("ident", 0, b - a), True, True)
+            if not end:
+                act(v("tq", qa, qb), v(ph, 0, w))
+                keys, banks = v("tq", qa, qb), [pg_, ph]
+            else:
+                cp(v("tq", qa + 16, qb + 16), v(ph, 0, w))
+                keys, banks = v("tq", qa + 15, qb + 16), [pg_, "p6", "p7", ph]
+            per = min(512 // keys[2], 8 // len(banks))
+            for k in range(0, 8, per):
+                pb = banks[k // per % len(banks)]
+                for e in range(per):
+                    mm(v(pb, keys[2] * e, keys[2] * (e + 1)), fam("lg", k + e), keys, True, True)
+                for e in range(per):
+                    red(v("ms%d" % h, k + e, k + e + 1), v(pb, keys[2] * e, keys[2] * (e + 1)), Op.min, True)
+            if 0 < h and not end:
+                tt(v("mt%d" % h), v("ms%d" % h), v("mt%d" % (h - 1) if h > 1 else "ms0"), Op.min)
+        if not last:
+            scat(v("ctr"), pl16, v("ac"))
+            act(v("ctr", nq, nq + 32), bs)
+        for k in range(8):
+            ts(v("zx", 16 * k, 16 * k + 16), v("r16"), v("ms%d" % h, k, k + 1), Op.mult, v("mt%d" % (h - 1) if h > 1 else "ms0", k, k + 1), Op.min)
+        mm(p0(0, 8), v("zx"), v("cs"), True, True)
+        cp(v("ls16"), p0(0, 8))
+        cp(v(mf), ind(v("xg"), v("ls16")))
+        send([v(mf, 32 * q, 32 * q + 32) for q in others],
+             [v(arr, 32 * place(q), 32 * place(q) + 32) for q in others], [v(arr)], "rm%d" % t)
+
+        stage[0] = "book"
+        cp(v("lsi"), p0(0, 8))
+        ts(v("lqi"), v("lsi"), 4, Op.arith_shift_right)
+        ts(v("lmi"), v("lsi"), 15, Op.bitwise_and)
+        cp(lq16, v("lqi"))
+        cp(v("lm16"), v("lmi"))
+        act(v("oh"), ind(v("miw"), v("lm16")))
+        if not last:
+            act(v("lgt"), ind(v("live"), lq16))
+            tt(v("lval", 0, 128), v("lgt"), v("oh"), Op.subtract)
+            scat(v("live"), v(lst), v("lval"))
+            count_full(nq)
+        act(v("pg"), ind(v("postf"), lq16))
+        tt(v("pgm"), v("pg"), v("oh"), Op.mult)
+        mm(p1(0, 32), v("bof"), v("pgm", 32 * r, 32 * r + 32), True, True)
         for k in range(16):
-            mm(v("p6", 0, 8), fam("e16f", k), v("pgm", k, 128, 16), k == 0, k == 15)
-
-        def split_list():
-            tt(v("spa"), v("postp"), v("tr"), Op.subtract)
-            tt(v("spb"), v("spa"), v("go"), Op.mult)
-            tt(v("spa"), v("spb"), v("tr"), Op.add)
-            cp(v("spl16"), v("spa"))
-
-        def split_homes(t=t):
-            tt(v("hw"), v("vst%d" % t, 0, 512, 16), v("p7", 0, 32), Op.add)
-            cp(v("rl16"), v("p6", 0, 8))
-            cp(v("vm", 32 * r, 32 * r + 32), v("hw"))
-            scat(v("hh"), v("spl16"), v("vst%d" % t))
-            scat(v("hh"), v("rl16"), v("vm"))
-
-        def arrival_homes(t=t):
-            ts(v("hd"), v("hw"), -255.0, Op.add)
-            for k in range(3):
-                tt(v("eq", 32 * k, 32 * k + 32), v("fa", 32 * k, 32 * k + 32), v("wv"), Op.is_equal)
-            for k in range(3):
-                tt(v("fa", 32 * k, 32 * k + 32), v("eq", 32 * k, 32 * k + 32), v("hd"), Op.mult)
-            ts(v("hh", R0 + 96 * t, R0 + 96 * t + 96), v("fa"), 255.0, Op.add)
-
-        def homes(t=t):
-            split_homes(t)
-            arrival_homes(t)
-
-        def rest(t=t, nq=nq):
-            cp(v("wi"), v("wv"))
-            ts(v("wr"), v("wi"), 8191, Op.bitwise_and)
-            cp(v("wd"), v("wr"))
-            tt(v("wb"), v("wd"), v("postp"), Op.subtract)
-            tt(v("wd"), v("wb"), v("rwf"), Op.mult)
-            tt(v("postf", nq, nq + 32), v("wd"), v("postp"), Op.add)
-            if t < RO - 1:
-                cp(v("post16", nq, nq + 32), v("postf", nq, nq + 32))
-                act(v("nearp"), ind(v("nearf"), v("pl16")))
-                cp(v("near16", nq, nq + 32), v("nearp"))
-                act(v("nearf", nq, nq + 32), v("nearp"))
-                scat(v("ctr"), v("pl16"), v("ac"))
-                act(v("ctr", nq, nq + 32), v("bs%d" % t))
-                split_list()
-
+            mm(p1(32, 40), fam("e16f", k), v("pgm", k, 128, 16), k == 0, k == 15)
+        ts(v("ra"), v(mf, 32 * r, 32 * r + 32), 0.0, Op.is_lt, 8192.0, Op.mult)
+        tt(v("ownv"), v("ra"), p1(0, 32), Op.add)
+        cp(v("rl16"), p1(32, 40))
+        scat(v("hh"), v("rl16"), v("vm"))
+        ts(v("hd"), v("hw"), -255.0, Op.add, N14, Op.mult)
         if last:
-            split_list()
-            split_homes()
-            dma("y", (T.yh[0:16:2, :], []), (T["hh"][14:128:16, 0:R0], [("hh", 0, R0)]))
-            dma("s", (T.yh[1:16:2, :], []), (T["hh"][15:128:16, 0:R0], [("hh", 0, R0)]))
+            dma("y", (T.yh[0:16:2, :], []), (T["hh"][14:128:16, 0:R0], [("hh", 0, R0, 1)]), 1e5)
+            dma("s", (T.yh[1:16:2, :], []), (T["hh"][15:128:16, 0:R0], [("hh", 0, R0, 1)]), 1e5)
+            dma("y", (T.ypost[:, 0:nq], []), v("postf", 0, nq), 2.5e5)
+            ts(v("ya1", 0, 192), v("x1", R0, R0 + 192), CF, Op.mult)
+            ts(v("ya2", 0, 192), v("hh", R0, R0 + 192), N14, Op.mult)
+            tt(v("ya3", 0, 192), v("ya1", 0, 192), v("ya2", 0, 192), Op.add)
+            dma("s", (T.ya[:, 0:192], []), v("ya3", 0, 192), 5e4)
 
-        ts(v("eq"), v(arr), 0.0, Op.is_ge)
-        tt(v("fa"), v("eq"), v("atab%d" % t), Op.mult)
-        tt(v("wv"), v("fa", 0, 32), v("ownv"), Op.max)
-        tt(v("wb"), v("fa", 32, 64), v("fa", 64, 96), Op.max)
-        tt(v("wv"), v("wv"), v("wb"), Op.max)
-        ts(v("wf"), v("wv"), 8191.5, Op.is_ge)
+        stage[0] = "moves"
+        if not last:
+            for b in ("x1", "x2"):
+                ts(v(b, R0 + 96 * t, R0 + 96 * t + 96), v(arr), 0.0, Op.max)
+            tt(v("wfa"), v(arr, 0, 32), v(arr, 32, 64), Op.max)
+            tt(v("wfb"), v(arr, 64, 96), v(mf, 32 * r, 32 * r + 32), Op.max)
+            tt(v("wfm"), v("wfa"), v("wfb"), Op.max)
+            tt(v("full", nq, nq + 32), v("wfm"), v("thr"), Op.is_ge)
+        ts(v("fb"), v(arr), 0.0, Op.is_lt, 8192.0, Op.mult)
+        tt(v("fa"), v("fb"), v("atab%d" % t), Op.add)
+        tt(v("wc"), v("fa", 0, 32), v("ownv"), Op.min)
+        tt(v("wb"), v("fa", 32, 64), v("fa", 64, 96), Op.min)
+        tt(v("wv"), v("wc"), v("wb"), Op.min)
+        ts(v("wf"), v("wv"), 8191.5, Op.is_lt)
         tt(v("rwf"), v("rw"), v("wf"), Op.mult)
+        tt(v("wd"), v("wv"), v("postp"), Op.subtract)
+        tt(v("we"), v("wd"), v("rwf"), Op.mult)
+        tt(v("postf", nq, nq + 32), v("we"), v("postp"), Op.add)
+        for k in range(3):
+            tt(v("eq", 32 * k, 32 * k + 32), v("atab%d" % t, 32 * k, 32 * k + 32), v("wv"), Op.is_equal)
+        for k in range(3):
+            tt(v("eh", 32 * k, 32 * k + 32), v("eq", 32 * k, 32 * k + 32), v("hd"), Op.mult)
         if not last:
             tt(v("live", nq, nq + 32), v("go"), v("rwf"), Op.add)
-        ts(v(xb, R0 + 96 * t, R0 + 96 * t + 96), v(arr), 0.0, Op.max)
-        if last:
-            rest()
-            arrival_homes()
+            cp(v("post16", nq, nq + 32), v("postf", nq, nq + 32))
+            ts(v("hh", R0 + 96 * t, R0 + 96 * t + 96), v("eh"), 255.0, Op.add)
         else:
-            deferred = [rest, homes]
-
-    dma("y", (T.ypost[:, :], []), v("postf", 0, 512))
-    ts(v("ya1"), v("x1", R0, R), CF, Op.mult)
-    ts(v("ya2"), v("hh", R0, R), N14, Op.mult)
-    tt(v("ya3"), v("ya1"), v("ya2"), Op.add)
-    dma("y", (T.ya[:, :], []), v("ya3"))
-    for sem, val in total.items():
-        g.wait_ge(T.sem[sem], val)
+            dma("y", (T.ypost[:, nq:512], []), v("postf", nq, 512), 2e4)
+            ts(v("ya1", 192, 288), v(arr), N255, Op.max)
+            tt(v("ya3", 192, 288), v("ya1", 192, 288), v("eh"), Op.add)
+            dma("s", (T.ya[:, 192:288], []), v("ya3", 192, 288), 3e4)
+    emit()

@@ -9,16 +9,19 @@ WP = 672
 XW = 16 * WP
 TS = 544
 BIG = 262144.0
-HOME = "svsssss"
-SLOT = ["vvvvsss", "vvvvvss", "vvvvvsss"]
-NEAR = ["ssss", "ssss", "ssss"]
-HELP = [4, 7, 7]
+HOME = "ssvvsvs"
+SLOT = ["vvvvsss", "vvsvsvs", "vvvvsssv"]
+NEAR = ["ssssvss", "sssssss", "ssssssss"]
+HELP = [8, 3, 7]
 PARTS = [(0, 2), (2, 4)]
-SU = [[(16, 16), (6, 6)]] * 3
-CYCLE, GATHER, SCATTER, WAKE, LOOK, HOP = 0.00087, 1.56, 3.8, 0.13, 0.15, 4.5
+TURN = "vv"
+SU = [[(14, 16), (14, 16)], [(14, 12), (16, 16)], [(16, 16), (16, 12)]]
+CYCLE, GATHER, SCATTER, WAKE, HOP = 0.00087, 1.56, 3.8, 0.15, 4.2
 FIXED = {"v": 0.0, "s": 0.15, "p": 0.0, "g": 0.15}
-START, RATE, PASSES = 1.8, 2e5, 4
-EARLY = {"tab": 8, "near0": 2, "near1": 4, "near2": 4, "first0": 4, "offer0": 3, "offer1": 3, "slot1": 8, "dist11": 3}
+START, RATE, PASSES = 1.8, 3.5e5, 2
+AT = {'rows': 0, 'tab': 0, 'bt0': 3.2, 'split': 6.6, 'bt1': 8.2, 'slot5': 12.6, 'slot7': 19.4, 'list': 20.8, 'near3': 26.5, 'near2': 32.6, 'offer1': 38.1, 'slot0': 41.1, 'absorb': 46.0, 'near6': 50.4, 'first1': 50.8, 'slot3': 53.5, 'near5': 54.4, 'near1': 55.7, 'near7': 56.0, 'dist01': 56.8, 'go': 61.7, 'copy': 62.5, 'dist00': 71.9, 'offer0': 73.4, 'first0': 80.2, 'slot6': 81.5, 'slot2': 81.9, 'slot1': 83.8, 'homes': 89.5, 'near0': 102.7, 'dist10': 108.3, 'moves': 108.5, 'near4': 121.2, 'book': 130.4, 'slot4': 133.1, 'dist11': 157.2, 'win': 173.9}
+URGENT = ['moves', 'list', 'split', 'bt0', 'slot3', 'near1', 'near7', 'offer1', 'bt1', 'slot1', 'dist10', 'near5', 'near3', 'copy', 'slot5', 'near2', 'near4']
+LOOK = 0.2
 HOOK = []
 
 SCRATCH = {}
@@ -43,8 +46,9 @@ _b("hh", R + 512)
 _b("xd", R0)
 _b("xg", XW)
 _b("ng mc md", 16 * 480)
-_b("e16 rmp rx nm hm em", 2048)
-_b("e16f", 2048, F)
+_b("nm", 2048)
+_b("e16 rmp rx hm em zi", 144)
+_b("e16f", 144, F)
 _b("postI nearI nsh", P0, I)
 _b("abI", 1152, I)
 _b("ab16", 1152, U)
@@ -62,26 +66,27 @@ for _t in range(RO):
     _b("arr%d" % _t, 96)
     _b("atab%d" % _t, 96, F)
     _b("vst%d" % _t, 512)
-_b("full scan sd1 sd2 junk0 junk1", TS)
+_b("full scan sd1 junk0 junk1", TS)
 _b("cm0 cm1", 130, F)
-_b("cidx", TS, F)
-_b("ident nid ibig bo bo14p bo14n px mw mw15 lga ni u128 w128 wa128 wb128 wc128 bou nsp vm oh lgt dat", 128)
-_b(" ".join("su%dp su%dn su%da su%db" % (i, i, i, i) for i in (range(1, 16) if HOOK else sorted({x for a in SU for b in a for x in b} - {0, 16}))), 128)
+_b("ident nid ibig d14 d15 bo bo14p bo14n bo32 px lga ni dcp cg n15 ck w128 wa128 wb128 wc128 bou nsp vm oh lgt dat", 128)
+_b(" ".join("su%dp su%dn su%da" % (i, i, i) for i in sorted({x for a in SU for b in a for x in b} - {0, 16})), 128)
 _b("lval", 160)
 _b("bof zx pg pgm", 128, F)
 _b("lg", 1024)
-_b("ones n15 ck cka ckb rst", 256)
+_b("ones n15r cka ckb rst", 256)
 _b("kt0 kt1", 256, F)
-_b("wt ff xs ma mb vhi vlo bt", 512)
+_b("wt ff xs ma mb vhi vlo bt tb0 tb1", 512)
 _b("tq", 512)
-_b("fc", 64, F)
-_b("i32k i32 tr whi postp nearp ktk kts spa spb spc ownv ra wv wb wc wd we hd thr", 32, F)
+_b("fc", 32, F)
+_b("cidx i32k i32 tr whi postp nearp ktk kts spa spb spc ownv ra wv wb wc wd we hd thr", 32, F)
 _b("kmi0 kmi1 kma0 kma1", 16, I)
-_b("lp oa obt ob go nog rw rwf wf wfa wfb wfm ac hw", 32)
+_b("sd2 sd3 lp oa obt ob go nog rw rwf wf wfa wfb wfm ac hw", 32)
 _b("g8 rgp rgn kd", 8)
 _b("miw", 16)
-_b("pcol pr", 2, I)
-_b("i16 r16", 16, F)
+_b("pcol", 2, I)
+_b("r16 wk wl", 16, F)
+_b("k5", 5, F)
+_b("h4", 4, F)
 _b("i8 cs ms0 ms1 ms2 ms3 mt1 mt2", 8, F)
 _b("acc", 2, F)
 _b("lac lbc", 2, U)
@@ -91,11 +96,48 @@ _b("lsi lqi lmi", 8, I)
 _b("fa fb eq eh", 96, F)
 _b("ya1 ya2 ya3", 288)
 for _i in range(8):
-    _b("p%d" % _i, 512, F, "psum")
+    _b("p%d" % _i, *((1024, "bfloat16") if _i in (2, 3, 7) else (512, F)), "psum")
 
 NDMA = 28
 SEMAPHORES = ["qv", "qs", "qp", "qg", "sent"] + ["d%d" % i for i in range(NDMA)] + \
     ["%s%d" % (a, t) for a in ("rp", "rb", "rm") for t in range(RO)]
+
+
+def arrange(ops, before, behind, lay, at):
+    n = len(ops)
+    key = [100 * o["at"][1] + at.get(o["at"][0], 999) for o in ops]
+    for i in range(n - 1, -1, -1):
+        key[i] = min([key[i]] + [key[j] for j, gap in behind[i]])
+    left = [len(b) for b in before]
+    ready = [0.0] * n
+    free = {q: 0.0 for q in "vspgydr"}
+    cand = {q: [i for i in range(n) if ops[i]["q"] == q and not left[i]] for q in free}
+    soon = [LOOK if o["at"][0] in URGENT else 0.0 for o in ops]
+    turn = []
+    while len(turn) < n:
+        t0, q = min((max(free[q], min(ready[i] for i in c)), q) for q, c in cand.items() if c)
+        i = min((key[i], i) for i in cand[q] if ready[i] <= t0 + soon[i])[1]
+        cand[q].remove(i)
+        turn.append(i)
+        free[q] = max(t0, ready[i]) + ops[i]["time"]
+        for j, gap in behind[i]:
+            ready[j] = max(ready[j], free[q] + gap)
+            left[j] -= 1
+            if not left[j]:
+                cand[ops[j]["q"]].append(j)
+    best = (max(free.values()), turn)
+    if PASSES == 0:
+        return best
+    for k in range(PASSES):
+        if k:
+            turn = [turn[k] for k in sorted(range(n), key=lambda k: (-end[turn[k]], -k))]
+            end = lay(turn, behind)
+            turn = [turn[k] for k in sorted(range(n), key=lambda k: (-end[turn[k]], -k))]
+        end = lay(turn, before)
+        turn = [turn[k] for k in sorted(range(n), key=lambda k: (end[turn[k]] - ops[turn[k]]["time"], k))]
+        if best is None or max(end) < best[0]:
+            best = (max(end), turn)
+    return best
 
 
 def rank_program(g, core, T, topo):
@@ -106,7 +148,7 @@ def rank_program(g, core, T, topo):
     ops = []
     acc = {}
     dn = [0]
-    stage = [""]
+    stage = ["", 0]
 
     def meet(a, b):
         if a[0] >= b[1] or b[0] >= a[1]:
@@ -130,7 +172,7 @@ def rank_program(g, core, T, topo):
                             dep[d] = True
                     elif (is_w or w2) and meet(reg[1:], o):
                         dep[d] = True
-        ops.append({"q": q, "fn": fn, "time": time, "lag": lag, "dep": dep, "sem": sem, "early": EARLY.get(stage[0], 0.0), "tag": HOOK[0]() if HOOK else None})
+        ops.append({"q": q, "fn": fn, "time": time, "lag": lag, "dep": dep, "sem": sem, "at": tuple(stage), "tag": HOOK[0]() if HOOK else None})
         me += mine
         for reg in writes:
             ps = SCRATCH[reg[0]][0] == "psum"
@@ -179,25 +221,9 @@ def rank_program(g, core, T, topo):
                 end[i] = at + time
             return end
 
-        way = [0.0] * n
-        for i in range(n - 1, -1, -1):
-            way[i] = ops[i]["time"] + max([way[j] + gap for j, gap in behind[i]] + [0.0])
-        turn = sorted(range(n), key=lambda i: (-way[i], i))
-        best = None
-        for _ in range(PASSES):
-            end = lay(turn, before)
-            turn = [turn[k] for k in sorted(range(n), key=lambda k: (end[turn[k]] - ops[turn[k]]["time"], k))]
-            if best is None or max(end) < best[0]:
-                best = (max(end), turn)
-            turn = [turn[k] for k in sorted(range(n), key=lambda k: (-end[turn[k]], -k))]
-            end = lay(turn, behind)
-            key = [-end[i] - ops[i]["early"] for i in range(n)]
-            for i in range(n - 1, -1, -1):
-                key[i] = min([key[i]] + [key[j] - ops[i]["time"] for j, gap in behind[i]])
-            turn = sorted(range(n), key=lambda i: (key[i], i))
-        order = best[1]
-        if HOOK:
-            HOOK.append(best[0])
+        if len(HOOK) > 2:
+            return HOOK[2](ops, before, behind, lay)
+        order = arrange(ops, before, behind, lay, AT)[1]
         cnt = {}
         known = {q: {} for q in Q}
         tok = {}
@@ -237,7 +263,7 @@ def rank_program(g, core, T, topo):
             b, o, w = ALIAS[b]
             c0, c1 = o + c0, o + (w if c1 is None else c1)
         c1 = SCRATCH[b][1][1] if c1 is None else c1
-        kind = "psum" if SCRATCH[b][0] == "psum" else "two" if SCRATCH[b][2] in (U, "bfloat16") else "four"
+        kind = "two" if SCRATCH[b][2] in (U, "bfloat16") else "four"
         return (T[b][0:n, c0:c1] if s == 1 else T[b][0:n, c0:c1:s], [(b, c0, c1, s)], len(range(c0, c1, s)), kind)
 
     def ind(win, off):
@@ -247,13 +273,17 @@ def rank_program(g, core, T, topo):
         return v("fc", i, i + 1)
 
     def fam(b, m):
+        return v(b, 15 - m, 143 - m)
+
+    def blk(b, m):
         return v(b, 128 * m, 128 * m + 128)
 
     def cyc(out, a):
         return max(64, a[2] * (GATHER if a[3] == "ind" else 0.5 if out[3] == a[3] == "two" else 1))
 
     def tt(out, a, b, op):
-        c = cyc(out, a) if a[3] == "ind" else max(64, a[2] * (1 if "psum" in (a[3], b[3]) else 2))
+        psum = any(SCRATCH[x[1][0][0]][0] == "psum" for x in (a, b))
+        c = cyc(out, a) if a[3] == "ind" else max(64, a[2] * (1 if psum else 2) * (0.5 if out[3] == a[3] == b[3] == "two" else 1))
         run("v", lambda: g.vector.tensor_tensor(out[0], a[0], b[0], op), c, a[1] + b[1], out[1])
 
     def ts(out, a, s1, o1, s2=None, o2=None):
@@ -315,32 +345,35 @@ def rank_program(g, core, T, topo):
         c = max(min(64, lhsT[2]), rhs[2]) * (2 if rhs[3] == "four" else 0.5)
         run("p", lambda: g.tensor.matmul(out[0], lhsT[0], rhs[0], start, stop), c, lhsT[1] + rhs[1], out[1], not (start or stop))
 
+    def turn(out, a, ident):
+        run("p", lambda: g.tensor.transpose(out[0], a[0], ident[0]), 0.5 * max(64, out[2]), a[1] + ident[1], out[1])
+
     def iota(out, pat, base=0, cm=0, flag=True):
         kw = {"allow_small_or_imprecise_dtypes": True} if flag else {}
         run("g", lambda: g.iota(out[0], pat, base, cm, **kw), 2 * out[2], [], out[1])
 
     others = [q for q in range(len(T.cores)) if q != r]
-    NE = 2
 
     def send(bufs, dsts, lands, sem):
-        trs = []
-        regs = []
-        for i, q in enumerate(others):
-            dst = T.cores[q]
-            rid, pid, _ = topo.addr(dst)
-            eng = topo.engines(core, dst)[NE * i:NE * i + NE]
-            trs.append(RemoteDMATransfer(dst_ids=[DstId(rid=rid, pnc=pid)], dma_engine_mask=sum(1 << e for e in eng),
-                                         remote_sem=T.sem[sem], srcs=[bufs[i][0]], dsts=[dsts[i][0]]))
-            regs += bufs[i][1]
-        n = NE * len(others)
-        me = note("g", lambda: g.remote_dma_fused(trs, local_sem=T.sem["sent"]), 0.6, HOP, regs, [], sem=("sent", n))
-        note("r", None, 0.001, 0.0, [], [reg for x in lands for reg in x[1]], after=[me], sem=(sem, n))
+        turns = sorted(range(len(others)), key=lambda i: (others[i] - r) % len(T.cores))
+        mask = topo.mask(core, T.cores[others[0]])
+        ne = len(topo.engines(core, T.cores[others[0]]))
+        calls = [turns] if all(b[0] is bufs[0][0] for b in bufs) else [[i] for i in turns]
+        mine = []
+        for k, call in enumerate(calls):
+            ids = [DstId(rid=topo.addr(T.cores[others[i]])[0], pnc=topo.addr(T.cores[others[i]])[1]) for i in call]
+            one = RemoteDMATransfer(dst_ids=ids, dma_engine_mask=mask, remote_sem=T.sem[sem], srcs=[bufs[call[0]][0]],
+                                    dsts=[dsts[i][0] for i in call])
+            mine.append(note("g", lambda one=one: g.remote_dma_fused([one], local_sem=T.sem["sent"]), 2.6 if sem == "rp0" else 0.6,
+                             HOP - 0.5 * k, bufs[call[0]][1], [], sem=("sent", ne)))
+            if k:
+                ops[mine[k]]["dep"][mine[k - 1]] = False
+        note("r", None, 0.001, 0.0, [], [reg for x in lands for reg in x[1]], after=mine, sem=(sem, ne * len(others)))
 
     def place(q):
         return r - (1 if r > q else 0)
 
     third = R0 // 3
-    fill(v("tab0"), 0.0)
     dma("y", v("postI"), (T.post[:, :], []), 2e5)
     for i in range(3):
         dma("y", v("hh", third * i, third * i + third), (T.rec[:, third * i:third * i + third], []), 5e5, True)
@@ -348,22 +381,28 @@ def rank_program(g, core, T, topo):
     dma("y", v("nearI"), (T.near[:, :], []), 2e5, True)
     dma("y", v("ctr", 0, P0), (T.cen[:, :], []), 1e5, True)
     dma("y", v("abI", 384, 1152), (T.absorb[:, 384:1152], []), 4e5, True)
-    for k in range(1, RO):
-        dma("y", v("tab%d" % k), v("tab0"), 5e5, True)
 
     pI, p15 = v("pcol", 0, 1), v("pcol", 1, 2)
     NI = v("ni")
+    PF, MF_, PB = col(0), col(1), col(2)
     iota(pI, [[0, 1]], 0, 1, False)
+    iota(PF, [[0, 1]], 0, 1)
     iota(NI, [[1, 128]])
+    iota(v("dcp"), [[1, 128]], 0, -1)
+    iota(v("cg"), [[16, 8], [0, 16]])
+    iota(v("zi"), [[1, 144]], -15)
     iota(v("i32k"), [[16, 32]])
     iota(v("i32"), [[1, 32]])
     iota(v("w128"), [[-1, 128]], 128)
     iota(v("slot"), [[16, P0]])
-    iota(v("whi"), [[8, 4], [0, 8]])
-    iota(v("n15"), [[0, 16], [1, 16]])
-    iota(v("i16"), [[1, 16]])
+    iota(v("whi"), [[128, 4], [0, 8]])
+    iota(v("n15"), [[0, 8], [1, 16]])
+    iota(v("n15r"), [[0, 16], [-1, 16]], 15)
     iota(v("i8"), [[16, 8]])
-    iota(v("cidx"), [[1, TS]])
+    iota(v("k5"), [[-16, 5]], 32)
+    iota(v("h4"), [[512, 2], [16, 2]])
+    iota(v("cidx"), [[1, 32]], PD + 1)
+    iota(v("sd1", 0, PD), [[0, PD]])
     iota(v("postf", MD, WP), [[1, 128]], R)
     iota(v("postf", PD, MD), [[0, 32]])
     iota(v("vhi"), [[1, 2], [0, 256]], 26)
@@ -371,100 +410,78 @@ def rank_program(g, core, T, topo):
     for k in range(RO):
         iota(v("atab%d" % k), [[1, 96]], R0 + 96 * k)
         iota(v("bw%d" % k, 128, 144), [[0, 16]], 8192)
+        for q in range(4):
+            iota(v("tab%d" % k, TS * q, TS * q + TS), [[0, TS]])
     iota(v("vm"), [[0, 128]], 255)
     iota(v("wt"), [[0, 512]])
+    for k in (4, 5):
+        iota(v("wt", k, 512, 16), [[0, 32]], 1)
     iota(v("ones"), [[0, 256]], 1)
-    iota(v("nearf", P0, WP), [[0, WP - P0]])
-    iota(v("ctr", P0, WP), [[0, WP - P0]])
     iota(v("xg", 16 * MD, XW, 16), [[0, 128]], -1)
-    for b in ("hh", "x1", "x2"):
-        fill(v(b, R0, R), 0.0)
-    fill(v("live", P0, WP), 0.0)
-    fill(v("full", P0, TS), 0.0)
-    fill(v("ff", P0, 512), 0.0)
-    PF, MF_, PB = col(0), col(1), col(2)
+    for b, a, e in (("hh", R0, R), ("x1", R0, R), ("x2", R0, R), ("live", P0, WP), ("full", P0, TS), ("ff", P0, 512),
+                    ("nearf", P0, WP), ("ctr", P0, WP)):
+        iota(v(b, a, e), [[0, e - a]])
+    for i, w in enumerate((32768, 1, -256, -16, -32768 * 128, -15, 0, 2 ** 23, 0, 0, 0, 0, 32768, 0, 16, 0)):
+        iota(v("wk", i, i + 1), [[0, 1]], w)
     ts(p15, pI, 15, Op.bitwise_and)
-    cp(PF, pI)
     cp(MF_, p15)
     tt(PB, PF, MF_, Op.subtract)
-    for i in range(8):
-        ts(col(8 + i), MF_, float(i), Op.is_equal)
-    C14, C15, N14, CF = col(16), col(17), col(18), col(19)
-    ts(C14, MF_, 14.0, Op.is_equal)
-    ts(C15, MF_, 15.0, Op.is_equal)
+    ts(v("r16"), v("i32", 0, 16), MF_, Op.is_equal)
+
+    def row(i):
+        return v("r16", i, i + 1)
+
+    C14, C15, N14, CF, N255 = row(14), row(15), col(3), col(4), col(5)
     ts(CF, MF_, 13.5, Op.is_le)
     ts(N14, MF_, 13.5, Op.is_gt)
-    ts(col(20), C14, 256.0, Op.mult, C15, Op.add)
-    K32, KN32, KN16, K16c, N255 = col(21), col(22), col(23), col(24), col(25)
-    ts(K32, CF, 32.0, Op.mult)
-    ts(KN32, CF, -32.0, Op.mult)
-    ts(KN16, CF, -16.0, Op.mult)
-    ts(K16c, CF, 16.0, Op.mult)
-    ts(N255, N14, 255.0, Op.mult)
-    HB = (col(26), col(27))
-    ts(HB[0], MF_, 0.5, Op.add)
-    ts(HB[1], MF_, 16.5, Op.add)
-    ts(v("u128"), NI, PB, Op.subtract)
-    for m in range(16):
-        ts(fam("hm", m), v("u128"), float(m), Op.is_equal, col(20), Op.mult)
-    for m in range(16):
-        ts(fam("e16", m), v("u128"), float(m), Op.is_equal)
-    act(v("em"), v("e16"), scale=MF_)
-    act(v("rx"), v("e16"), scale=KN16)
-    act(v("rmp"), v("e16"), scale=K32)
-    act(v("e16f"), v("e16"))
+    ts(N255, MF_, 13.5, Op.is_gt, 255.0, Op.mult)
+    ts(col(6), C14, 256.0, Op.mult, C15, Op.add)
+    ts(v("fc", 8, 13), v("k5"), CF, Op.mult)
+    K32, K16c, KN16, KN32 = col(8), col(9), col(11), col(12)
+    ts(v("fc", 16, 20), v("h4"), MF_, Op.add, 0.5, Op.add)
+    HB = (col(16), col(17))
+    ts(v("e16"), v("zi"), PB, Op.is_equal)
+    ts(v("e16f"), v("zi"), PB, Op.is_equal)
+    for b, w in (("hm", col(6)), ("em", MF_), ("rx", KN16), ("rmp", K32)):
+        ts(v(b), v("zi"), PB, Op.is_equal, w, Op.mult)
     cp(v("post16", 0, P0), v("postI"))
     cp(v("postf", 0, P0), v("postI"))
     act(v("slot"), v("slot"), Fn.Identity, bias=MF_)
-    ts(v("wa128"), v("u128"), 0.0, Op.is_ge)
-    ts(v("wb128"), v("u128"), 15.5, Op.is_le)
-    tt(v("bo"), v("wa128"), v("wb128"), Op.mult)
-    ts(v("g8"), v("i8"), PB, Op.is_equal)
-    ts(v("rgp"), v("g8"), K32, Op.mult)
-    ts(v("rgn"), v("g8"), KN32, Op.mult)
-    ts(v("bo14p"), v("bo"), K16c, Op.mult)
-    ts(v("bo14n"), v("bo"), KN16, Op.mult)
-    ts(v("wc128"), v("u128"), col(8), Op.add)
+    ts(col(20), row(1), -256.0, Op.mult, row(0), Op.add)
+    ts(col(21), row(1), -256.0, Op.mult)
+    for b in ("bo", "bof"):
+        ts(v(b), v("cg"), PB, Op.is_equal)
+    for b, w in (("bo14p", K16c), ("bo14n", KN16), ("bo32", K32), ("nsp", col(21))):
+        ts(v(b), v("cg"), PB, Op.is_equal, w, Op.mult)
+    for b in ("g8", "cs"):
+        ts(v(b), v("i8"), PB, Op.is_equal)
+    for b, w in (("rgp", K32), ("rgn", KN32)):
+        ts(v(b), v("i8"), PB, Op.is_equal, w, Op.mult)
+    ts(v("wc128"), v("n15"), row(0), Op.add)
     tt(v("bou"), v("wc128"), v("bo"), Op.mult)
-    ts(col(37), col(9), -256.0, Op.mult, col(8), Op.add)
-    ts(col(38), col(9), -256.0, Op.mult)
     for j in range(16):
-        ts(fam("nm", j), v("bou"), float(j), Op.is_gt, col(37), Op.mult)
-    ts(v("nsp"), v("bo"), col(38), Op.mult)
-    A0, A1, B = col(33), col(34), [col(48 + i) for i in range(6)]
-    ts(A0, col(12), 32768.0, Op.mult)
-    ts(A1, col(14), 16.0, Op.mult, A0, Op.add)
-    ts(B[0], col(8), 32768.0, Op.mult, col(9), Op.add)
-    for n, (i, w) in enumerate(((10, -256.0), (11, -16.0), (12, -32768.0 * 128), (13, -15.0), (15, 2.0 ** 23))):
-        ts(B[n + 1], col(i), w, Op.mult, B[n], Op.add)
-    ts(v("lga"), NI, A1, Op.mult, B[5], Op.add)
+        ts(blk("nm", j), v("bou"), float(j), Op.is_gt, col(20), Op.mult)
+    for h in range(2):
+        tt(v("wl", 8 * h, 8 * h + 8), v("wk", 8 * h, 8 * h + 8), v("r16", 0, 8), Op.mult)
+        red(col(22 + h), v("wl", 8 * h, 8 * h + 8), Op.add)
+    ts(v("lga"), NI, col(23), Op.mult, col(22), Op.add)
     for k in range(8):
-        ts(col(40 + k), PB, 16.0 * k, Op.is_equal)
-        ts(fam("lg", k), v("lga"), col(40 + k), Op.mult)
-    ts(col(28), MF_, 512.0, Op.add)
-    ts(col(29), MF_, 528.0, Op.add)
-    ts(v("sd2"), v("cidx"), col(28), Op.is_ge, 16.0, Op.mult)
-    ts(v("sd1"), v("cidx"), col(29), Op.is_ge, 84.0, Op.mult)
-    tt(v("sd1", PD, TS), v("sd1", PD, TS), v("sd2", PD, TS), Op.add)
-    ts(v("ident"), NI, PF, Op.is_equal)
-    ts(v("ibig"), v("ident"), BIG, Op.mult)
-    ts(v("nid"), v("ident"), -1.0, Op.mult)
-    ts(v("wa128"), NI, PF, Op.is_gt, -32.0, Op.mult)
+        act(blk("lg", k), v("lga"), scale=v("cs", k, k + 1))
+    ts(v("sd2"), v("cidx"), col(18), Op.is_ge, 16.0, Op.mult)
+    ts(v("sd3"), v("cidx"), col(19), Op.is_ge, 84.0, Op.mult)
+    tt(v("sd1", PD, TS), v("sd2"), v("sd3"), Op.add)
+    for b, w in (("ident", 1.0), ("ibig", BIG), ("nid", -1.0), ("d14", C14), ("d15", C15)):
+        ts(v(b), v("dcp"), 0.0, Op.is_equal, w, Op.mult)
+    ts(v("wa128"), v("dcp"), 0.0, Op.is_gt, -32.0, Op.mult)
     tt(v("wb128"), v("wa128"), v("bo"), Op.mult)
     tt(v("px"), v("wb128"), v("ident"), Op.add)
-    ts(v("mw"), v("bo"), MF_, Op.mult)
-    ts(col(30), PF, 0.0, Op.is_equal)
-    ts(col(31), PF, 1.0, Op.is_equal)
-    ts(col(32), col(30), -BIG, Op.mult)
-    ts(v("kd", 0, 1), MF_, 16.0, Op.mult)
-    ts(v("kd", 1, 2), MF_, 16.0, Op.mult, 256.0, Op.add)
+    ts(v("kd", 0, 2), v("h4", 0, 2), MF_, Op.add, 16.0, Op.mult)
     cp(v("kx16"), v("i32"))
-    ts(v("dat"), v("w128"), col(8), Op.mult, col(9), Op.add)
-    ts(v("ck"), v("n15"), -1.0, Op.mult, 15.0, Op.add)
-    ts(v("ckb"), v("ck"), col(31), Op.mult)
-    ts(v("cka"), v("n15"), 0.0, Op.mult, col(32), Op.add)
-    ts(v("ck"), v("ckb"), col(32), Op.add)
-    ts(v("rst"), v("n15"), 0.0, Op.is_equal, -2.0 ** 22, Op.mult)
+    ts(v("dat"), v("w128"), row(0), Op.mult, row(1), Op.add)
+    ts(v("ckb"), v("n15r"), v("ident", 1, 2), Op.mult)
+    ts(v("cka"), v("ones"), v("ibig", 0, 1), Op.mult, -1.0, Op.mult)
+    ts(v("ck"), v("n15r", 0, 128), v("ident", 1, 2), Op.mult, v("ibig", 0, 1), Op.subtract)
+    ts(v("rst"), v("n15r"), 15.0, Op.is_equal, -2.0 ** 22, Op.mult)
     ts(v("nsh"), v("nearI"), 4, Op.arith_shift_right, 96, Op.bitwise_and)
     tt(v("nearf", 0, P0), v("nsh"), v("nearI"), Op.add)
     cp(v("near16", 0, P0), v("nearf", 0, P0))
@@ -475,42 +492,31 @@ def rank_program(g, core, T, topo):
     def signs(su):
         if su not in made:
             made[su] = ("su%dp" % su, "su%dn" % su)
-            ts(v("su%da" % su), v("n15", 0, 128), su - 0.5, Op.is_ge, -2.0, Op.mult)
-            ts(v("su%db" % su), v("su%da" % su), 1.0, Op.add)
-            tt(v(made[su][0]), v("su%db" % su), v("bo14p"), Op.mult)
+            ts(v("su%da" % su), v("n15"), su - 0.5, Op.is_lt, 0.5, Op.subtract)
+            tt(v(made[su][0]), v("su%da" % su), v("bo32"), Op.mult)
             ts(v(made[su][1]), v(made[su][0]), -1.0, Op.mult)
         return made[su]
 
-    ts(v("pr", 0, 1), pI, 4, Op.arith_shift_right)
-    cp(col(35), v("pr", 0, 1))
-    ts(v("wt", 2, 512, 16), v("whi"), col(35), Op.add)
+    ts(v("wt", 2, 512, 16), v("whi"), PB, Op.add, 1 / 16, Op.mult)
     ts(v("wt", 3, 512, 16), v("whi"), 0.0, Op.mult, MF_, Op.add)
-    for k in (4, 5):
-        ts(v("wt", k, 512, 16), v("whi"), 0.0, Op.mult, 1.0, Op.add)
-    ts(v("tq", 128 * PARTS[-1][0] + 15, 128 * PARTS[-1][0] + 16), col(10), -34.0, Op.mult, col(14), Op.add)
-    ts(v("r16"), v("i16"), MF_, Op.is_equal)
-    ts(v("cs"), v("i8"), PB, Op.is_equal)
-    ts(v("miw"), v("i16"), MF_, Op.is_equal)
-    ts(v("wc128"), v("n15", 0, 128), 15.0, Op.is_equal)
-    tt(v("mw15"), v("mw"), v("wc128"), Op.mult)
-    cp(v("bof"), v("bo"))
+    ts(v("tq", 128 * PARTS[-1][0] + 15, 128 * PARTS[-1][0] + 16), row(2), -34.0, Op.mult, row(6), Op.add)
+    ts(v("miw"), v("i32", 0, 16), MF_, Op.is_equal)
     ts(v("tr"), v("i32k"), MF_, Op.add, float(R), Op.add)
-    ts(v("vhi"), v("vhi"), C14, Op.mult)
-    ts(v("vlo"), v("vlo"), C15, Op.mult)
-    tt(v("vst0"), v("vhi"), v("vlo"), Op.add)
-    for t in range(1, RO):
-        ts(col(56 + t), C14, 2.0 * t, Op.mult)
-        ts(v("vst%d" % t), v("vst0"), col(56 + t), Op.add)
+    mm(v("p1"), v("d14"), v("vhi"), True, False)
+    mm(v("p1"), v("d15"), v("vlo"), False, True)
+    for t in range(RO):
+        ts(col(24 + t), C14, 2.0 * t, Op.mult)
+        act(v("vst%d" % t), v("p1"), Fn.Identity, bias=col(24 + t))
 
-    X = v("hh", 0, R)
+    X = v("hh", 0, R0)
     for i, q in enumerate(HOME):
         a, b = 64 * i, min(P0, 64 * i + 64)
         copy(q, v("xg", 16 * a, 16 * b), ind(X, v("post16", a, b)))
     for c in range(4):
         a, b = 128 * c, min(P0, 128 * c + 128)
         for m in range(16):
-            mm(v("p%d" % (2 + c), a, b), fam("hm", m), v("xg", 16 * a + m, 16 * b, 16), m == 0, m == 15)
-        tt(v("live", a, b), v("slot", a, b), v("p%d" % (2 + c), a, b), Op.is_equal)
+            mm(v("p%d" % (4 + c % 3), a, b), fam("hm", m), v("xg", 16 * a + m, 16 * b, 16), m == 0, m == 15)
+        tt(v("live", a, b), v("slot", a, b), v("p%d" % (4 + c % 3), a, b), Op.is_equal)
 
     def count_full(n):
         mm(v("p0", 0, n), v("bo"), v("live", 0, n), True, True)
@@ -534,13 +540,13 @@ def rank_program(g, core, T, topo):
         p0 = lambda a=0, b=512: v("p0", a, b)
         p1 = lambda a=0, b=512: v("p1", a, b)
 
-        stage[0] = "list"
+        stage[:] = ["list", t]
         scan(v("scan", ne, TS), v("full", ne, TS), v("sd1", ne, TS), v("scan", ne - 1, ne), Op.add, Op.max)
         for h in range(2):
             ts(v("cm%d" % h, 1, 1 + TS - ne), v("scan", ne, TS), HB[h], Op.is_le, 2.0, Op.mult)
             red(v("acc", h, h + 1), v("cm%d" % h, 0, 1 + TS - ne), Op.add)
         ts(v(pls), v("acc"), 0.5, Op.mult, ne / 2 + TS * r, Op.add)
-        send([v(pls)] * 3, [v(plr, 2 * place(q), 2 * place(q) + 2) for q in others], [v(plr)], "rp%d" % t)
+        send([v(pls)] * len(others), [v(plr, 2 * place(q), 2 * place(q) + 2) for q in others], [v(plr)], "rp%d" % t)
         ts(pl16, v("acc"), 0.5, Op.mult, ne / 2, Op.add)
         scat(v(tab), v(pls), v("dat", 32 * r, 32 * r + 32))
         stage[0] = "rows"
@@ -565,14 +571,12 @@ def rank_program(g, core, T, topo):
                 a, b = third * i, min(own, third * i + third)
                 if a < b:
                     cp(v("xd", a, b), v("hh", a, b))
-        for a in range(0, own, 1024):
-            b = min(own, a + 1024)
+        for a in range(0, own, 512):
+            b = min(own, a + 512)
             tt(v(xb, a, b), ind(Xa, v("ab16", 384 * t + a // 16, 384 * t + b // 16)), v("xd", a, b), Op.max)
         for i, a in enumerate(range(own, R0, 512)):
             act(v("md", a - own, a - own + 512), ind(Xa, v("ab16", 384 * t + a // 16, 384 * t + a // 16 + 32)))
-            pb = v("p%d" % (6 + i % 2))
-            mm(pb, v("ident"), v(xa, a, a + 512), True, True)
-            tt(v(xb, a, a + 512), v("md", a - own, a - own + 512), pb, Op.max)
+            tt(v(xb, a, a + 512), v("md", a - own, a - own + 512), v(xa, a, a + 512), Op.max)
         if not last and HELP[t + 1] < 12:
             dma("y", v("xd", 0, R0 - 512 * HELP[t + 1]), v(xb, 0, R0 - 512 * HELP[t + 1]), 16e5)
         stage[0] = "tab"
@@ -581,9 +585,10 @@ def rank_program(g, core, T, topo):
                 scat(v(tab), v(plr, c0, c1), v("dat", d0, d1))
         chunks = [(c, 128 * c, min(nq, 128 * c + 128)) for c in range(4)]
         parts = [(h, chunks[a][1], chunks[b - 1][2], chunks[a:b]) for h, (a, b) in enumerate(PARTS)]
-        for c, a, b in chunks:
-            stage[0] = "near%d" % c
-            copy(NEAR[t][c], v("ng", 16 * a, 16 * b), ind(v(tab), v("near16", a, b)))
+        for i, q in enumerate(NEAR[t]):
+            a, b = 64 * i, min(nq, 64 * i + 64)
+            stage[0] = "near%d" % i
+            copy(q, v("ng", 16 * a, 16 * b), ind(v(tab), v("near16", a, b)))
         stage[0] = "split"
         XS = v("xs")
         cp(XS, ind(Xb, v("ps16")))
@@ -606,7 +611,7 @@ def rank_program(g, core, T, topo):
 
         for i, q in enumerate(SLOT[t]):
             a, b = 64 * i, min(nq, 64 * i + 64)
-            stage[0] = "slot%d" % (i // 2)
+            stage[0] = "slot%d" % i
             copy(q, v("xg", 16 * a, 16 * b), ind(Xb, v("post16", a, b)))
 
         for h, qa, qb, cs in parts:
@@ -614,7 +619,7 @@ def rank_program(g, core, T, topo):
             for c, a, b in cs:
                 mm(p1(a - qa, b - qa), v("nsp"), v(tab, TS * r + a, TS * r + b), True, False)
                 for j in range(16):
-                    mm(p1(a - qa, b - qa), fam("nm", j), v("ng", 16 * a + j, 16 * b, 16), False, j == 15)
+                    mm(p1(a - qa, b - qa), blk("nm", j), v("ng", 16 * a + j, 16 * b, 16), False, j == 15)
             act(v("ff", qa, qb), p1(0, qb - qa), Fn.Relu)
             nl = (qb - qa) // 16
             for k in range(16):
@@ -623,28 +628,29 @@ def rank_program(g, core, T, topo):
                 mm(p1(32 + 8 * i, 40 + 8 * i), v("ff", a, a + 128), v("g8"), True, True)
             ts(v("tgl", qa // 16, qa // 16 + nl), p1(0, nl), -1.0, Op.mult, 128.0, Op.add)
             cp(v("wt", qa, qa + 128 * len(cs), 16), p1(32, 32 + 8 * len(cs)))
+            stage[0] = "bt%d" % h
             act(v("bt", qa, qb), ind(v(bw, 0, 144), v("tgl", qa // 16, qa // 16 + nl)))
 
         stage[0] = "go"
         tt(v("mb"), ind(bs, v("kx16")), XS, Op.max)
-        mm(p1(0, 32), v("ck", 0, 128), v("ones", 0, 32), True, False)
-        mm(p1(0, 32), v("ibig"), v("lp"), False, False)
+        mm(p0(0, 32), v("ck", 0, 128), v("ones", 0, 32), True, False)
+        mm(p0(0, 32), v("ibig"), v("lp"), False, False)
         for m in range(16):
-            mm(p1(0, 32), fam("rmp", m), v("ma", m, 512, 16), False, False)
+            mm(p0(0, 32), fam("rmp", m), v("ma", m, 512, 16), False, False)
         for m in range(32):
-            mm(p1(0, 32), fam("rx", m // 2), v("mb", m // 2, 512, 16), False, False)
-        mm(p1(0, 32), v("bo14p"), bs, False, False)
-        mm(p1(0, 32), v("bo14n"), v("ac"), False, True)
-        ts(v("go"), p1(0, 32), 15.5, Op.is_ge)
-        ts(v("nog"), p1(0, 32), 15.5, Op.is_lt)
-        mm(p1(0, 32), v("px"), v("nog"), True, True)
+            mm(p0(0, 32), fam("rx", m // 2), v("mb", m // 2, 512, 16), False, False)
+        mm(p0(0, 32), v("bo14p"), bs, False, False)
+        mm(p0(0, 32), v("bo14n"), v("ac"), False, True)
+        ts(v("go"), p0(0, 32), 15.5, Op.is_ge)
+        ts(v("nog"), p0(0, 32), 15.5, Op.is_lt)
+        mm(p0(0, 32), v("px"), v("nog"), True, True)
         if not last:
-            mm(p1(32, 64), v("bo"), v("go"), True, True)
-            ts(v("thr"), p1(32, 64), -301.0, Op.mult, 13 * 301 - 0.5, Op.add)
+            mm(p0(32, 64), v("bo"), v("go"), True, True)
+            ts(v("thr"), p0(32, 64), -301.0, Op.mult, 13 * 301 - 0.5, Op.add)
             tt(v("lval", 128, 160), v("lp"), v("go"), Op.subtract)
-        ts(v("rw"), p1(0, 32), 0.0, Op.max)
-        mm(p1(0, 32), v("mw15"), v("rw"), True, True)
-        tt(v("hw"), v("vst%d" % t, 0, 512, 16), p1(0, 32), Op.add)
+        ts(v("rw"), p0(0, 32), 0.0, Op.max)
+        mm(p0(0, 32), fam("em", 15), v("rw"), True, True)
+        tt(v("hw"), v("vst%d" % t, 0, 512, 16), p0(0, 32), Op.add)
         stage[0] = "homes"
         tt(v("spa"), v("postp"), v("tr"), Op.subtract)
         tt(v("spb"), v("spa"), v("go"), Op.mult)
@@ -669,7 +675,14 @@ def rank_program(g, core, T, topo):
                 su = SU[t][h][d]
                 stage[0] = "dist%d%d" % (h, d)
                 if su:
-                    mm(v(ph, 256 * d, 256 * d + w), v("ident"), v(other, qa, qb), True, True)
+                    tb = "tb%d" % d
+                    for c, a, b in cs:
+                        turn(v("p7", a - qa, a - qa + 128, 1, b - a), v(other, a, b), v("ident"))
+                    for c, a, b in (cs if qb % 128 else [(0, qa, qa + 128)]):
+                        e = 128 if qb % 128 else wg
+                        copy(TURN[d], v(tb, a, a + e, 1, b - a), v("p7", a - qa, a - qa + e, 1, b - a))
+                    for c, a, b in cs:
+                        turn(v(ph, 256 * d + a - qa, 256 * d + b - qa), v(tb, a, a + 128, 1, b - a), v("ident", 0, b - a, 1, b - a))
                 for c, a, b in cs:
                     mm(v(pg_, a - qa, a - qa + 128, 1, b - a), v(other, a, b), v(signs(su)[1 - d]), False, False)
                 o = 16 * qa
@@ -678,7 +691,7 @@ def rank_program(g, core, T, topo):
                     if m0 < su:
                         tt(v(dst, o + m0 * w, o + m1 * w), v("xg", o + m0, 16 * qb, 16), v(ph, 256 * d, 256 * d + w), Op.max)
                     else:
-                        pb = "p%d" % (6 + flip[0] % 2)
+                        pb = ("p6", "p1")[flip[0] % 2]
                         flip[0] += 1
                         for m in range(m0, m1):
                             e = m - m0
@@ -699,18 +712,18 @@ def rank_program(g, core, T, topo):
             ts(v(kma, 0, wg // 16), v(kmi, 0, wg // 16), 15, Op.bitwise_and)
             cp(v("wt", qa + 1, qa + wg, 16), v(kma, 0, wg // 16))
             for c, a, b in cs:
-                mm(v(ph, a - qa, b - qa), v("wt", a, a + 128), v("ident", 0, b - a), True, True)
+                turn(v(ph, a - qa, b - qa), v("wt", a, a + 128, 1, b - a), v("ident", 0, b - a, 1, b - a))
             if not end:
-                act(v("tq", qa, qb), v(ph, 0, w))
-                keys, banks = v("tq", qa, qb), [pg_, ph]
+                cp(v("tq", qa, qb), v(ph, 0, w))
+                keys, banks = v("tq", qa, qb), [pg_, "p6"]
             else:
                 cp(v("tq", qa + 16, qb + 16), v(ph, 0, w))
-                keys, banks = v("tq", qa + 15, qb + 16), [pg_, "p6", "p7", ph]
+                keys, banks = v("tq", qa + 15, qb + 16), [pg_, "p1", "p%d" % (5 - h % 2), "p6"]
             per = min(512 // keys[2], 8 // len(banks))
             for k in range(0, 8, per):
                 pb = banks[k // per % len(banks)]
                 for e in range(per):
-                    mm(v(pb, keys[2] * e, keys[2] * (e + 1)), fam("lg", k + e), keys, True, True)
+                    mm(v(pb, keys[2] * e, keys[2] * (e + 1)), blk("lg", k + e), keys, True, True)
                 for e in range(per):
                     red(v("ms%d" % h, k + e, k + e + 1), v(pb, keys[2] * e, keys[2] * (e + 1)), Op.min, True)
             if 0 < h and not end:
@@ -738,6 +751,7 @@ def rank_program(g, core, T, topo):
             tt(v("lval", 0, 128), v("lgt"), v("oh"), Op.subtract)
             scat(v("live"), v(lst), v("lval"))
             count_full(nq)
+        stage[0] = "copy"
         act(v("pg"), ind(v("postf"), lq16))
         tt(v("pgm"), v("pg"), v("oh"), Op.mult)
         mm(p1(0, 32), v("bof"), v("pgm", 32 * r, 32 * r + 32), True, True)
@@ -765,6 +779,7 @@ def rank_program(g, core, T, topo):
             tt(v("wfb"), v(arr, 64, 96), v(mf, 32 * r, 32 * r + 32), Op.max)
             tt(v("wfm"), v("wfa"), v("wfb"), Op.max)
             tt(v("full", nq, nq + 32), v("wfm"), v("thr"), Op.is_ge)
+        stage[0] = "win"
         ts(v("fb"), v(arr), 0.0, Op.is_lt, 8192.0, Op.mult)
         tt(v("fa"), v("fb"), v("atab%d" % t), Op.add)
         tt(v("wc"), v("fa", 0, 32), v("ownv"), Op.min)

@@ -9,20 +9,19 @@ WP = 672
 XW = 16 * WP
 TS = 544
 BIG = 262144.0
-HOME = "ssvvsvs"
-SLOT = ["vvvvsss", "vvsvsvs", "vvvvsssv"]
-NEAR = ["ssssvss", "sssssss", "ssssssss"]
-HELP = [8, 3, 7]
-PARTS = [(0, 2), (2, 4)]
-TURN = "vv"
-SU = [[(14, 16), (14, 16)], [(14, 12), (16, 16)], [(16, 16), (16, 12)]]
-CYCLE, GATHER, SCATTER, WAKE, HOP = 0.00087, 1.56, 3.8, 0.15, 4.2
+HOME = "vvsvsvs"
+SLOT = ["sssvsss", "vsvvsss", "vvvvssvs"]
+NEAR = ["svvsvss", "ssvvsss", "sssssvss"]
+HELP = [8, 9, 8]
+FIRST = ("slot4 slot2 near0 const slot0 bt1 split home near6 near3 dist01 go rows offer1 slot6 near1 slot1 slot3 absorb list "
+         "bt0 dist00 copy near7 win dist11 moves first0 dist10 offer0 slot7 homes slot5 late book near2 first1 near4 tab near5").split()
+LATER = ("copy dist00 win rows slot4 list offer1 split dist10 near0 bt0 near2 near1 near7 tab const near3 slot7 near4 first1 "
+         "offer0 slot0 dist01 slot3 near5 slot5 first0 go dist11 homes home late slot1 book slot2 near6 bt1 slot6 moves absorb").split()
+URGENT = ("moves", "list", "split")
+CYCLE, GATHER, SCATTER, WAKE, LOOK = 0.00087, 1.85, 3.7, 0.18, 0.2
 FIXED = {"v": 0.0, "s": 0.15, "p": 0.0, "g": 0.15}
-START, RATE, PASSES = 1.8, 3.5e5, 2
-AT = {'rows': 0, 'tab': 0, 'bt0': 3.2, 'split': 6.6, 'bt1': 8.2, 'slot5': 12.6, 'slot7': 19.4, 'list': 20.8, 'near3': 26.5, 'near2': 32.6, 'offer1': 38.1, 'slot0': 41.1, 'absorb': 46.0, 'near6': 50.4, 'first1': 50.8, 'slot3': 53.5, 'near5': 54.4, 'near1': 55.7, 'near7': 56.0, 'dist01': 56.8, 'go': 61.7, 'copy': 62.5, 'dist00': 71.9, 'offer0': 73.4, 'first0': 80.2, 'slot6': 81.5, 'slot2': 81.9, 'slot1': 83.8, 'homes': 89.5, 'near0': 102.7, 'dist10': 108.3, 'moves': 108.5, 'near4': 121.2, 'book': 130.4, 'slot4': 133.1, 'dist11': 157.2, 'win': 173.9}
-URGENT = ['moves', 'list', 'split', 'bt0', 'slot3', 'near1', 'near7', 'offer1', 'bt1', 'slot1', 'dist10', 'near5', 'near3', 'copy', 'slot5', 'near2', 'near4']
-LOOK = 0.2
-HOOK = []
+START, RATE, ISSUE = 1.8, 3e5, 0.6
+HOP = {"rp": 5.7, "rb": 4.7, "rm": 4.2}
 
 SCRATCH = {}
 ALIAS = {}
@@ -68,18 +67,16 @@ for _t in range(RO):
     _b("vst%d" % _t, 512)
 _b("full scan sd1 junk0 junk1", TS)
 _b("cm0 cm1", 130, F)
-_b("ident nid ibig d14 d15 bo bo14p bo14n bo32 px lga ni dcp cg n15 ck w128 wa128 wb128 wc128 bou nsp vm oh lgt dat", 128)
-_b(" ".join("su%dp su%dn su%da" % (i, i, i) for i in sorted({x for a in SU for b in a for x in b} - {0, 16})), 128)
+_b("ident ibig d14 d15 bo bo14p bo14n px lga ni dcp cg n15 ck w128 wa128 wb128 wc128 bou nsp vm oh lgt dat", 128)
 _b("lval", 160)
 _b("bof zx pg pgm", 128, F)
 _b("lg", 1024)
 _b("ones n15r cka ckb rst", 256)
 _b("kt0 kt1", 256, F)
-_b("wt ff xs ma mb vhi vlo bt tb0 tb1", 512)
-_b("tq", 512)
+_b("kmi0 kmi1 kma0 kma1", 16, I)
+_b("wt ff xs ma mb vhi vlo bt tb0 tb1 tq", 512)
 _b("fc", 32, F)
 _b("cidx i32k i32 tr whi postp nearp ktk kts spa spb spc ownv ra wv wb wc wd we hd thr", 32, F)
-_b("kmi0 kmi1 kma0 kma1", 16, I)
 _b("sd2 sd3 lp oa obt ob go nog rw rwf wf wfa wfb wfm ac hw", 32)
 _b("g8 rgp rgn kd", 8)
 _b("miw", 16)
@@ -87,7 +84,7 @@ _b("pcol", 2, I)
 _b("r16 wk wl", 16, F)
 _b("k5", 5, F)
 _b("h4", 4, F)
-_b("i8 cs ms0 ms1 ms2 ms3 mt1 mt2", 8, F)
+_b("i8 cs ms0 ms1", 8, F)
 _b("acc", 2, F)
 _b("lac lbc", 2, U)
 _b("ps16 spl16 tgl kx16", 32, U)
@@ -98,16 +95,45 @@ _b("ya1 ya2 ya3", 288)
 for _i in range(8):
     _b("p%d" % _i, *((1024, "bfloat16") if _i in (2, 3, 7) else (512, F)), "psum")
 
-NDMA = 28
+NDMA = 20
 SEMAPHORES = ["qv", "qs", "qp", "qg", "sent"] + ["d%d" % i for i in range(NDMA)] + \
     ["%s%d" % (a, t) for a in ("rp", "rb", "rm") for t in range(RO)]
 
 
-def arrange(ops, before, behind, lay, at):
+def edges(ops):
+    before = [[(d, ops[d]["lag"] if o["q"] in "dr" else WAKE if w else 0.0) for d, w in o["dep"].items()] for o in ops]
+    behind = [[] for _ in ops]
+    for i, b in enumerate(before):
+        for d, gap in b:
+            behind[d].append((i, gap))
+    return before, behind
+
+
+def lay(ops, turn, follows):
+    end = [0.0] * len(ops)
+    busy = {q: [] for q in "vspgydr"}
+    for i in turn:
+        at = max([end[d] + gap for d, gap in follows[i]] + [0.0])
+        time, b = ops[i]["time"], busy[ops[i]["q"]]
+        lo, hi = 0, len(b)
+        while lo < hi:
+            mid = (lo + hi) // 2
+            lo, hi = (mid + 1, hi) if b[mid][1] <= at else (lo, mid)
+        while lo < len(b) and b[lo][0] < at + time:
+            at = max(at, b[lo][1])
+            lo += 1
+        b.insert(lo, (at, at + time))
+        end[i] = at + time
+    return end
+
+
+def arrange(ops):
     n = len(ops)
-    key = [100 * o["at"][1] + at.get(o["at"][0], 999) for o in ops]
+    before, behind = edges(ops)
+    key = [0] * n
     for i in range(n - 1, -1, -1):
-        key[i] = min([key[i]] + [key[j] for j, gap in behind[i]])
+        step, t = ops[i]["at"]
+        key[i] = 100 * t + (LATER if t else FIRST).index(step) if step else min([999] + [key[j] for j, gap in behind[i]])
     left = [len(b) for b in before]
     ready = [0.0] * n
     free = {q: 0.0 for q in "vspgydr"}
@@ -125,19 +151,17 @@ def arrange(ops, before, behind, lay, at):
             left[j] -= 1
             if not left[j]:
                 cand[ops[j]["q"]].append(j)
-    best = (max(free.values()), turn)
-    if PASSES == 0:
-        return best
-    for k in range(PASSES):
-        if k:
-            turn = [turn[k] for k in sorted(range(n), key=lambda k: (-end[turn[k]], -k))]
-            end = lay(turn, behind)
-            turn = [turn[k] for k in sorted(range(n), key=lambda k: (-end[turn[k]], -k))]
-        end = lay(turn, before)
-        turn = [turn[k] for k in sorted(range(n), key=lambda k: (end[turn[k]] - ops[turn[k]]["time"], k))]
-        if best is None or max(end) < best[0]:
-            best = (max(end), turn)
-    return best
+
+    def by(value):
+        return [turn[k] for k in sorted(range(n), key=value)]
+
+    end = lay(ops, turn, before)
+    turn = by(lambda k: (end[turn[k]] - ops[turn[k]]["time"], k))
+    turn = by(lambda k: (-end[turn[k]], -k))
+    end = lay(ops, turn, behind)
+    turn = by(lambda k: (-end[turn[k]], -k))
+    end = lay(ops, turn, before)
+    return by(lambda k: (end[turn[k]] - ops[turn[k]]["time"], k)), max(end)
 
 
 def rank_program(g, core, T, topo):
@@ -148,6 +172,7 @@ def rank_program(g, core, T, topo):
     ops = []
     acc = {}
     dn = [0]
+    small = []
     stage = ["", 0]
 
     def meet(a, b):
@@ -172,62 +197,34 @@ def rank_program(g, core, T, topo):
                             dep[d] = True
                     elif (is_w or w2) and meet(reg[1:], o):
                         dep[d] = True
-        ops.append({"q": q, "fn": fn, "time": time, "lag": lag, "dep": dep, "sem": sem, "at": tuple(stage), "tag": HOOK[0]() if HOOK else None})
-        me += mine
+        ops.append({"q": q, "fn": fn, "time": time, "lag": lag, "dep": dep, "sem": sem, "at": tuple(stage)})
         for reg in writes:
             ps = SCRATCH[reg[0]][0] == "psum"
             old = acc.get(reg[0], [])
             if not adds:
                 old = [o for o in old if not (ps or (reg[3] == 1 and reg[1] <= o[0][0] and o[0][1] <= reg[2]) or reg[1:] == o[0])]
-            acc[reg[0]] = old + [(reg[1:], True, me, adds)]
+            acc[reg[0]] = old + [(reg[1:], True, me + mine, adds)]
         for reg in reads:
-            acc.setdefault(reg[0], []).append((reg[1:], False, me, False))
-        return me - mine
+            acc.setdefault(reg[0], []).append((reg[1:], False, me + mine, False))
+        return me
 
     def run(q, fn, cycles, reads, writes, adds=False):
         note(q, fn, cycles * CYCLE + FIXED[q], 0.0, reads, writes, adds)
 
-    def dma(q, out, in_, nbytes, turn=False):
+    def dma(q, out, in_, nbytes, next_=False):
         sem = "d%d" % dn[0]
         dn[0] += 1
         me = note(q, lambda: Q[q].dma_start(out[0], in_[0]).then_inc(T.sem[sem], 16), 0.1, START, in_[1], out[1], sem=(sem, 0), mine=1)
         note("d", None, nbytes / RATE, 0.0, [], [], after=[me], sem=(sem, 16))
-        if turn:
+        if next_:
             ops[me]["dep"][me - 2] = False
             ops[me + 1]["dep"][me - 1] = False
 
     def emit():
-        n = len(ops)
-        before = [[(d, ops[d]["lag"] if o["q"] in "dr" else WAKE if w else 0.0) for d, w in o["dep"].items()] for o in ops]
-        behind = [[] for _ in ops]
-        for i in range(n):
-            for d, gap in before[i]:
-                behind[d].append((i, gap))
-
-        def lay(turn, edges):
-            end = [0.0] * n
-            busy = {q: [] for q in "vspgydr"}
-            for i in turn:
-                at = max([end[d] + gap for d, gap in edges[i]] + [0.0])
-                time, b = ops[i]["time"], busy[ops[i]["q"]]
-                lo, hi = 0, len(b)
-                while lo < hi:
-                    mid = (lo + hi) // 2
-                    lo, hi = (mid + 1, hi) if b[mid][1] <= at else (lo, mid)
-                while lo < len(b) and b[lo][0] < at + time:
-                    at = max(at, b[lo][1])
-                    lo += 1
-                b.insert(lo, (at, at + time))
-                end[i] = at + time
-            return end
-
-        if len(HOOK) > 2:
-            return HOOK[2](ops, before, behind, lay)
-        order = arrange(ops, before, behind, lay, AT)[1]
         cnt = {}
         known = {q: {} for q in Q}
         tok = {}
-        for i in order:
+        for i in arrange(ops)[0]:
             o = ops[i]
             q = o["q"]
             if q in "dr":
@@ -244,8 +241,6 @@ def rank_program(g, core, T, topo):
             for tk in need.values():
                 for s2, v2 in list(tk[2].items()) + [tk[:2]]:
                     known[q][s2] = max(known[q].get(s2, 0), v2)
-            if HOOK:
-                HOOK[1](o["tag"])
             if o["sem"] is None:
                 sem = "q" + q
                 cnt[sem] = cnt.get(sem, 0) + 1
@@ -279,7 +274,7 @@ def rank_program(g, core, T, topo):
         return v(b, 128 * m, 128 * m + 128)
 
     def cyc(out, a):
-        return max(64, a[2] * (GATHER if a[3] == "ind" else 0.5 if out[3] == a[3] == "two" else 1))
+        return 60 + a[2] * GATHER if a[3] == "ind" else max(64, a[2] * (0.5 if out[3] == a[3] == "two" else 1))
 
     def tt(out, a, b, op):
         psum = any(SCRATCH[x[1][0][0]][0] == "psum" for x in (a, b))
@@ -336,7 +331,7 @@ def rank_program(g, core, T, topo):
         if accum is not None:
             kw["accum_out"] = accum[0]
             w += accum[1]
-        run("s", lambda: g.scalar.activation(out[0], a[0], fn, **kw), a[2] * (GATHER if a[3] == "ind" else 1), regs, w)
+        run("s", lambda: g.scalar.activation(out[0], a[0], fn, **kw), a[2] * GATHER - 100 if a[3] == "ind" else a[2], regs, w)
 
     def copy(q, out, a):
         (cp if q == "v" else act)(out, a)
@@ -351,58 +346,72 @@ def rank_program(g, core, T, topo):
     def iota(out, pat, base=0, cm=0, flag=True):
         kw = {"allow_small_or_imprecise_dtypes": True} if flag else {}
         run("g", lambda: g.iota(out[0], pat, base, cm, **kw), 2 * out[2], [], out[1])
+        if small:
+            ops[-1]["dep"].setdefault(small[-1], False)
+        if stage[0] == "const":
+            small.append(len(ops) - 1)
 
     others = [q for q in range(len(T.cores)) if q != r]
+    NE = 2
 
     def send(bufs, dsts, lands, sem):
-        turns = sorted(range(len(others)), key=lambda i: (others[i] - r) % len(T.cores))
-        mask = topo.mask(core, T.cores[others[0]])
-        ne = len(topo.engines(core, T.cores[others[0]]))
-        calls = [turns] if all(b[0] is bufs[0][0] for b in bufs) else [[i] for i in turns]
-        mine = []
-        for k, call in enumerate(calls):
-            ids = [DstId(rid=topo.addr(T.cores[others[i]])[0], pnc=topo.addr(T.cores[others[i]])[1]) for i in call]
-            one = RemoteDMATransfer(dst_ids=ids, dma_engine_mask=mask, remote_sem=T.sem[sem], srcs=[bufs[call[0]][0]],
-                                    dsts=[dsts[i][0] for i in call])
-            mine.append(note("g", lambda one=one: g.remote_dma_fused([one], local_sem=T.sem["sent"]), 2.6 if sem == "rp0" else 0.6,
-                             HOP - 0.5 * k, bufs[call[0]][1], [], sem=("sent", ne)))
-            if k:
-                ops[mine[k]]["dep"][mine[k - 1]] = False
-        note("r", None, 0.001, 0.0, [], [reg for x in lands for reg in x[1]], after=mine, sem=(sem, ne * len(others)))
+        trs = []
+        for i, q in enumerate(others):
+            rid, pid, _ = topo.addr(T.cores[q])
+            eng = topo.engines(core, T.cores[q])[NE * i:NE * i + NE]
+            trs.append(RemoteDMATransfer(dst_ids=[DstId(rid=rid, pnc=pid)], dma_engine_mask=sum(1 << e for e in eng),
+                                         remote_sem=T.sem[sem], srcs=[bufs[i][0]], dsts=[dsts[i][0]]))
+        n = NE * len(others)
+        me = note("g", lambda: g.remote_dma_fused(trs, local_sem=T.sem["sent"]), ISSUE + (2.0 if sem == "rp0" else 0.0),
+                  HOP[sem[:2]], [reg for b in bufs for reg in b[1]], [], sem=("sent", n))
+        note("r", None, 0.001, 0.0, [], [reg for x in lands for reg in x[1]], after=[me], sem=(sem, n))
 
     def place(q):
         return r - (1 if r > q else 0)
 
     third = R0 // 3
+    stage[0] = "home"
+    fill(v("x2", 0, 1024), 0.0)
+    fill(v("x2", 1024, 4096), 0.0)
+    for a in (4096, 5120):
+        act(v("x2", a, a + 1024), v("x2", 0, 1024))
+    stage[0] = ""
     dma("y", v("postI"), (T.post[:, :], []), 2e5)
+    dma("y", v("nearI"), (T.near[:, :], []), 2e5, True)
+    dma("y", v("abI", 0, 384), (T.absorb[:, 0:384], []), 2e5, True)
+    for i in (14, 15):
+        dma("y", (T["x2"][i:128:16, 0:R0], [("x2", i - 14, R0, 2)]), (T.rec[i:128:16, :], []), 1e5, True)
     for i in range(3):
         dma("y", v("hh", third * i, third * i + third), (T.rec[:, third * i:third * i + third], []), 5e5, True)
-    dma("y", v("abI", 0, 384), (T.absorb[:, 0:384], []), 2e5, True)
-    dma("y", v("nearI"), (T.near[:, :], []), 2e5, True)
     dma("y", v("ctr", 0, P0), (T.cen[:, :], []), 1e5, True)
     dma("y", v("abI", 384, 1152), (T.absorb[:, 384:1152], []), 4e5, True)
 
     pI, p15 = v("pcol", 0, 1), v("pcol", 1, 2)
-    NI = v("ni")
     PF, MF_, PB = col(0), col(1), col(2)
+    stage[0] = "const"
     iota(pI, [[0, 1]], 0, 1, False)
     iota(PF, [[0, 1]], 0, 1)
-    iota(NI, [[1, 128]])
-    iota(v("dcp"), [[1, 128]], 0, -1)
-    iota(v("cg"), [[16, 8], [0, 16]])
-    iota(v("zi"), [[1, 144]], -15)
-    iota(v("i32k"), [[16, 32]])
     iota(v("i32"), [[1, 32]])
-    iota(v("w128"), [[-1, 128]], 128)
-    iota(v("slot"), [[16, P0]])
-    iota(v("whi"), [[128, 4], [0, 8]])
-    iota(v("n15"), [[0, 8], [1, 16]])
-    iota(v("n15r"), [[0, 16], [-1, 16]], 15)
-    iota(v("i8"), [[16, 8]])
     iota(v("k5"), [[-16, 5]], 32)
     iota(v("h4"), [[512, 2], [16, 2]])
+    iota(v("i8"), [[16, 8]])
+    iota(v("zi"), [[1, 144]], -15)
+    iota(v("cg"), [[16, 8], [0, 16]])
+    iota(v("dcp"), [[1, 128]], 0, -1)
+    iota(v("n15"), [[0, 8], [1, 16]])
     iota(v("cidx"), [[1, 32]], PD + 1)
-    iota(v("sd1", 0, PD), [[0, PD]])
+    iota(v("w128"), [[-1, 128]], 128)
+    iota(v("ni"), [[1, 128]])
+    iota(v("whi"), [[128, 4], [0, 8]])
+    iota(v("i32k"), [[16, 32]])
+    iota(v("n15r"), [[0, 16], [-1, 16]], 15)
+    iota(v("slot"), [[16, P0]])
+    for b, a, e in (("hh", R0, R), ("live", P0, WP), ("full", P0, TS), ("wk", 0, 16)):
+        fill(v(b, a, e), 0.0)
+    fill(v("ones"), 1.0)
+    for i, w in ((0, 32768), (1, 1), (2, -256), (3, -16), (4, -32768 * 128), (5, -15), (7, 2 ** 23), (12, 32768), (14, 16)):
+        fill(v("wk", i, i + 1), float(w))
+    stage[0] = ""
     iota(v("postf", MD, WP), [[1, 128]], R)
     iota(v("postf", PD, MD), [[0, 32]])
     iota(v("vhi"), [[1, 2], [0, 256]], 26)
@@ -413,16 +422,14 @@ def rank_program(g, core, T, topo):
         for q in range(4):
             iota(v("tab%d" % k, TS * q, TS * q + TS), [[0, TS]])
     iota(v("vm"), [[0, 128]], 255)
+    iota(v("sd1", 0, PD), [[0, PD]])
     iota(v("wt"), [[0, 512]])
     for k in (4, 5):
         iota(v("wt", k, 512, 16), [[0, 32]], 1)
-    iota(v("ones"), [[0, 256]], 1)
     iota(v("xg", 16 * MD, XW, 16), [[0, 128]], -1)
-    for b, a, e in (("hh", R0, R), ("x1", R0, R), ("x2", R0, R), ("live", P0, WP), ("full", P0, TS), ("ff", P0, 512),
-                    ("nearf", P0, WP), ("ctr", P0, WP)):
+    for b, a, e in (("x1", R0, R), ("x2", R0, R), ("ff", P0, 512), ("nearf", P0, WP), ("ctr", P0, WP)):
         iota(v(b, a, e), [[0, e - a]])
-    for i, w in enumerate((32768, 1, -256, -16, -32768 * 128, -15, 0, 2 ** 23, 0, 0, 0, 0, 32768, 0, 16, 0)):
-        iota(v("wk", i, i + 1), [[0, 1]], w)
+    stage[0] = "const"
     ts(p15, pI, 15, Op.bitwise_and)
     cp(MF_, p15)
     tt(PB, PF, MF_, Op.subtract)
@@ -441,18 +448,17 @@ def rank_program(g, core, T, topo):
     ts(v("fc", 16, 20), v("h4"), MF_, Op.add, 0.5, Op.add)
     HB = (col(16), col(17))
     ts(v("e16"), v("zi"), PB, Op.is_equal)
-    ts(v("e16f"), v("zi"), PB, Op.is_equal)
-    for b, w in (("hm", col(6)), ("em", MF_), ("rx", KN16), ("rmp", K32)):
-        ts(v(b), v("zi"), PB, Op.is_equal, w, Op.mult)
+    ts(v("hm"), v("zi"), PB, Op.is_equal, col(6), Op.mult)
+    for b, w in (("em", MF_), ("rx", KN16), ("rmp", K32), ("e16f", 1.0)):
+        act(v(b), v("e16"), scale=w)
     cp(v("post16", 0, P0), v("postI"))
     cp(v("postf", 0, P0), v("postI"))
     act(v("slot"), v("slot"), Fn.Identity, bias=MF_)
     ts(col(20), row(1), -256.0, Op.mult, row(0), Op.add)
     ts(col(21), row(1), -256.0, Op.mult)
-    for b in ("bo", "bof"):
-        ts(v(b), v("cg"), PB, Op.is_equal)
-    for b, w in (("bo14p", K16c), ("bo14n", KN16), ("bo32", K32), ("nsp", col(21))):
-        ts(v(b), v("cg"), PB, Op.is_equal, w, Op.mult)
+    ts(v("bo"), v("cg"), PB, Op.is_equal)
+    for b, w in (("nsp", col(21)), ("bo14p", K16c), ("bo14n", KN16), ("bof", 1.0)):
+        act(v(b), v("bo"), scale=w)
     for b in ("g8", "cs"):
         ts(v(b), v("i8"), PB, Op.is_equal)
     for b, w in (("rgp", K32), ("rgn", KN32)):
@@ -464,14 +470,18 @@ def rank_program(g, core, T, topo):
     for h in range(2):
         tt(v("wl", 8 * h, 8 * h + 8), v("wk", 8 * h, 8 * h + 8), v("r16", 0, 8), Op.mult)
         red(col(22 + h), v("wl", 8 * h, 8 * h + 8), Op.add)
-    ts(v("lga"), NI, col(23), Op.mult, col(22), Op.add)
+    ts(v("lga"), v("ni"), col(23), Op.mult, col(22), Op.add)
+    stage[0] = "late"
     for k in range(8):
         act(blk("lg", k), v("lga"), scale=v("cs", k, k + 1))
+    stage[0] = "const"
     ts(v("sd2"), v("cidx"), col(18), Op.is_ge, 16.0, Op.mult)
     ts(v("sd3"), v("cidx"), col(19), Op.is_ge, 84.0, Op.mult)
     tt(v("sd1", PD, TS), v("sd2"), v("sd3"), Op.add)
-    for b, w in (("ident", 1.0), ("ibig", BIG), ("nid", -1.0), ("d14", C14), ("d15", C15)):
+    for b, w in (("ident", 1.0), ("ibig", BIG)):
         ts(v(b), v("dcp"), 0.0, Op.is_equal, w, Op.mult)
+    for b, w in (("d14", C14), ("d15", C15)):
+        act(v(b), v("ident"), scale=w)
     ts(v("wa128"), v("dcp"), 0.0, Op.is_gt, -32.0, Op.mult)
     tt(v("wb128"), v("wa128"), v("bo"), Op.mult)
     tt(v("px"), v("wb128"), v("ident"), Op.add)
@@ -485,33 +495,25 @@ def rank_program(g, core, T, topo):
     ts(v("nsh"), v("nearI"), 4, Op.arith_shift_right, 96, Op.bitwise_and)
     tt(v("nearf", 0, P0), v("nsh"), v("nearI"), Op.add)
     cp(v("near16", 0, P0), v("nearf", 0, P0))
-    for t in range(RO):
-        cp(v("ab16", 384 * t, 384 * t + 384), v("abI", 384 * t, 384 * t + 384))
-    made = {16: ("bo14p", "bo14n"), 0: ("bo14n", "bo14p")}
-
-    def signs(su):
-        if su not in made:
-            made[su] = ("su%dp" % su, "su%dn" % su)
-            ts(v("su%da" % su), v("n15"), su - 0.5, Op.is_lt, 0.5, Op.subtract)
-            tt(v(made[su][0]), v("su%da" % su), v("bo32"), Op.mult)
-            ts(v(made[su][1]), v(made[su][0]), -1.0, Op.mult)
-        return made[su]
-
     ts(v("wt", 2, 512, 16), v("whi"), PB, Op.add, 1 / 16, Op.mult)
     ts(v("wt", 3, 512, 16), v("whi"), 0.0, Op.mult, MF_, Op.add)
-    ts(v("tq", 128 * PARTS[-1][0] + 15, 128 * PARTS[-1][0] + 16), row(2), -34.0, Op.mult, row(6), Op.add)
+    ts(v("tq", 271, 272), row(2), -34.0, Op.mult, row(6), Op.add)
     ts(v("miw"), v("i32", 0, 16), MF_, Op.is_equal)
     ts(v("tr"), v("i32k"), MF_, Op.add, float(R), Op.add)
+    stage[0] = ""
+    for t in range(RO):
+        cp(v("ab16", 384 * t, 384 * t + 384), v("abI", 384 * t, 384 * t + 384))
+    stage[0] = "late"
     mm(v("p1"), v("d14"), v("vhi"), True, False)
     mm(v("p1"), v("d15"), v("vlo"), False, True)
     for t in range(RO):
         ts(col(24 + t), C14, 2.0 * t, Op.mult)
         act(v("vst%d" % t), v("p1"), Fn.Identity, bias=col(24 + t))
 
-    X = v("hh", 0, R0)
+    stage[0] = "home"
     for i, q in enumerate(HOME):
         a, b = 64 * i, min(P0, 64 * i + 64)
-        copy(q, v("xg", 16 * a, 16 * b), ind(X, v("post16", a, b)))
+        copy(q, v("xg", 16 * a, 16 * b), ind(v("x2", 0, R0), v("post16", a, b)))
     for c in range(4):
         a, b = 128 * c, min(P0, 128 * c + 128)
         for m in range(16):
@@ -525,6 +527,18 @@ def rank_program(g, core, T, topo):
         for h in range(2):
             act(v("junk%d" % h, 0, n), v("scan", 0, n), Fn.Sign, bias=HB[h], scale=-1.0, accum=v("cm%d" % h, 0, 1))
 
+    def p0(a, b):
+        return v("p0", a, b)
+
+    def p1(a, b):
+        return v("p1", a, b)
+
+    def row_list(out, one):
+        mm(p0(0, 2), v("ident"), v("kd", 0, 2), True, False)
+        for j in range(16):
+            mm(p0(0, 2), fam("em", j), v(one, j, 32, 16), False, j == 15)
+        cp(v(out), p0(0, 2))
+
     count_full(P0)
     for t in range(RO):
         nq = P0 + SP * t
@@ -537,8 +551,8 @@ def rank_program(g, core, T, topo):
         tab, plr, pls, lst, bw, mf, arr = [n + str(t) for n in ("tab", "plr", "pls", "lst", "bw", "mf", "arr")]
         pl16, lq16 = v(lst, 8, 10), v(lst, 0, 8)
         bs = v(bw, 32 * r, 32 * r + 32)
-        p0 = lambda a=0, b=512: v("p0", a, b)
-        p1 = lambda a=0, b=512: v("p1", a, b)
+        chunks = [(128 * c, min(nq, 128 * c + 128)) for c in range(4)]
+        halves = [(0, 0, 256, chunks[0:2]), (1, 256, nq, chunks[2:4])]
 
         stage[:] = ["list", t]
         scan(v("scan", ne, TS), v("full", ne, TS), v("sd1", ne, TS), v("scan", ne - 1, ne), Op.add, Op.max)
@@ -555,36 +569,24 @@ def rank_program(g, core, T, topo):
         cp(v("ps16"), v("postp"))
         mm(p0(0, 32), v("px"), v("lp"), True, True)
         ts(v("oa"), p0(0, 32), 0.0, Op.max)
-
-        def row_list(out, one):
-            mm(p0(0, 2), v("ident"), v("kd", 0, 2), True, False)
-            for j in range(16):
-                mm(p0(0, 2), fam("em", j), v(one, j, 32, 16), False, j == 15)
-            cp(v(out), p0(0, 2))
-
         row_list("lac", "oa")
         stage[0] = "absorb"
-        nh = HELP[t]
-        own = R0 - 512 * nh
+        own = R0 - 512 * HELP[t]
         if t == 0:
-            for i in range(3):
-                a, b = third * i, min(own, third * i + third)
-                if a < b:
-                    cp(v("xd", a, b), v("hh", a, b))
-        for a in range(0, own, 512):
-            b = min(own, a + 512)
-            tt(v(xb, a, b), ind(Xa, v("ab16", 384 * t + a // 16, 384 * t + b // 16)), v("xd", a, b), Op.max)
-        for i, a in enumerate(range(own, R0, 512)):
-            act(v("md", a - own, a - own + 512), ind(Xa, v("ab16", 384 * t + a // 16, 384 * t + a // 16 + 32)))
-            tt(v(xb, a, a + 512), v("md", a - own, a - own + 512), v(xa, a, a + 512), Op.max)
-        if not last and HELP[t + 1] < 12:
-            dma("y", v("xd", 0, R0 - 512 * HELP[t + 1]), v(xb, 0, R0 - 512 * HELP[t + 1]), 16e5)
+            act(v("xd", 0, own), v("hh", 0, own))
+        for a in range(0, R0, 512):
+            which = ind(Xa, v("ab16", 384 * t + a // 16, 384 * t + a // 16 + 32))
+            if a < own:
+                tt(v(xb, a, a + 512), which, v("xd", a, a + 512), Op.max)
+            else:
+                act(v(xb, a, a + 512), which)
+                tt(v(xb, a, a + 512), v(xb, a, a + 512), v(xa, a, a + 512), Op.max)
+        if not last:
+            dma("y", v("xd", 0, R0 - 512 * HELP[t + 1]), v(xb, 0, R0 - 512 * HELP[t + 1]), 131072 * (12 - HELP[t + 1]))
         stage[0] = "tab"
         for (c0, c1, d0, d1) in ((0, 2 * r, 0, 32 * r), (2 * r, 6, 32 * r + 32, 128)):
             if c1 > c0:
                 scat(v(tab), v(plr, c0, c1), v("dat", d0, d1))
-        chunks = [(c, 128 * c, min(nq, 128 * c + 128)) for c in range(4)]
-        parts = [(h, chunks[a][1], chunks[b - 1][2], chunks[a:b]) for h, (a, b) in enumerate(PARTS)]
         for i, q in enumerate(NEAR[t]):
             a, b = 64 * i, min(nq, 64 * i + 64)
             stage[0] = "near%d" % i
@@ -594,7 +596,7 @@ def rank_program(g, core, T, topo):
         cp(XS, ind(Xb, v("ps16")))
         cp(v("ac"), ind(XS, v("lac")))
         tt(v("ma"), ind(v("ac"), v("kx16")), XS, Op.max)
-        mm(p0(0, 32), v("ck", 0, 128), v("ones", 0, 32), True, False)
+        mm(p0(0, 32), v("ck"), v("ones", 0, 32), True, False)
         mm(p0(0, 32), v("ibig"), v("lp"), False, False)
         for m in range(16):
             mm(p0(0, 32), fam("rx", m), v("xs", m, 512, 16), False, False)
@@ -607,16 +609,18 @@ def rank_program(g, core, T, topo):
         tr(v("ob"), v("obt"))
         row_list("lbc", "ob")
         cp(bs, ind(XS, v("lbc")))
-        send([bs] * 3, [bs] * 3, [v(bw, 32 * q, 32 * q + 32) for q in others], "rb%d" % t)
+        send([bs] * len(others), [bs] * len(others), [v(bw, 32 * q, 32 * q + 32) for q in others], "rb%d" % t)
 
         for i, q in enumerate(SLOT[t]):
-            a, b = 64 * i, min(nq, 64 * i + 64)
             stage[0] = "slot%d" % i
-            copy(q, v("xg", 16 * a, 16 * b), ind(Xb, v("post16", a, b)))
+            step = 32 if q == "v" else 64
+            for a in range(64 * i, min(nq, 64 * i + 64), step):
+                b = min(nq, a + step)
+                copy(q, v("xg", 16 * a, 16 * b), ind(Xb, v("post16", a, b)))
 
-        for h, qa, qb, cs in parts:
+        for h, qa, qb, cs in halves:
             stage[0] = "first%d" % h
-            for c, a, b in cs:
+            for a, b in cs:
                 mm(p1(a - qa, b - qa), v("nsp"), v(tab, TS * r + a, TS * r + b), True, False)
                 for j in range(16):
                     mm(p1(a - qa, b - qa), blk("nm", j), v("ng", 16 * a + j, 16 * b, 16), False, j == 15)
@@ -624,16 +628,18 @@ def rank_program(g, core, T, topo):
             nl = (qb - qa) // 16
             for k in range(16):
                 mm(p1(0, nl), fam("e16", k), v("ff", qa + k, qb, 16), k == 0, k == 15)
-            for i, (c, a, b) in enumerate(cs):
+            for i, (a, b) in enumerate(cs):
                 mm(p1(32 + 8 * i, 40 + 8 * i), v("ff", a, a + 128), v("g8"), True, True)
             ts(v("tgl", qa // 16, qa // 16 + nl), p1(0, nl), -1.0, Op.mult, 128.0, Op.add)
-            cp(v("wt", qa, qa + 128 * len(cs), 16), p1(32, 32 + 8 * len(cs)))
+            cp(v("wt", qa, qa + 256, 16), p1(32, 48))
             stage[0] = "bt%d" % h
-            act(v("bt", qa, qb), ind(v(bw, 0, 144), v("tgl", qa // 16, qa // 16 + nl)))
+            act(v("bt", qa, qb), ind(v(bw), v("tgl", qa // 16, qa // 16 + nl)))
 
         stage[0] = "go"
-        tt(v("mb"), ind(bs, v("kx16")), XS, Op.max)
-        mm(p0(0, 32), v("ck", 0, 128), v("ones", 0, 32), True, False)
+        for m in range(16):
+            mm(v("p6", m, 512, 16), v("ident"), bs, True, True)
+        tt(v("mb"), XS, v("p6"), Op.max)
+        mm(p0(0, 32), v("ck"), v("ones", 0, 32), True, False)
         mm(p0(0, 32), v("ibig"), v("lp"), False, False)
         for m in range(16):
             mm(p0(0, 32), fam("rmp", m), v("ma", m, 512, 16), False, False)
@@ -664,75 +670,51 @@ def rank_program(g, core, T, topo):
             cp(v("near16", nq, nq + 32), v("nearp"))
             act(v("nearf", nq, nq + 32), v("nearp"))
 
-        flip = [0]
-        for h, qa, qb, cs in parts:
-            w, wg = qb - qa, 128 * len(cs)
-            ph, pg_ = "p%d" % (2 + h % 2), "p%d" % (4 + h % 2)
-            mm(v(pg_, 0, wg), v("ones", 0, 128), v("cka", 0, wg), True, False)
-            for c, a, b in cs:
+        for h, qa, qb, cs in halves:
+            w = qb - qa
+            ph, pg_ = "p%d" % (2 + h), "p%d" % (4 + h)
+            mm(v(pg_, 0, 256), v("ones", 0, 128), v("cka"), True, False)
+            for a, b in cs:
                 mm(v(pg_, a - qa, a - qa + 128), v("live", a, a + 128), v("ibig"), False, False)
-            for d, (other, dst, sums) in enumerate((("ctr", "mc", "rgp"), ("bt", "md", "rgn"))):
-                su = SU[t][h][d]
+            for d, (other, dst, sums, alone) in enumerate((("ctr", "mc", "rgp", "bo14n"), ("bt", "md", "rgn", "bo14p"))):
                 stage[0] = "dist%d%d" % (h, d)
-                if su:
-                    tb = "tb%d" % d
-                    for c, a, b in cs:
-                        turn(v("p7", a - qa, a - qa + 128, 1, b - a), v(other, a, b), v("ident"))
-                    for c, a, b in (cs if qb % 128 else [(0, qa, qa + 128)]):
-                        e = 128 if qb % 128 else wg
-                        copy(TURN[d], v(tb, a, a + e, 1, b - a), v("p7", a - qa, a - qa + e, 1, b - a))
-                    for c, a, b in cs:
-                        turn(v(ph, 256 * d + a - qa, 256 * d + b - qa), v(tb, a, a + 128, 1, b - a), v("ident", 0, b - a, 1, b - a))
-                for c, a, b in cs:
-                    mm(v(pg_, a - qa, a - qa + 128, 1, b - a), v(other, a, b), v(signs(su)[1 - d]), False, False)
-                o = 16 * qa
-                step = 512 // w
-                for m0, m1 in [(m, m + 1) for m in range(su)] + [(m, min(16, m + step)) for m in range(su, 16, step)]:
-                    if m0 < su:
-                        tt(v(dst, o + m0 * w, o + m1 * w), v("xg", o + m0, 16 * qb, 16), v(ph, 256 * d, 256 * d + w), Op.max)
-                    else:
-                        pb = ("p6", "p1")[flip[0] % 2]
-                        flip[0] += 1
-                        for m in range(m0, m1):
-                            e = m - m0
-                            mm(v(pb, e * w, e * w + w), v("ident"), v("xg", o + m, 16 * qb, 16), True, False)
-                            mm(v(pb, e * w, e * w + w), v("nid"), v(other, qa, qb), False, True)
-                        act(v(dst, o + m0 * w, o + m1 * w), v(pb, 0, (m1 - m0) * w), Fn.Relu)
-                    for k in range(m0, m1):
-                        for c, a, b in cs:
-                            mm(v(pg_, a - qa + k, a - qa + 128, 16, b - a), v(dst, o + k * w + a - qa, o + k * w + b - qa), v(sums), False, False)
-            mm(v(pg_, 0, wg), v("ones", 0, 128), v("ckb", 0, wg), False, True)
+                tb = "tb%d" % d
+                for a, b in cs:
+                    turn(v("p7", a - qa, a - qa + 128, 1, b - a), v(other, a, b), v("ident"))
+                for a, b, e in ([(qa, qa + 128, 256)] if h == 0 else [c + (128,) for c in cs]):
+                    cp(v(tb, a, a + e, 1, b - a), v("p7", a - qa, a - qa + e, 1, b - a))
+                for a, b in cs:
+                    turn(v(ph, 256 * d + a - qa, 256 * d + b - qa), v(tb, a, a + 128, 1, b - a), v("ident", 0, b - a, 1, b - a))
+                for a, b in cs:
+                    mm(v(pg_, a - qa, a - qa + 128, 1, b - a), v(other, a, b), v(alone), False, False)
+                for m in range(16):
+                    o = 16 * qa + m * w
+                    tt(v(dst, o, o + w), v("xg", 16 * qa + m, 16 * qb, 16), v(ph, 256 * d, 256 * d + w), Op.max)
+                    for a, b in cs:
+                        mm(v(pg_, a - qa + m, a - qa + 128, 16, b - a), v(dst, o + a - qa, o + b - qa), v(sums), False, False)
+            mm(v(pg_, 0, 256), v("ones", 0, 128), v("ckb"), False, True)
 
-            kt, kmi, kma = "kt%d" % (h % 2), "kmi%d" % (h % 2), "kma%d" % (h % 2)
-            end = h == len(parts) - 1
+            kt, kmi, kma = "kt%d" % h, "kmi%d" % h, "kma%d" % h
             stage[0] = "offer%d" % h
-            scan(v(kt, 0, wg), v("rst", 0, wg), v(pg_, 0, wg), 0.0, Op.add, Op.max)
-            cp(v(kmi, 0, wg // 16), v(kt, 15, wg, 16))
-            ts(v("wt", qa + 7, qa + wg, 16), v(kt, 15, wg, 16), 15.5, Op.is_lt)
-            ts(v(kma, 0, wg // 16), v(kmi, 0, wg // 16), 15, Op.bitwise_and)
-            cp(v("wt", qa + 1, qa + wg, 16), v(kma, 0, wg // 16))
-            for c, a, b in cs:
+            scan(v(kt), v("rst"), v(pg_, 0, 256), 0.0, Op.add, Op.max)
+            cp(v(kmi), v(kt, 15, 256, 16))
+            ts(v("wt", qa + 7, qa + 256, 16), v(kt, 15, 256, 16), 15.5, Op.is_lt)
+            ts(v(kma), v(kmi), 15, Op.bitwise_and)
+            cp(v("wt", qa + 1, qa + 256, 16), v(kma))
+            for a, b in cs:
                 turn(v(ph, a - qa, b - qa), v("wt", a, a + 128, 1, b - a), v("ident", 0, b - a, 1, b - a))
-            if not end:
-                cp(v("tq", qa, qb), v(ph, 0, w))
-                keys, banks = v("tq", qa, qb), [pg_, "p6"]
-            else:
-                cp(v("tq", qa + 16, qb + 16), v(ph, 0, w))
-                keys, banks = v("tq", qa + 15, qb + 16), [pg_, "p1", "p%d" % (5 - h % 2), "p6"]
-            per = min(512 // keys[2], 8 // len(banks))
-            for k in range(0, 8, per):
-                pb = banks[k // per % len(banks)]
-                for e in range(per):
+            cp(v("tq", qa + 16 * h, qb + 16 * h), v(ph, 0, w))
+            keys = v("tq", qa + 15 * h, qb + 16 * h)
+            for k, pb in zip(range(0, 8, 2), (["p4", "p6", "p4", "p6"], ["p5", "p1", "p4", "p6"])[h]):
+                for e in range(2):
                     mm(v(pb, keys[2] * e, keys[2] * (e + 1)), blk("lg", k + e), keys, True, True)
-                for e in range(per):
+                for e in range(2):
                     red(v("ms%d" % h, k + e, k + e + 1), v(pb, keys[2] * e, keys[2] * (e + 1)), Op.min, True)
-            if 0 < h and not end:
-                tt(v("mt%d" % h), v("ms%d" % h), v("mt%d" % (h - 1) if h > 1 else "ms0"), Op.min)
+                for e in range(k, k + 2 * h):
+                    ts(v("zx", 16 * e, 16 * e + 16), v("r16"), v("ms1", e, e + 1), Op.mult, v("ms0", e, e + 1), Op.min)
         if not last:
             scat(v("ctr"), pl16, v("ac"))
             act(v("ctr", nq, nq + 32), bs)
-        for k in range(8):
-            ts(v("zx", 16 * k, 16 * k + 16), v("r16"), v("ms%d" % h, k, k + 1), Op.mult, v("mt%d" % (h - 1) if h > 1 else "ms0", k, k + 1), Op.min)
         mm(p0(0, 8), v("zx"), v("cs"), True, True)
         cp(v("ls16"), p0(0, 8))
         cp(v(mf), ind(v("xg"), v("ls16")))

@@ -1,3 +1,4 @@
+import numpy as np
 from concourse.bass import DstId, RemoteDMATransfer
 from concourse.mybir import AluOpType as Op, AxisListType as Ax, ActivationFunctionType as Fn
 
@@ -9,22 +10,38 @@ WP = 672
 XW = 16 * WP
 TS = 544
 BIG = 262144.0
-HOME = "vvsvsvs"
-SLOT = ["sssvsss", "vsvvsss", "vvvvssvs"]
-NEAR = ["svvsvss", "ssvvsss", "sssssvss"]
-HELP = [8, 9, 8]
-FIRST = ("slot4 slot2 near0 const slot0 bt1 split home near6 near3 dist01 go rows offer1 slot6 near1 slot1 slot3 absorb list "
-         "bt0 dist00 copy near7 win dist11 moves first0 dist10 offer0 slot7 homes slot5 late book near2 first1 near4 tab near5").split()
-LATER = ("copy dist00 win rows slot4 list offer1 split dist10 near0 bt0 near2 near1 near7 tab const near3 slot7 near4 first1 "
-         "offer0 slot0 dist01 slot3 near5 slot5 first0 go dist11 homes home late slot1 book slot2 near6 bt1 slot6 moves absorb").split()
-URGENT = ("moves", "list", "split")
-CYCLE, GATHER, SCATTER, WAKE, LOOK = 0.00087, 1.85, 3.7, 0.18, 0.2
+MAGIC = 1.5 * 2 ** 27
+HOME = "vsvsssv"
+COMP = "sssvsss"
+SLOT = ["sssvsss", "ssvvvvvv", "sssvsvvv"]
+NEAR = ["svsvsss", "sssssss", "svssssss"]
+HELP = [7, 12]
+EARLY = 6
+FOLD = [0, 0, 3, 0]
+XSQ = "vss"
+MAB = ["vvv", "vss"]
+LOADS = "post rec0 homes rec1 rec2 ab0 near xd0 xd1 xd2 ab ctr"
+TBQ = "vv"
+RELU, BTQ, TQQ = "ssvv", "ssvv", "vvsv"
+FULLQ = "svs"
+MISC = "vvvvv"
+CONST = "ssssvssvvvvvsv"
+PARTS = [[[0, 1], [2, 3]]] * 3
+ORDER = ("moves list rows split tab first0 bt0 first1 bt1 first2 bt2 first3 bt3 dist0 offer0 dist1 offer1 dist2 offer2 "
+         "dist3 offer3 book").split()
+URGENT = ("moves", "list", "split", "rows", "tab", "first0", "first1", "bt0", "bt1", "offer1")
+CYCLE, GATHER, SCATTER = np.array([[0.00095, 1.6, 3.7], [0.0012, 1.15, 4.5], [0.00087, 2.0, 3.0]]).T
+SLOW = dict(zip("pgrd", np.array([[1.0, 1.1, 1.0, 1.15], [1.0, 1.2, 1.25, 1.0], [1.3, 1.1, 0.85, 1.6]]).T))
+WAKE, LOOK = 0.18, 0.3
 FIXED = {"v": 0.0, "s": 0.15, "p": 0.0, "g": 0.15}
 START, RATE, ISSUE = 1.8, 3e5, 0.6
 HOP = {"rp": 5.7, "rb": 4.7, "rm": 4.2}
+FRATE, FLAG = 1.2e5, 8.0
+QUEUES, TRIES, SEED, SLACK = "vspgydfr", 3500, 1, 2e-5
 
 SCRATCH = {}
 ALIAS = {}
+ORDERS = {}
 OWN = ("plr", "pls", "bw", "mf", "arr", "p0", "p1", "p2", "p3", "p4", "p5", "p6", "p7")
 
 
@@ -46,15 +63,15 @@ _b("xd", R0)
 _b("xg", XW)
 _b("ng mc md", 16 * 480)
 _b("nm", 2048)
-_b("e16 rmp rx hm em zi", 144)
-_b("e16f", 144, F)
+_b("e16 rmp rmn rx hm em zi cw1 cw2", 144)
 _b("postI nearI nsh", P0, I)
 _b("abI", 1152, I)
-_b("ab16", 1152, U)
-_b("post16 near16", 512, U)
-_b("postf nearf", WP, F)
-_b("slot", P0, F)
-_b("ctr live", WP)
+_b("ab16", 768, U)
+_b("abh", 1536)
+_b("post16 near16 cmu1 cmu2 w16", 512, U)
+_b("postf nearf cmf1 cmf2", WP, F)
+_b("slot pm h16", P0, F)
+_b("ctr live gone0 gone1", WP)
 for _t in range(RO):
     _b("tab%d" % _t, 4 * TS)
     _b("plr%d" % _t, 6, U)
@@ -66,42 +83,81 @@ for _t in range(RO):
     _b("atab%d" % _t, 96, F)
     _b("vst%d" % _t, 512)
 _b("full scan sd1 junk0 junk1", TS)
+_b("cnt", 480)
 _b("cm0 cm1", 130, F)
-_b("ident ibig d14 d15 bo bo14p bo14n px lga ni dcp cg n15 ck w128 wa128 wb128 wc128 bou nsp vm oh lgt dat", 128)
-_b("lval", 160)
-_b("bof zx pg pgm", 128, F)
+_b("ident ibig d14 d15 bo bo14p bo14n px dcp cg n15 ck w128 wa128 wb128 wc128 bou nsp vm oh lgt dat away lval", 128)
+_b("bo64k nident", 128)
+_b("bof bofn pg pgc pgm identf d384 dneg rlf fa", 128, F)
 _b("lg", 1024)
 _b("ones n15r cka ckb rst", 256)
-_b("kt0 kt1", 256, F)
-_b("kmi0 kmi1 kma0 kma1", 16, I)
-_b("wt ff xs ma mb vhi vlo bt tb0 tb1 tq", 512)
-_b("fc", 32, F)
-_b("cidx i32k i32 tr whi postp nearp ktk kts spa spb spc ownv ra wv wb wc wd we hd thr", 32, F)
-_b("sd2 sd3 lp oa obt ob go nog rw rwf wf wfa wfb wfm ac hw", 32)
+_b("kt", 512, F)
+_b("wt ff xs ma mb vhi vlo bt tb0 tb1 tq0", 512)
+_b("tq1", 528)
+_b("fc kn", 32, F)
+_b("cidx i32k i32 tr whi postp nearp ktk kts spa spb spc wv wd we rwt cp1 cp2 ce1 ce2 cd cs1 cu", 32, F)
+_b("wc", 64, F)
+_b("sd2 sd3 lp oa obt ob go nog rw rwf ac hw stay own", 32)
 _b("g8 rgp rgn kd", 8)
-_b("miw", 16)
 _b("pcol", 2, I)
 _b("r16 wk wl", 16, F)
 _b("k5", 5, F)
 _b("h4", 4, F)
-_b("i8 cs ms0 ms1", 8, F)
+_b("i8 ms lsf lqf lmf", 8, F)
 _b("acc", 2, F)
-_b("lac lbc", 2, U)
-_b("ps16 spl16 tgl kx16", 32, U)
+_b("lac lbc lrc", 2, U)
+_b("ps16 cps16 spl16 tgl", 32, U)
 _b("ls16 lm16 rl16", 8, U)
-_b("lsi lqi lmi", 8, I)
-_b("fa fb eq eh", 96, F)
+_b("eq eh hd", 96)
 _b("ya1 ya2 ya3", 288)
 for _i in range(8):
     _b("p%d" % _i, *((1024, "bfloat16") if _i in (2, 3, 7) else (512, F)), "psum")
 
-NDMA = 20
-SEMAPHORES = ["qv", "qs", "qp", "qg", "sent"] + ["d%d" % i for i in range(NDMA)] + \
+
+def runs(places, most):
+    out = []
+    for i in places:
+        if out and out[-1][-1] == i - 1 and len(out[-1]) < most:
+            out[-1].append(i)
+        else:
+            out.append([i])
+    return out
+
+
+def folds():
+    out = []
+    for t in range(RO):
+        if t and FOLD[2 * t - 1]:
+            ne = P0 + SP * (t - 1)
+            out += [("xg", 1024 * x[0], min(16 * ne, 1024 * x[-1] + 1024))
+                    for x in runs([i for i in range(7) if SLOT[t][i] == "s"], FOLD[2 * t - 1])]
+        if t < 2 and FOLD[2 * t]:
+            out += [("x%d" % (t + 1), 512 * x[0], 512 * x[-1] + 512) for x in runs(range(12 - HELP[t], EARLY if t else 12), FOLD[2 * t])]
+    return out
+
+
+NDMA = 28
+SEMAPHORES = ["qv", "qs", "qp", "qg", "sent"] + ["f%d" % i for i in range(30)] + ["d%d" % i for i in range(NDMA)] + \
     ["%s%d" % (a, t) for a in ("rp", "rb", "rm") for t in range(RO)]
 
 
-def edges(ops):
-    before = [[(d, ops[d]["lag"] if o["q"] in "dr" else WAKE if w else 0.0) for d, w in o["dep"].items()] for o in ops]
+def helper(core, T, topo):
+    return [c for c in topo.cores_of(core) if c != core and topo.die(c) == topo.die(core) and T.rank_of(c) is None][-1]
+
+
+def hand_back(g, core, T, topo):
+    for to in T.cores:
+        if helper(to, T, topo) == core and folds():
+            rid, pid, _ = topo.addr(to)
+            n = len(topo.engines(core, to))
+            for i, (b, c0, c1) in enumerate(folds()):
+                g.wait_ge(T.sem["f%d" % i], n // 2)
+                g.remote_dma(T[b][:, c0:c1], T[b][:, c0:c1], T.sem["f%d" % i], T.sem["sent"], pid, rid, topo.mask(core, to))
+            g.wait_ge(T.sem["sent"], n * len(folds()))
+
+
+def edges(ops, far=1.0):
+    before = [[(d, ops[d]["lag"] * (far if o["q"] == "r" else 1.0) if o["q"] in "dfr" and w else WAKE if w else 0.0)
+               for d, w in o["dep"].items()] for o in ops]
     behind = [[] for _ in ops]
     for i, b in enumerate(before):
         for d, gap in b:
@@ -109,35 +165,56 @@ def edges(ops):
     return before, behind
 
 
-def lay(ops, turn, follows):
-    end = [0.0] * len(ops)
-    busy = {q: [] for q in "vspgydr"}
-    for i in turn:
-        at = max([end[d] + gap for d, gap in follows[i]] + [0.0])
-        time, b = ops[i]["time"], busy[ops[i]["q"]]
-        lo, hi = 0, len(b)
-        while lo < hi:
-            mid = (lo + hi) // 2
-            lo, hi = (mid + 1, hi) if b[mid][1] <= at else (lo, mid)
-        while lo < len(b) and b[lo][0] < at + time:
-            at = max(at, b[lo][1])
+def lay(time, queue, turn, follows, end=None, fixed=0):
+    end = list(end) if end else [0.0] * len(time)
+    busy = {q: ([], []) for q in QUEUES}
+    for i in turn[:fixed]:
+        busy[queue[i]][0].append(end[i] - time[i])
+        busy[queue[i]][1].append(end[i])
+    for i in turn[fixed:]:
+        at = 0.0
+        for d, gap in follows[i]:
+            if end[d] + gap > at:
+                at = end[d] + gap
+        s, e = busy[queue[i]]
+        lo = len(e)
+        while lo and e[lo - 1] > at:
+            lo -= 1
+        while lo < len(s) and s[lo] < at + time[i]:
+            at = max(at, e[lo])
             lo += 1
-        b.insert(lo, (at, at + time))
-        end[i] = at + time
+        s.insert(lo, at)
+        e.insert(lo, at + time[i])
+        end[i] = at + time[i]
     return end
+
+
+def play(time, queue, turn, follows):
+    end, why, prev = [0.0] * len(time), [-1] * len(time), [-1] * len(time)
+    last = dict.fromkeys(QUEUES, -1)
+    for i in turn:
+        w = prev[i] = last[queue[i]]
+        at = end[w] if w >= 0 else 0.0
+        for d, gap in follows[i]:
+            if end[d] + gap > at:
+                at, w = end[d] + gap, d
+        end[i], why[i], last[queue[i]] = at + time[i], w, i
+    return end, why, prev
 
 
 def arrange(ops):
     n = len(ops)
     before, behind = edges(ops)
-    key = [0] * n
+    times = np.array([o["time"] * np.ones(len(CYCLE)) for o in ops]).T.tolist()
+    time, queue = times[0], [o["q"] for o in ops]
+    key = [999] * n
     for i in range(n - 1, -1, -1):
         step, t = ops[i]["at"]
-        key[i] = 100 * t + (LATER if t else FIRST).index(step) if step else min([999] + [key[j] for j, gap in behind[i]])
+        key[i] = min([100 * t + (ORDER.index(step) if step in ORDER else 99)] + [key[j] for j, gap in behind[i]])
     left = [len(b) for b in before]
     ready = [0.0] * n
-    free = {q: 0.0 for q in "vspgydr"}
-    cand = {q: [i for i in range(n) if ops[i]["q"] == q and not left[i]] for q in free}
+    free = {q: 0.0 for q in QUEUES}
+    cand = {q: [i for i in range(n) if queue[i] == q and not left[i]] for q in free}
     soon = [LOOK if o["at"][0] in URGENT else 0.0 for o in ops]
     turn = []
     while len(turn) < n:
@@ -145,34 +222,80 @@ def arrange(ops):
         i = min((key[i], i) for i in cand[q] if ready[i] <= t0 + soon[i])[1]
         cand[q].remove(i)
         turn.append(i)
-        free[q] = max(t0, ready[i]) + ops[i]["time"]
+        free[q] = max(t0, ready[i]) + time[i]
         for j, gap in behind[i]:
             ready[j] = max(ready[j], free[q] + gap)
             left[j] -= 1
             if not left[j]:
-                cand[ops[j]["q"]].append(j)
+                cand[queue[j]].append(j)
 
-    def by(value):
-        return [turn[k] for k in sorted(range(n), key=value)]
+    def settle(turn, back, end=None, fixed=0):
+        end = lay(time, queue, turn, before, end, fixed)
+        turn = sorted(turn, key=lambda i: end[i] - time[i])
+        if back:
+            late = lay(time, queue, sorted(turn[::-1], key=lambda i: -end[i]), behind)
+            return settle(sorted(turn, key=lambda i: -late[i]), False)
+        return turn, end
 
-    end = lay(ops, turn, before)
-    turn = by(lambda k: (end[turn[k]] - ops[turn[k]]["time"], k))
-    turn = by(lambda k: (-end[turn[k]], -k))
-    end = lay(ops, turn, behind)
-    turn = by(lambda k: (-end[turn[k]], -k))
-    end = lay(ops, turn, before)
-    return by(lambda k: (end[turn[k]] - ops[turn[k]]["time"], k)), max(end)
+    def value(turn):
+        out = [play(x, queue, turn, b) for x, b in zip(times, befores)]
+        return sum(max(o[0]) / z for o, z in zip(out, scale)), out
+
+    befores = [edges(ops, float(x))[0] for x in SLOW["r"]]
+    turn, end = settle(turn, True)
+    scale = [sum(x[i] for i in range(n) if queue[i] in "vs") for x in times]
+    best, out = value(turn)
+    seed = [SEED]
+
+    def draw(k):
+        seed[0] = (seed[0] * 1103515245 + 12345) % 2 ** 31
+        return (seed[0] >> 8) % k
+
+    for k in range(TRIES):
+        e, why, prev = out[draw(len(out))]
+        chain = [max(range(n), key=lambda i: e[i])]
+        while why[chain[-1]] >= 0:
+            chain.append(why[chain[-1]])
+        a, by = draw(len(chain)), (0.3, 1, 2, 4, 8)[draw(5)]
+        kind = draw(4)
+        some = chain[a:a + (1, 1, 3, 10, 30)[draw(5)]]
+        if kind % 2:
+            some, by = [prev[i] for i in some if prev[i] == why[i] >= 0], -by
+        if kind > 1 and some:
+            some = [i for i in range(n) if ops[i]["at"] == ops[some[0]]["at"] and queue[i] == queue[some[0]]]
+        if not some:
+            continue
+        key = [end[i] - time[i] for i in range(n)]
+        first = min(key[i] for i in some)
+        for i in some:
+            key[i] -= by
+        for i in (turn[::-1] if by > 0 else turn):
+            for j, gap in (before if by > 0 else behind)[i]:
+                if (key[j] - key[i]) * by >= 0:
+                    key[j] = key[i] - 1e-6 * by
+                    first = min(first, end[j] - time[j])
+        first -= max(by, 0) + 0.01
+        fixed = 0
+        while end[turn[fixed]] - time[turn[fixed]] < first:
+            fixed += 1
+        new, en = settle(turn[:fixed] + sorted(turn[fixed:], key=lambda i: key[i]), draw(3) == 0, end, fixed)
+        val, o = value(new)
+        if val <= best + SLACK * draw(100) * (1 - k / TRIES):
+            turn, end, best, out = new, en, val, o
+    return turn, max(end)
 
 
 def rank_program(g, core, T, topo):
     r = T.rank_of(core)
     if r is None:
-        return
+        return hand_back(g, core, T, topo)
     Q = {"v": g.vector, "s": g.scalar, "p": g.tensor, "g": g, "y": g.sync}
     ops = []
     acc = {}
     dn = [0]
-    small = []
+    line = {}
+    put_off = {}
+    mark = [0]
     stage = ["", 0]
 
     def meet(a, b):
@@ -209,13 +332,30 @@ def rank_program(g, core, T, topo):
         return me
 
     def run(q, fn, cycles, reads, writes, adds=False):
-        note(q, fn, cycles * CYCLE + FIXED[q], 0.0, reads, writes, adds)
+        note(q, fn, (cycles * CYCLE + FIXED[q]) * SLOW.get(q, 1.0), 0.0, reads, writes, adds)
+
+    def in_turn(*kind):
+        if kind in line:
+            ops[-1]["dep"].setdefault(line[kind], False)
+        line[kind] = len(ops) - 1
+
+    def together(first):
+        some = ops[first:]
+        del ops[first:]
+        dep = {}
+        for o in some:
+            for d, w in o["dep"].items():
+                if d < first:
+                    dep[d] = dep.get(d, False) or w
+        ops.append(dict(some[0], fn=lambda: [o["fn"]() for o in some], time=sum(o["time"] for o in some), dep=dep))
+        for b in acc:
+            acc[b] = [x if x[2] < first else x[:2] + (first,) + x[3:] for x in acc[b]]
 
     def dma(q, out, in_, nbytes, next_=False):
         sem = "d%d" % dn[0]
         dn[0] += 1
         me = note(q, lambda: Q[q].dma_start(out[0], in_[0]).then_inc(T.sem[sem], 16), 0.1, START, in_[1], out[1], sem=(sem, 0), mine=1)
-        note("d", None, nbytes / RATE, 0.0, [], [], after=[me], sem=(sem, 16))
+        note("d", None, nbytes / RATE * SLOW.get("d", 1.0), 0.0, [], [], after=[me], sem=(sem, 16))
         if next_:
             ops[me]["dep"][me - 2] = False
             ops[me + 1]["dep"][me - 1] = False
@@ -224,9 +364,14 @@ def rank_program(g, core, T, topo):
         cnt = {}
         known = {q: {} for q in Q}
         tok = {}
-        for i in arrange(ops)[0]:
+        form = tuple((o["q"], o["at"], tuple(sorted(o["dep"].items()))) for o in ops)
+        if form not in ORDERS:
+            ORDERS[form] = arrange(ops)[0]
+        for i in ORDERS[form]:
             o = ops[i]
             q = o["q"]
+            if q == "f":
+                continue
             if q in "dr":
                 tok[i] = (o["sem"][0], o["sem"][1], {})
                 cnt[o["sem"][0]] = o["sem"][1]
@@ -243,8 +388,10 @@ def rank_program(g, core, T, topo):
                     known[q][s2] = max(known[q].get(s2, 0), v2)
             if o["sem"] is None:
                 sem = "q" + q
-                cnt[sem] = cnt.get(sem, 0) + 1
-                o["fn"]().then_inc(T.sem[sem], 1)
+                made = o["fn"]()
+                for x in made if isinstance(made, list) else [made]:
+                    x.then_inc(T.sem[sem], 1)
+                    cnt[sem] = cnt.get(sem, 0) + 1
             else:
                 o["fn"]()
                 sem = o["sem"][0]
@@ -299,7 +446,7 @@ def rank_program(g, core, T, topo):
         run("v", lambda: g.vector.tensor_copy(out[0], a[0]), cyc(out, a), a[1], out[1])
 
     def scat(win, off, a):
-        run("v", lambda: g.vector.tensor_copy(win[0].indirect(off[0]), a[0]), max(64, SCATTER * a[2]), a[1] + off[1], win[1])
+        run("v", lambda: g.vector.tensor_copy(win[0].indirect(off[0]), a[0]), np.maximum(64, SCATTER * a[2]), a[1] + off[1], win[1])
 
     def red(out, a, op, ab=False):
         kw = {"apply_absolute_value": True} if ab else {}
@@ -333,12 +480,29 @@ def rank_program(g, core, T, topo):
             w += accum[1]
         run("s", lambda: g.scalar.activation(out[0], a[0], fn, **kw), a[2] * GATHER - 100 if a[3] == "ind" else a[2], regs, w)
 
+    def times(q, out, a, w):
+        if q == "v":
+            ts(out, a, w, Op.mult)
+        else:
+            act(out, a, scale=w)
+
+    def relu(q, out, a):
+        if q == "v":
+            ts(out, a, 0.0, Op.max)
+        else:
+            act(out, a, Fn.Relu)
+
     def copy(q, out, a):
         (cp if q == "v" else act)(out, a)
 
-    def mm(out, lhsT, rhs, start, stop):
-        c = max(min(64, lhsT[2]), rhs[2]) * (2 if rhs[3] == "four" else 0.5)
-        run("p", lambda: g.tensor.matmul(out[0], lhsT[0], rhs[0], start, stop), c, lhsT[1] + rhs[1], out[1], not (start or stop))
+    def mms(calls):
+        c = sum(max(min(64, a[2]), b[2]) * (2 if b[3] == "four" else 0.5) for o, a, b, s, e in calls)
+        run("p", lambda: [g.tensor.matmul(o[0], a[0], b[0], s, e) for o, a, b, s, e in calls], c,
+            [reg for x in calls for reg in x[1][1] + x[2][1]], [reg for x in calls for reg in x[0][1]],
+            not any(x[3] or x[4] for x in calls))
+
+    def mm(*call):
+        mms([call])
 
     def turn(out, a, ident):
         run("p", lambda: g.tensor.transpose(out[0], a[0], ident[0]), 0.5 * max(64, out[2]), a[1] + ident[1], out[1])
@@ -346,10 +510,13 @@ def rank_program(g, core, T, topo):
     def iota(out, pat, base=0, cm=0, flag=True):
         kw = {"allow_small_or_imprecise_dtypes": True} if flag else {}
         run("g", lambda: g.iota(out[0], pat, base, cm, **kw), 2 * out[2], [], out[1])
-        if small:
-            ops[-1]["dep"].setdefault(small[-1], False)
         if stage[0] == "const":
-            small.append(len(ops) - 1)
+            in_turn("small")
+        else:
+            ops[-1]["dep"].setdefault(line[("small",)], False)
+
+    def keep(out, pat, base, cm):
+        run("g", lambda: g.affine_select(out[0], out[0], pat, Op.is_ge, 0.0, base, cm), 2 * out[2], out[1], out[1])
 
     others = [q for q in range(len(T.cores)) if q != r]
     NE = 2
@@ -365,26 +532,50 @@ def rank_program(g, core, T, topo):
         me = note("g", lambda: g.remote_dma_fused(trs, local_sem=T.sem["sent"]), ISSUE + (2.0 if sem == "rp0" else 0.0),
                   HOP[sem[:2]], [reg for b in bufs for reg in b[1]], [], sem=("sent", n))
         note("r", None, 0.001, 0.0, [], [reg for x in lands for reg in x[1]], after=[me], sem=(sem, n))
+        line[sem] = me
+        for i in put_off.get(sem, ()):
+            ops[i]["dep"][me] = False
+
+    todo = list(enumerate(folds()))
+
+    def fold(other):
+        i, piece = todo.pop(0)
+        out, a = v(*piece), v(other, *piece[1:])
+        to = helper(core, T, topo)
+        rid, pid, _ = topo.addr(to)
+        eng = topo.engines(core, to)
+        one = RemoteDMATransfer(dst_ids=[DstId(rid=rid, pnc=pid)], dma_engine_mask=sum(1 << e for e in eng[len(eng) // 2:]),
+                                remote_sem=T.sem["f%d" % i], srcs=[out[0], a[0]], dsts=[out[0]], alu_op=2)
+        me = note("g", lambda: g.remote_dma_fused([one], local_sem=T.sem["sent"]), ISSUE, START, a[1], out[1],
+                  sem=("sent", len(eng) // 2), mine=2)
+        in_turn("fold")
+        ops[me]["dep"].setdefault(line["rb%d" % stage[1]], False)
+        note("f", None, 256 * out[2] / FRATE, FLAG + (0.0 if i else 3.0), [], [], after=[me])
+        in_turn("bytes")
+        note("r", None, 0.001, 0.0, [], [], after=[me + 1], sem=("f%d" % i, len(eng)))
+        in_turn("back")
 
     def place(q):
         return r - (1 if r > q else 0)
 
     third = R0 // 3
     stage[0] = "home"
-    fill(v("x2", 0, 1024), 0.0)
-    fill(v("x2", 1024, 4096), 0.0)
-    for a in (4096, 5120):
-        act(v("x2", a, a + 1024), v("x2", 0, 1024))
+    fill(v("x2", 0, 768), 0.0)
+    fill(v("x2", 768, 4608), 0.0)
+    for a in (4608, 5376):
+        act(v("x2", a, a + 768), v("x2", 0, 768))
     stage[0] = ""
-    dma("y", v("postI"), (T.post[:, :], []), 2e5)
-    dma("y", v("nearI"), (T.near[:, :], []), 2e5, True)
-    dma("y", v("abI", 0, 384), (T.absorb[:, 0:384], []), 2e5, True)
-    for i in (14, 15):
-        dma("y", (T["x2"][i:128:16, 0:R0], [("x2", i - 14, R0, 2)]), (T.rec[i:128:16, :], []), 1e5, True)
+    loads = {"post": [(v("postI"), T.post[:, :], 2e5)], "near": [(v("nearI"), T.near[:, :], 2e5)],
+             "ab0": [(v("abI", 0, 384), T.absorb[:, 0:384], 2e5)], "ab": [(v("abI", 384, 1152), T.absorb[:, 384:1152], 4e5)],
+             "ctr": [(v("ctr", 0, P0), T.cen[:, :], 1e5)],
+             "homes": [((T["x2"][i:128:16, 0:R0], [("x2", i - 14, R0, 2)]), T.rec[i:128:16, :], 1e5) for i in (14, 15)]}
     for i in range(3):
-        dma("y", v("hh", third * i, third * i + third), (T.rec[:, third * i:third * i + third], []), 5e5, True)
-    dma("y", v("ctr", 0, P0), (T.cen[:, :], []), 1e5, True)
-    dma("y", v("abI", 384, 1152), (T.absorb[:, 384:1152], []), 4e5, True)
+        a, b = third * i, third * i + third
+        loads["rec%d" % i] = [(v("hh", a, b), T.rec[:, a:b], 5e5)]
+        b = min(b, R0 - 512 * HELP[0])
+        loads["xd%d" % i] = [(v("xd", a, b), T.rec[:, a:b], 256 * (b - a))] if b > a else []
+    for i, (out, in_, size) in enumerate(x for name in LOADS.split() for x in loads[name]):
+        dma("y", out, (in_, []), size, i > 0)
 
     pI, p15 = v("pcol", 0, 1), v("pcol", 1, 2)
     PF, MF_, PB = col(0), col(1), col(2)
@@ -401,32 +592,40 @@ def rank_program(g, core, T, topo):
     iota(v("n15"), [[0, 8], [1, 16]])
     iota(v("cidx"), [[1, 32]], PD + 1)
     iota(v("w128"), [[-1, 128]], 128)
-    iota(v("ni"), [[1, 128]])
     iota(v("whi"), [[128, 4], [0, 8]])
     iota(v("i32k"), [[16, 32]])
     iota(v("n15r"), [[0, 16], [-1, 16]], 15)
     iota(v("slot"), [[16, P0]])
-    for b, a, e in (("hh", R0, R), ("live", P0, WP), ("full", P0, TS), ("wk", 0, 16)):
-        fill(v(b, a, e), 0.0)
-    fill(v("ones"), 1.0)
-    for i, w in ((0, 32768), (1, 1), (2, -256), (3, -16), (4, -32768 * 128), (5, -15), (7, 2 ** 23), (12, 32768), (14, 16)):
-        fill(v("wk", i, i + 1), float(w))
     stage[0] = ""
-    iota(v("postf", MD, WP), [[1, 128]], R)
-    iota(v("postf", PD, MD), [[0, 32]])
+    for b, a, e in (("hh", R0, R), ("live", P0, WP), ("full", P0, TS), ("wk", 0, 16)):
+        iota(v(b, a, e), [[0, e - a]])
+    iota(v("ones"), [[0, 256]], 1)
+    iota(col(31), [[0, 1]], -13)
+    for i, w in ((0, 32768), (1, 1), (2, -256), (3, -16), (4, -32768 * 128), (5, -16), (7, 2 ** 23), (12, 32768), (14, 16)):
+        iota(v("wk", i, i + 1), [[0, 1]], w)
+    for b in ("postf", "cmf1", "cmf2"):
+        iota(v(b, MD, WP), [[1, 128]], R)
+        iota(v(b, PD, MD), [[0, 32]])
+    iota(v("lg"), [[16, 8], [0, 8], [1, 16]])
     iota(v("vhi"), [[1, 2], [0, 256]], 26)
     iota(v("vlo"), [[0, 2], [1, 256]])
     for k in range(RO):
-        iota(v("atab%d" % k), [[1, 96]], R0 + 96 * k)
+        first = len(ops)
         iota(v("bw%d" % k, 128, 144), [[0, 16]], 8192)
         for q in range(4):
             iota(v("tab%d" % k, TS * q, TS * q + TS), [[0, TS]])
+        put_off.setdefault("rb%d" % (k - 1), []).extend(range(first, len(ops)))
+        first = len(ops)
+        iota(v("atab%d" % k), [[-1, 96]], -R0 - 96 * k)
+        if k < RO - 1:
+            iota(v("gone%d" % k), [[0, WP]])
+        put_off.setdefault("rb%d" % k, []).extend(range(first, len(ops)))
     iota(v("vm"), [[0, 128]], 255)
     iota(v("sd1", 0, PD), [[0, PD]])
     iota(v("wt"), [[0, 512]])
     for k in (4, 5):
         iota(v("wt", k, 512, 16), [[0, 32]], 1)
-    iota(v("xg", 16 * MD, XW, 16), [[0, 128]], -1)
+    iota(v("xg", 16 * MD, XW, 16), [[0, 128]], -8192)
     for b, a, e in (("x1", R0, R), ("x2", R0, R), ("ff", P0, 512), ("nearf", P0, WP), ("ctr", P0, WP)):
         iota(v(b, a, e), [[0, e - a]])
     stage[0] = "const"
@@ -449,7 +648,7 @@ def rank_program(g, core, T, topo):
     HB = (col(16), col(17))
     ts(v("e16"), v("zi"), PB, Op.is_equal)
     ts(v("hm"), v("zi"), PB, Op.is_equal, col(6), Op.mult)
-    for b, w in (("em", MF_), ("rx", KN16), ("rmp", K32), ("e16f", 1.0)):
+    for b, w in (("em", MF_), ("rx", KN16), ("rmp", K32), ("rmn", KN32)):
         act(v(b), v("e16"), scale=w)
     cp(v("post16", 0, P0), v("postI"))
     cp(v("postf", 0, P0), v("postI"))
@@ -457,39 +656,42 @@ def rank_program(g, core, T, topo):
     ts(col(20), row(1), -256.0, Op.mult, row(0), Op.add)
     ts(col(21), row(1), -256.0, Op.mult)
     ts(v("bo"), v("cg"), PB, Op.is_equal)
-    for b, w in (("nsp", col(21)), ("bo14p", K16c), ("bo14n", KN16), ("bof", 1.0)):
-        act(v(b), v("bo"), scale=w)
-    for b in ("g8", "cs"):
-        ts(v(b), v("i8"), PB, Op.is_equal)
+    for q, b, w in zip(CONST, ("nsp", "bo14p", "bo14n", "bof", "bofn"), (col(21), K16c, KN16, 1.0, -1.0)):
+        times(q, v(b), v("bo"), w)
+    ts(v("g8"), v("i8"), PB, Op.is_equal)
+    ts(v("bo64k"), v("bo"), 65536.0, Op.mult)
+    ts(v("nident"), v("dcp"), 0.0, Op.is_equal, -1.0, Op.mult)
     for b, w in (("rgp", K32), ("rgn", KN32)):
         ts(v(b), v("i8"), PB, Op.is_equal, w, Op.mult)
     ts(v("wc128"), v("n15"), row(0), Op.add)
     tt(v("bou"), v("wc128"), v("bo"), Op.mult)
     for j in range(16):
         ts(blk("nm", j), v("bou"), float(j), Op.is_gt, col(20), Op.mult)
+        if j % 4 == 3:
+            together(len(ops) - 4)
     for h in range(2):
         tt(v("wl", 8 * h, 8 * h + 8), v("wk", 8 * h, 8 * h + 8), v("r16", 0, 8), Op.mult)
         red(col(22 + h), v("wl", 8 * h, 8 * h + 8), Op.add)
-    ts(v("lga"), v("ni"), col(23), Op.mult, col(22), Op.add)
     stage[0] = "late"
-    for k in range(8):
-        act(blk("lg", k), v("lga"), scale=v("cs", k, k + 1))
+    ts(v("lg"), v("lg"), col(23), Op.mult, col(22), Op.add)
+    keep(v("lg"), [[0, 8], [-16, 8], [0, 16]], 0, 1)
+    keep(v("lg"), [[0, 8], [16, 8], [0, 16]], 15, -1)
     stage[0] = "const"
     ts(v("sd2"), v("cidx"), col(18), Op.is_ge, 16.0, Op.mult)
     ts(v("sd3"), v("cidx"), col(19), Op.is_ge, 84.0, Op.mult)
     tt(v("sd1", PD, TS), v("sd2"), v("sd3"), Op.add)
     for b, w in (("ident", 1.0), ("ibig", BIG)):
         ts(v(b), v("dcp"), 0.0, Op.is_equal, w, Op.mult)
-    for b, w in (("d14", C14), ("d15", C15)):
-        act(v(b), v("ident"), scale=w)
+    for q, b, w in zip(CONST[5:], ("d14", "d15", "identf", "d384", "dneg"), (C14, C15, 1.0, 384.0, -6143 / 16)):
+        times(q, v(b), v("ident"), w)
     ts(v("wa128"), v("dcp"), 0.0, Op.is_gt, -32.0, Op.mult)
     tt(v("wb128"), v("wa128"), v("bo"), Op.mult)
     tt(v("px"), v("wb128"), v("ident"), Op.add)
+    ts(v("away"), v("n15"), MF_, Op.not_equal, -BIG, Op.mult)
     ts(v("kd", 0, 2), v("h4", 0, 2), MF_, Op.add, 16.0, Op.mult)
-    cp(v("kx16"), v("i32"))
     ts(v("dat"), v("w128"), row(0), Op.mult, row(1), Op.add)
-    ts(v("ckb"), v("n15r"), v("ident", 1, 2), Op.mult)
-    ts(v("cka"), v("ones"), v("ibig", 0, 1), Op.mult, -1.0, Op.mult)
+    ts(v("ckb"), v("n15r"), -7.5, Op.add, v("ident", 1, 2), Op.mult)
+    ts(v("cka"), v("ones", 0, 256), v("ibig", 0, 1), Op.mult, -1.0, Op.mult)
     ts(v("ck"), v("n15r", 0, 128), v("ident", 1, 2), Op.mult, v("ibig", 0, 1), Op.subtract)
     ts(v("rst"), v("n15r"), 15.0, Op.is_equal, -2.0 ** 22, Op.mult)
     ts(v("nsh"), v("nearI"), 4, Op.arith_shift_right, 96, Op.bitwise_and)
@@ -497,35 +699,60 @@ def rank_program(g, core, T, topo):
     cp(v("near16", 0, P0), v("nearf", 0, P0))
     ts(v("wt", 2, 512, 16), v("whi"), PB, Op.add, 1 / 16, Op.mult)
     ts(v("wt", 3, 512, 16), v("whi"), 0.0, Op.mult, MF_, Op.add)
-    ts(v("tq", 271, 272), row(2), -34.0, Op.mult, row(6), Op.add)
-    ts(v("miw"), v("i32", 0, 16), MF_, Op.is_equal)
+    ts(col(13), row(5), -8.5 / 16, Op.mult, row(6), Op.add)
+    for a in sorted({128 * p[-1][0] + 15 for p in PARTS}):
+        ts(v("tq1", a, a + 1), row(2), -34.0, Op.mult, col(13), Op.add)
     ts(v("tr"), v("i32k"), MF_, Op.add, float(R), Op.add)
     stage[0] = ""
-    for t in range(RO):
+    for t in range(RO - 1):
         cp(v("ab16", 384 * t, 384 * t + 384), v("abI", 384 * t, 384 * t + 384))
     stage[0] = "late"
     mm(v("p1"), v("d14"), v("vhi"), True, False)
     mm(v("p1"), v("d15"), v("vlo"), False, True)
-    for t in range(RO):
+    act(v("vst0"), v("p1"))
+    for t in range(1, RO):
         ts(col(24 + t), C14, 2.0 * t, Op.mult)
-        act(v("vst%d" % t), v("p1"), Fn.Identity, bias=col(24 + t))
+        if CONST[11] == "v":
+            ts(v("vst%d" % t), v("vst0"), col(24 + t), Op.add)
+        else:
+            act(v("vst%d" % t), v("vst0"), Fn.Identity, bias=col(24 + t))
 
     stage[0] = "home"
     for i, q in enumerate(HOME):
         a, b = 64 * i, min(P0, 64 * i + 64)
         copy(q, v("xg", 16 * a, 16 * b), ind(v("x2", 0, R0), v("post16", a, b)))
+        in_turn("home", q)
     for c in range(4):
         a, b = 128 * c, min(P0, 128 * c + 128)
-        for m in range(16):
-            mm(v("p%d" % (4 + c % 3), a, b), fam("hm", m), v("xg", 16 * a + m, 16 * b, 16), m == 0, m == 15)
+        mms([(v("p%d" % (4 + c % 3), a, b), fam("hm", m), v("xg", 16 * a + m, 16 * b, 16), m == 0, m == 15) for m in range(16)])
         tt(v("live", a, b), v("slot", a, b), v("p%d" % (4 + c % 3), a, b), Op.is_equal)
 
-    def count_full(n):
-        mm(v("p0", 0, n), v("bo"), v("live", 0, n), True, True)
-        ts(v("full", 0, n), v("p0", 0, n), 13.5, Op.is_ge)
+    stage[0] = "prep"
+    for k in range(2):
+        whole = v("abI", 384 * k + 384, 384 * k + 768)
+        cp(v("abh", 768 * k, 768 * k + 384), whole)
+        tt(v("abh", 768 * k + 384, 768 * k + 768), whole, v("abh", 768 * k, 768 * k + 384), Op.subtract)
+        ts(col(27 + k), row(2 * k), 1.0, Op.mult, row(2 * k + 1), Op.add)
+        times(CONST[10], v("cw%d" % (k + 1)), v("e16"), col(27 + k))
+    for k in range(4):
+        dma("y", (T["x2"][k:128:16, 0:R0], [("x2", k, R0, 4)]), v("abh", 384 * k, 384 * k + 384), 1e5)
+    fill(col(29), -7.5)
+    act(v("pm"), v("postf", 0, P0), Fn.Identity, bias=col(29))
+    ts(v("h16"), v("pm"), MAGIC, Op.add, MAGIC, Op.subtract)
+    mm(v("p5", 0, P0), v("d384"), v("postf", 0, P0), True, False)
+    mm(v("p5", 0, P0), v("dneg"), v("h16"), False, True)
+    cp(v("w16", 0, P0), v("p5", 0, P0))
+    stage[0] = "home"
+
+    def count_full(n, k):
         scan(v("scan", 0, n), v("full", 0, n), v("sd1", 0, n), 0.0, Op.add, Op.max)
         for h in range(2):
-            act(v("junk%d" % h, 0, n), v("scan", 0, n), Fn.Sign, bias=HB[h], scale=-1.0, accum=v("cm%d" % h, 0, 1))
+            if FULLQ[k] == "v" and h:
+                ts(v("junk1", 0, n), v("scan", 0, n), HB[h], Op.is_le, 2.0, Op.mult)
+                red(col(30), v("junk1", 0, n), Op.add)
+                ts(v("cm1", 0, 1), col(30), float(-n), Op.add)
+            else:
+                act(v("junk%d" % h, 0, n), v("scan", 0, n), Fn.Sign, bias=HB[h], scale=-1.0, accum=v("cm%d" % h, 0, 1))
 
     def p0(a, b):
         return v("p0", a, b)
@@ -533,19 +760,28 @@ def rank_program(g, core, T, topo):
     def p1(a, b):
         return v("p1", a, b)
 
+    def above(q, out, a):
+        if q == "v":
+            mms([(v("p6", m, 512, 16), v("ident"), a, True, True) for m in range(16)])
+            tt(v(out), v("xs"), v("p6"), Op.max)
+        else:
+            mms([(v("p6"), v("ident"), v("xs"), True, False)] + [(v("p6", m, 512, 16), v("nident"), a, False, m == 15) for m in range(16)])
+            act(v(out), v("p6"), Fn.Relu)
+
     def row_list(out, one):
         mm(p0(0, 2), v("ident"), v("kd", 0, 2), True, False)
-        for j in range(16):
-            mm(p0(0, 2), fam("em", j), v(one, j, 32, 16), False, j == 15)
+        mms([(p0(0, 2), fam("em", j), v(one, j, 32, 16), False, j == 15) for j in range(16)])
         cp(v(out), p0(0, 2))
 
-    count_full(P0)
+    mm(v("p0", 0, P0), v("bo"), v("live", 0, P0), True, True)
+    ts(v("full", 0, P0), v("p0", 0, P0), 13.5, Op.is_ge)
+    count_full(P0, 0)
     for t in range(RO):
         nq = P0 + SP * t
         ne = max(P0, nq - SP)
         last = t == RO - 1
         xa = ["hh", "x1", "x2"][t]
-        xb = ["x1", "x2", "x1"][t]
+        xb = ["x1", "x2", "x2"][t]
         Xa = v(xa, 0, R)
         Xb = v(xb, 0, R)
         tab, plr, pls, lst, bw, mf, arr = [n + str(t) for n in ("tab", "plr", "pls", "lst", "bw", "mf", "arr")]
@@ -553,6 +789,28 @@ def rank_program(g, core, T, topo):
         bs = v(bw, 32 * r, 32 * r + 32)
         chunks = [(128 * c, min(nq, 128 * c + 128)) for c in range(4)]
         halves = [(0, 0, 256, chunks[0:2]), (1, 256, nq, chunks[2:4])]
+        parts = [(h, chunks[p[0]][0], chunks[p[-1]][1], [chunks[c] for c in p]) for h, p in enumerate(PARTS[t])]
+
+        def absorb():
+            stage[0] = "absorb"
+            own = R0 - 512 * HELP[t]
+            for a in range(0, R0, 512):
+                which = ind(Xa, v("ab16", 384 * t + a // 16, 384 * t + a // 16 + 32))
+                if a < own:
+                    tt(v(xb, a, a + 512), which, v("xd", a, a + 512), Op.max)
+                else:
+                    act(v(xb, a, a + 512), which)
+                    in_turn("absorb", t)
+                    if t and a >= 512 * EARLY:
+                        ops[-1]["dep"].setdefault(mark[0], False)
+                    elif t and FOLD[2 * t]:
+                        ops[near[0][1]]["dep"][len(ops) - 1] = False
+                    if not FOLD[2 * t] or (t and a >= 512 * EARLY):
+                        tt(v(xb, a, a + 512), v(xb, a, a + 512), v(xa, a, a + 512), Op.max)
+                    elif todo[0][1][2] == a + 512:
+                        fold(xa)
+            if t == 0 and HELP[1] < 12:
+                dma("y", v("xd", 0, R0 - 512 * HELP[1]), v(xb, 0, R0 - 512 * HELP[1]), 131072 * (12 - HELP[1]))
 
         stage[:] = ["list", t]
         scan(v("scan", ne, TS), v("full", ne, TS), v("sd1", ne, TS), v("scan", ne - 1, ne), Op.add, Op.max)
@@ -564,44 +822,46 @@ def rank_program(g, core, T, topo):
         ts(pl16, v("acc"), 0.5, Op.mult, ne / 2, Op.add)
         scat(v(tab), v(pls), v("dat", 32 * r, 32 * r + 32))
         stage[0] = "rows"
-        cp(v("lp"), ind(v("live"), pl16))
-        cp(v("postp"), ind(v("postf"), pl16))
+        copy(MISC[0], v("lp"), ind(v("live"), pl16))
+        copy(MISC[1], v("postp"), ind(v("postf"), pl16))
         cp(v("ps16"), v("postp"))
+        if t:
+            copy(MISC[2], v("cp%d" % t), ind(v("cmf%d" % t), pl16))
+            cp(v("cps16"), v("cp%d" % t))
         mm(p0(0, 32), v("px"), v("lp"), True, True)
         ts(v("oa"), p0(0, 32), 0.0, Op.max)
         row_list("lac", "oa")
-        stage[0] = "absorb"
-        own = R0 - 512 * HELP[t]
         if t == 0:
-            act(v("xd", 0, own), v("hh", 0, own))
-        for a in range(0, R0, 512):
-            which = ind(Xa, v("ab16", 384 * t + a // 16, 384 * t + a // 16 + 32))
-            if a < own:
-                tt(v(xb, a, a + 512), which, v("xd", a, a + 512), Op.max)
-            else:
-                act(v(xb, a, a + 512), which)
-                tt(v(xb, a, a + 512), v(xb, a, a + 512), v(xa, a, a + 512), Op.max)
-        if not last:
-            dma("y", v("xd", 0, R0 - 512 * HELP[t + 1]), v(xb, 0, R0 - 512 * HELP[t + 1]), 131072 * (12 - HELP[t + 1]))
+            absorb()
         stage[0] = "tab"
-        for (c0, c1, d0, d1) in ((0, 2 * r, 0, 32 * r), (2 * r, 6, 32 * r + 32, 128)):
-            if c1 > c0:
-                scat(v(tab), v(plr, c0, c1), v("dat", d0, d1))
+        near = []
+        cut = min(max(r, 1), 2)
+        for c0, c1 in ((0, cut), (cut, 3)):
+            scat(v(tab), v(plr, 2 * c0, 2 * c1), v("dat", 32 * others[c0], 32 * others[c1 - 1] + 32))
         for i, q in enumerate(NEAR[t]):
-            a, b = 64 * i, min(nq, 64 * i + 64)
             stage[0] = "near%d" % i
-            copy(q, v("ng", 16 * a, 16 * b), ind(v(tab), v("near16", a, b)))
+            step = 32 if q == "v" else 64
+            for a in range(64 * i, min(nq, 64 * i + 64), step):
+                b = min(nq, a + step)
+                copy(q, v("ng", 16 * a, 16 * b), ind(v(tab), v("near16", a, b)))
+                in_turn("near", t, q)
+                if q == "s":
+                    near.append((b, len(ops) - 1))
         stage[0] = "split"
         XS = v("xs")
-        cp(XS, ind(Xb, v("ps16")))
+        if t == 0:
+            copy(XSQ[t], XS, ind(Xb, v("ps16")))
+        else:
+            copy(XSQ[t], XS, ind(Xa, v("ps16")))
+            tt(XS, ind(Xa, v("cps16")), XS, Op.max)
+        if not last:
+            dma("y", v("xg", 16 * nq, 16 * nq + 512), XS, 131072)
         cp(v("ac"), ind(XS, v("lac")))
-        tt(v("ma"), ind(v("ac"), v("kx16")), XS, Op.max)
+        above(MAB[0][t], "ma", v("ac"))
         mm(p0(0, 32), v("ck"), v("ones", 0, 32), True, False)
         mm(p0(0, 32), v("ibig"), v("lp"), False, False)
-        for m in range(16):
-            mm(p0(0, 32), fam("rx", m), v("xs", m, 512, 16), False, False)
-        for m in range(16):
-            mm(p0(0, 32), fam("rmp", m), v("ma", m, 512, 16), False, m == 15)
+        mms([(p0(0, 32), fam("rx", m), v("xs", m, 512, 16), False, False) for m in range(16)])
+        mms([(p0(0, 32), fam("rmp", m), v("ma", m, 512, 16), False, m == 15) for m in range(16)])
         tr(v("ktk"), p0(0, 32))
         scan(v("kts"), v("rst", 0, 32), v("ktk"), 0.0, Op.add, Op.max)
         for h in range(2):
@@ -614,49 +874,66 @@ def rank_program(g, core, T, topo):
         for i, q in enumerate(SLOT[t]):
             stage[0] = "slot%d" % i
             step = 32 if q == "v" else 64
-            for a in range(64 * i, min(nq, 64 * i + 64), step):
-                b = min(nq, a + step)
-                copy(q, v("xg", 16 * a, 16 * b), ind(Xb, v("post16", a, b)))
+            lo, hi = (ne, nq) if i == 7 else (64 * i, min(ne, 64 * i + 64))
+            for a in range(lo, hi, step):
+                b = min(hi, a + step)
+                XG = v("xg", 16 * a, 16 * b)
+                if t == 0:
+                    copy(q, XG, ind(Xb, v("post16", a, b)))
+                    in_turn("slot", t, q)
+                    continue
+                which = ind(Xa, v("cmu%d" % t, a, b))
+                if q == "v" or i == 7:
+                    tt(XG, which, XG, Op.max)
+                    in_turn("slot", t, "v")
+                else:
+                    act(v("mc", 16 * a, 16 * b), which)
+                    in_turn("slot", t, q)
+                    if not FOLD[2 * t - 1]:
+                        for e in range(16 * a, 16 * b, 512):
+                            tt(v("xg", e, e + 512), v("mc", e, e + 512), v("xg", e, e + 512), Op.max)
+                    elif todo[0][1][2] == 16 * b:
+                        fold("mc")
 
-        for h, qa, qb, cs in halves:
+        for h, qa, qb, cs in parts:
             stage[0] = "first%d" % h
             for a, b in cs:
                 mm(p1(a - qa, b - qa), v("nsp"), v(tab, TS * r + a, TS * r + b), True, False)
-                for j in range(16):
-                    mm(p1(a - qa, b - qa), blk("nm", j), v("ng", 16 * a + j, 16 * b, 16), False, j == 15)
-            act(v("ff", qa, qb), p1(0, qb - qa), Fn.Relu)
+                mms([(p1(a - qa, b - qa), blk("nm", j), v("ng", 16 * a + j, 16 * b, 16), False, j == 15) for j in range(16)])
+            relu(RELU[h], v("ff", qa, qb), p1(0, qb - qa))
+            later = [i for b, i in near if b > qb]
+            for i in later[1:2] if RELU[h] == "s" else ():
+                ops[i]["dep"][len(ops) - 1] = False
             nl = (qb - qa) // 16
-            for k in range(16):
-                mm(p1(0, nl), fam("e16", k), v("ff", qa + k, qb, 16), k == 0, k == 15)
-            for i, (a, b) in enumerate(cs):
-                mm(p1(32 + 8 * i, 40 + 8 * i), v("ff", a, a + 128), v("g8"), True, True)
+            mms([(p1(0, nl), fam("e16", k), v("ff", qa + k, qb, 16), k == 0, k == 15) for k in range(16)] +
+                [(p1(32 + 8 * i, 40 + 8 * i), v("ff", a, a + 128), v("g8"), True, True) for i, (a, b) in enumerate(cs)])
             ts(v("tgl", qa // 16, qa // 16 + nl), p1(0, nl), -1.0, Op.mult, 128.0, Op.add)
-            cp(v("wt", qa, qa + 256, 16), p1(32, 48))
+            cp(v("wt", qa, qa + 128 * len(cs), 16), p1(32, 32 + 8 * len(cs)))
             stage[0] = "bt%d" % h
-            act(v("bt", qa, qb), ind(v(bw), v("tgl", qa // 16, qa // 16 + nl)))
+            copy(BTQ[h], v("bt", qa, qb), ind(v(bw), v("tgl", qa // 16, qa // 16 + nl)))
+            mark[0] = len(ops) - 1
+            for i in later[2:3] if BTQ[h] == "s" else ():
+                ops[i]["dep"][len(ops) - 1] = False
 
         stage[0] = "go"
-        for m in range(16):
-            mm(v("p6", m, 512, 16), v("ident"), bs, True, True)
-        tt(v("mb"), XS, v("p6"), Op.max)
+        above(MAB[1][t], "mb", bs)
         mm(p0(0, 32), v("ck"), v("ones", 0, 32), True, False)
         mm(p0(0, 32), v("ibig"), v("lp"), False, False)
-        for m in range(16):
-            mm(p0(0, 32), fam("rmp", m), v("ma", m, 512, 16), False, False)
-        for m in range(32):
-            mm(p0(0, 32), fam("rx", m // 2), v("mb", m // 2, 512, 16), False, False)
-        mm(p0(0, 32), v("bo14p"), bs, False, False)
-        mm(p0(0, 32), v("bo14n"), v("ac"), False, True)
+        mms([(p0(0, 32), fam("rmp", m), v("ma", m, 512, 16), False, False) for m in range(16)])
+        mms([(p0(0, 32), fam("rmn", m), v("mb", m, 512, 16), False, False) for m in range(16)])
+        mm(p0(0, 32), v("bo14p" if MAB[1][t] == "v" else "bo14n"), bs, False, False)
+        mm(p0(0, 32), v("bo14n" if MAB[0][t] == "v" else "bo14p"), v("ac"), False, True)
         ts(v("go"), p0(0, 32), 15.5, Op.is_ge)
         ts(v("nog"), p0(0, 32), 15.5, Op.is_lt)
         mm(p0(0, 32), v("px"), v("nog"), True, True)
         if not last:
-            mm(p0(32, 64), v("bo"), v("go"), True, True)
-            ts(v("thr"), p0(32, 64), -301.0, Op.mult, 13 * 301 - 0.5, Op.add)
-            tt(v("lval", 128, 160), v("lp"), v("go"), Op.subtract)
+            tt(v("stay"), v("lp"), v("go"), Op.subtract)
         ts(v("rw"), p0(0, 32), 0.0, Op.max)
+        ts(v("rwt"), v("rw"), -8001.0, Op.mult, 1.0, Op.add)
         mm(p0(0, 32), fam("em", 15), v("rw"), True, True)
         tt(v("hw"), v("vst%d" % t, 0, 512, 16), p0(0, 32), Op.add)
+        if not last:
+            row_list("lrc", "rw")
         stage[0] = "homes"
         tt(v("spa"), v("postp"), v("tr"), Op.subtract)
         tt(v("spb"), v("spa"), v("go"), Op.mult)
@@ -668,114 +945,169 @@ def rank_program(g, core, T, topo):
         if not last:
             act(v("nearp"), ind(v("nearf"), pl16))
             cp(v("near16", nq, nq + 32), v("nearp"))
-            act(v("nearf", nq, nq + 32), v("nearp"))
+            cp(v("nearf", nq, nq + 32), v("nearp"))
+
+        def maxima(q, other, tb, ph, dst, qa, qb, cs):
+            w = qb - qa
+            for a, b in cs:
+                turn(v("p7", a - qa, a - qa + 128, 1, b - a), v(other, a, b), v("ident"))
+            for a, b, e in ([(qa, qa + 128, w)] if w % 128 == 0 else [c + (128,) for c in cs]):
+                copy(q, v(tb, a, a + e, 1, b - a), v("p7", a - qa, a - qa + e, 1, b - a))
+            for a, b in cs:
+                turn(v(ph[0], ph[1] + a - qa, ph[1] + b - qa), v(tb, a, a + 128, 1, b - a), v("ident", 0, b - a, 1, b - a))
+            for m0 in range(0, 16, 4):
+                first = len(ops)
+                for m in range(m0, m0 + 4):
+                    o = 16 * qa + m * w
+                    tt(v(dst, o, o + w), v("xg", 16 * qa + m, 16 * qb, 16), v(ph[0], ph[1], ph[1] + w), Op.max)
+                together(first)
+                yield range(m0, m0 + 4)
+
+        def sums(pb, qa, m, dst, da, db, a, b, by):
+            o = 16 * da + m * (db - da) - da
+            return (v(pb, a - qa + m, a - qa + 128, 16, b - a), v(dst, o + a, o + b), v(by), False, False)
 
         for h, qa, qb, cs in halves:
-            w = qb - qa
-            ph, pg_ = "p%d" % (2 + h), "p%d" % (4 + h)
-            mm(v(pg_, 0, 256), v("ones", 0, 128), v("cka"), True, False)
-            for a, b in cs:
-                mm(v(pg_, a - qa, a - qa + 128), v("live", a, a + 128), v("ibig"), False, False)
-            for d, (other, dst, sums, alone) in enumerate((("ctr", "mc", "rgp", "bo14n"), ("bt", "md", "rgn", "bo14p"))):
-                stage[0] = "dist%d%d" % (h, d)
-                tb = "tb%d" % d
-                for a, b in cs:
-                    turn(v("p7", a - qa, a - qa + 128, 1, b - a), v(other, a, b), v("ident"))
-                for a, b, e in ([(qa, qa + 128, 256)] if h == 0 else [c + (128,) for c in cs]):
-                    cp(v(tb, a, a + e, 1, b - a), v("p7", a - qa, a - qa + e, 1, b - a))
-                for a, b in cs:
-                    turn(v(ph, 256 * d + a - qa, 256 * d + b - qa), v(tb, a, a + 128, 1, b - a), v("ident", 0, b - a, 1, b - a))
-                for a, b in cs:
-                    mm(v(pg_, a - qa, a - qa + 128, 1, b - a), v(other, a, b), v(alone), False, False)
-                for m in range(16):
-                    o = 16 * qa + m * w
-                    tt(v(dst, o, o + w), v("xg", 16 * qa + m, 16 * qb, 16), v(ph, 256 * d, 256 * d + w), Op.max)
-                    for a, b in cs:
-                        mm(v(pg_, a - qa + m, a - qa + 128, 16, b - a), v(dst, o + a - qa, o + b - qa), v(sums), False, False)
-            mm(v(pg_, 0, 256), v("ones", 0, 128), v("ckb"), False, True)
+            stage[0] = "centre%d" % h
+            list(maxima(TBQ[0], "ctr", "tb0", ("p2", qa), "mc", qa, qb, cs))
+        for h, qa, qb, cs in parts:
+            w, wide = qb - qa, 128 * len(cs)
+            ph, pb = ("p%d" % (3 - h % 2), 512), "p%d" % (4 + h % 2)
+            stage[0] = "dist%d" % h
+            mms([(v(pb, 0, wide), v("ones", 0, 128), v("cka", 0, wide), True, False)] +
+                [(v(pb, a - qa, a - qa + 128), v("live", a, a + 128), v("ibig"), False, False) for a, b in cs] +
+                [(v(pb, a - qa, a - qa + 128, 1, b - a), v("ctr", a, b), v("bo14n"), False, False) for a, b in cs] +
+                [sums(pb, qa, m, "mc", *halves[a // 256][1:3], a, b, "rgp") for a, b in cs for m in range(16)])
+            mms([(v(pb, a - qa, a - qa + 128, 1, b - a), v("bt", a, b), v("bo14p"), False, False) for a, b in cs])
+            for rows in maxima(TBQ[1], "bt", "tb1", ph, "md", qa, qb, cs):
+                mms([sums(pb, qa, m, "md", qa, qb, a, b, "rgn") for m in rows for a, b in cs])
+            mm(v(pb, 0, wide), v("ones", 0, 128), v("ckb", 0, wide), False, True)
 
-            kt, kmi, kma = "kt%d" % h, "kmi%d" % h, "kma%d" % h
             stage[0] = "offer%d" % h
-            scan(v(kt), v("rst"), v(pg_, 0, 256), 0.0, Op.add, Op.max)
-            cp(v(kmi), v(kt, 15, 256, 16))
-            ts(v("wt", qa + 7, qa + 256, 16), v(kt, 15, 256, 16), 15.5, Op.is_lt)
-            ts(v(kma), v(kmi), 15, Op.bitwise_and)
-            cp(v("wt", qa + 1, qa + 256, 16), v(kma))
+            best = v("kt", qa + 15, qa + wide, 16)
+            kn = v("kn", qa // 16, (qa + wide) // 16)
+            scan(v("kt", qa, qa + wide), v("rst", 0, wide), v(pb, 0, wide), 0.0, Op.add, Op.max)
+            ts(kn, best, MAGIC, Op.add, MAGIC, Op.subtract)
+            ts(v("wt", qa + 7, qa + wide, 16), best, 8.0, Op.is_lt)
+            tt(v("wt", qa + 1, qa + wide, 16), best, kn, Op.subtract)
             for a, b in cs:
-                turn(v(ph, a - qa, b - qa), v("wt", a, a + 128, 1, b - a), v("ident", 0, b - a, 1, b - a))
-            cp(v("tq", qa + 16 * h, qb + 16 * h), v(ph, 0, w))
-            keys = v("tq", qa + 15 * h, qb + 16 * h)
-            for k, pb in zip(range(0, 8, 2), (["p4", "p6", "p4", "p6"], ["p5", "p1", "p4", "p6"])[h]):
-                for e in range(2):
-                    mm(v(pb, keys[2] * e, keys[2] * (e + 1)), blk("lg", k + e), keys, True, True)
-                for e in range(2):
-                    red(v("ms%d" % h, k + e, k + e + 1), v(pb, keys[2] * e, keys[2] * (e + 1)), Op.min, True)
-                for e in range(k, k + 2 * h):
-                    ts(v("zx", 16 * e, 16 * e + 16), v("r16"), v("ms1", e, e + 1), Op.mult, v("ms0", e, e + 1), Op.min)
+                turn(v(ph[0], 512 + a - qa, 512 + b - qa), v("wt", a, a + 128, 1, b - a), v("ident", 0, b - a, 1, b - a))
+            end = h == len(parts) - 1
+            o = qa + 16 * end
+            copy(TQQ[h], v("tq%d" % end, o, o + w), v(ph[0], 512, 512 + w))
+            keys = v("tq%d" % end, o - end, o + w)
+            each = 4 if keys[2] <= 128 else 2
+            ms = "lsf" if h == 0 else "ms"
+            for k in range(0, 8, each):
+                kb = ("p6", pb)[k // each % 2]
+                mms([(v(kb, keys[2] * e, keys[2] * (e + 1)), blk("lg", k + e), keys, True, True) for e in range(each)])
+                first = len(ops)
+                for e in range(each):
+                    red(v(ms, k + e, k + e + 1), v(kb, keys[2] * e, keys[2] * (e + 1)), Op.min, True)
+                together(first)
+            if h:
+                tt(v("lsf"), v("lsf"), v("ms"), Op.min)
         if not last:
+            stage[0] = "count"
+            scat(v("live"), pl16, v("stay"))
+            mm(p1(0, nq), v("bo"), v("live", 0, nq), True, True)
+            act(v("cnt", 0, nq), p1(0, nq), Fn.Identity, bias=col(31))
             scat(v("ctr"), pl16, v("ac"))
-            act(v("ctr", nq, nq + 32), bs)
-        mm(p0(0, 8), v("zx"), v("cs"), True, True)
-        cp(v("ls16"), p0(0, 8))
-        cp(v(mf), ind(v("xg"), v("ls16")))
+            cp(v("ctr", nq, nq + 32), bs)
+        stage[0] = "offer%d" % (len(parts) - 1)
+        ts(v("ls16"), v("lsf"), -8.5, Op.add)
+        copy(MISC[3], v(mf), ind(v("xg"), v("ls16")))
         send([v(mf, 32 * q, 32 * q + 32) for q in others],
              [v(arr, 32 * place(q), 32 * place(q) + 32) for q in others], [v(arr)], "rm%d" % t)
 
         stage[0] = "book"
-        cp(v("lsi"), p0(0, 8))
-        ts(v("lqi"), v("lsi"), 4, Op.arith_shift_right)
-        ts(v("lmi"), v("lsi"), 15, Op.bitwise_and)
-        cp(lq16, v("lqi"))
-        cp(v("lm16"), v("lmi"))
-        act(v("oh"), ind(v("miw"), v("lm16")))
+        ts(v("lqf"), v("lsf"), MAGIC, Op.add, MAGIC, Op.subtract)
+        ts(lq16, v("lqf"), 1 / 16, Op.mult, -1.0, Op.add)
+        if not last:
+            scat(v("gone%d" % t), lq16, v("ones", 0, 128))
+            tt(v("full", 0, nq), v("cnt", 0, nq), v("gone%d" % t, 0, nq), Op.is_gt)
+            count_full(nq, t + 1)
+        stage[0] = "live"
+        tt(v("lmf"), v("lsf"), v("lqf"), Op.subtract)
+        ts(v("lm16"), v("lmf"), 7.5, Op.add)
+        act(v("oh"), ind(v("r16"), v("lm16")))
         if not last:
             act(v("lgt"), ind(v("live"), lq16))
-            tt(v("lval", 0, 128), v("lgt"), v("oh"), Op.subtract)
-            scat(v("live"), v(lst), v("lval"))
-            count_full(nq)
+            tt(v("lval"), v("lgt"), v("oh"), Op.subtract)
+            scat(v("live"), lq16, v("lval"))
+            relu("v", v("own"), v(mf, 32 * r, 32 * r + 32))
+            scat(v("xg", 16 * nq, 16 * nq + 512), v("lrc"), v("own"))
         stage[0] = "copy"
         act(v("pg"), ind(v("postf"), lq16))
         tt(v("pgm"), v("pg"), v("oh"), Op.mult)
-        mm(p1(0, 32), v("bof"), v("pgm", 32 * r, 32 * r + 32), True, True)
-        for k in range(16):
-            mm(p1(32, 40), fam("e16f", k), v("pgm", k, 128, 16), k == 0, k == 15)
-        ts(v("ra"), v(mf, 32 * r, 32 * r + 32), 0.0, Op.is_lt, 8192.0, Op.mult)
-        tt(v("ownv"), v("ra"), p1(0, 32), Op.add)
-        cp(v("rl16"), p1(32, 40))
+        mm(p1(0, 32), v("bofn"), v("pgm", 32 * r, 32 * r + 32), True, True)
+        mms([(p1(128, 256), v("bof"), v("pgm"), True, False), (p1(128, 256), v("ident"), v("away"), False, True)])
+        tt(v("fa", 96, 128), v(mf, 32 * r, 32 * r + 32), p1(0, 32), Op.min)
+        scan(v("rlf"), v("rst", 0, 128), p1(128, 256), 0.0, Op.add, Op.max)
+        cp(v("rl16"), v("rlf", 15, 128, 16))
         scat(v("hh"), v("rl16"), v("vm"))
-        ts(v("hd"), v("hw"), -255.0, Op.add, N14, Op.mult)
+        mms([(p1(32 * k, 32 * k + 32), v("ident"), v("hw"), True, True) for k in range(3)])
+        ts(v("hd"), p1(0, 96), -255.0, Op.add, N14, Op.mult)
+        if t == 0:
+            stage[0] = "comp"
+            for i, q in enumerate(COMP):
+                a, b = 64 * i, min(P0, 64 * i + 64)
+                copy(q, v("ng", 16 * a, 16 * b), ind(v("x2", 0, R0), v("w16", a, b)))
+                ops[-1]["dep"].setdefault(mark[0], False)
+                in_turn("comp", q)
+            for k in (1, 2):
+                for c in range(4):
+                    a, b = 128 * c, min(P0, 128 * c + 128)
+                    pb = v("p%d" % (4 + (c + k) % 3), a, b)
+                    mms([(pb, fam("cw%d" % k, m), v("ng", 16 * a + m, 16 * b, 16), m == 0, m == 15) for m in range(16)])
+                    copy(CONST[11 + k], v("cmf%d" % k, a, b), pb)
+                    cp(v("cmu%d" % k, a, b), v("cmf%d" % k, a, b))
+        if t == 1:
+            absorb()
+        stage[0] = "copy"
+        for k in range(t + 1, RO):
+            act(v("cp%d" % k), ind(v("cmf%d" % k), pl16))
+            act(v("pgc", 0, 32), ind(v("cmf%d" % k), v(lst, 2 * r, 2 * r + 2)))
+            tt(v("cd"), v("pgc", 0, 32), v("pg", 32 * r, 32 * r + 32), Op.subtract)
+            tt(v("cd"), v("cd"), v("oh", 32 * r, 32 * r + 32), Op.mult)
+            mm(p1(0, 32), v("bof"), v("cd"), True, True)
+            tt(v("ce%d" % k), p1(0, 32), v("cp%d" % k), Op.subtract)
         if last:
             dma("y", (T.yh[0:16:2, :], []), (T["hh"][14:128:16, 0:R0], [("hh", 0, R0, 1)]), 1e5)
             dma("s", (T.yh[1:16:2, :], []), (T["hh"][15:128:16, 0:R0], [("hh", 0, R0, 1)]), 1e5)
             dma("y", (T.ypost[:, 0:nq], []), v("postf", 0, nq), 2.5e5)
-            ts(v("ya1", 0, 192), v("x1", R0, R0 + 192), CF, Op.mult)
-            ts(v("ya2", 0, 192), v("hh", R0, R0 + 192), N14, Op.mult)
+            times("s", v("ya1", 0, 192), v("x2", R0, R0 + 192), CF)
+            times("s", v("ya2", 0, 192), v("hh", R0, R0 + 192), N14)
             tt(v("ya3", 0, 192), v("ya1", 0, 192), v("ya2", 0, 192), Op.add)
             dma("s", (T.ya[:, 0:192], []), v("ya3", 0, 192), 5e4)
 
         stage[0] = "moves"
         if not last:
-            for b in ("x1", "x2"):
-                ts(v(b, R0 + 96 * t, R0 + 96 * t + 96), v(arr), 0.0, Op.max)
-            tt(v("wfa"), v(arr, 0, 32), v(arr, 32, 64), Op.max)
-            tt(v("wfb"), v(arr, 64, 96), v(mf, 32 * r, 32 * r + 32), Op.max)
-            tt(v("wfm"), v("wfa"), v("wfb"), Op.max)
-            tt(v("full", nq, nq + 32), v("wfm"), v("thr"), Op.is_ge)
+            mms([(p0(0, 32), v("bo64k"), v("go"), True, False), (p0(0, 32), v("ident"), v(mf, 32 * r, 32 * r + 32), False, False)])
+            mms([(p0(0, 32), v("ident"), v(arr, 32 * k, 32 * k + 32), False, k == 2) for k in range(3)])
+            ts(v("full", nq, nq + 32), p0(0, 32), 13 * 65536.0 - 28000, Op.is_ge)
+            for b in ("x1", "x2")[t:]:
+                relu(MISC[4], v(b, R0 + 96 * t, R0 + 96 * t + 96), v(arr))
+        tt(v("fa", 0, 96), v(arr), v("atab%d" % t), Op.min)
+        tt(v("wc"), v("fa", 0, 64), v("fa", 64, 128), Op.max)
+        tt(v("wv"), v("wc", 0, 32), v("wc", 32, 64), Op.max)
         stage[0] = "win"
-        ts(v("fb"), v(arr), 0.0, Op.is_lt, 8192.0, Op.mult)
-        tt(v("fa"), v("fb"), v("atab%d" % t), Op.add)
-        tt(v("wc"), v("fa", 0, 32), v("ownv"), Op.min)
-        tt(v("wb"), v("fa", 32, 64), v("fa", 64, 96), Op.min)
-        tt(v("wv"), v("wc"), v("wb"), Op.min)
-        ts(v("wf"), v("wv"), 8191.5, Op.is_lt)
-        tt(v("rwf"), v("rw"), v("wf"), Op.mult)
-        tt(v("wd"), v("wv"), v("postp"), Op.subtract)
+        tt(v("rwf"), v("wv"), v("rwt"), Op.is_ge)
+        tt(v("wd"), v("wv"), v("postp"), Op.add)
         tt(v("we"), v("wd"), v("rwf"), Op.mult)
-        tt(v("postf", nq, nq + 32), v("we"), v("postp"), Op.add)
-        for k in range(3):
-            tt(v("eq", 32 * k, 32 * k + 32), v("atab%d" % t, 32 * k, 32 * k + 32), v("wv"), Op.is_equal)
-        for k in range(3):
-            tt(v("eh", 32 * k, 32 * k + 32), v("eq", 32 * k, 32 * k + 32), v("hd"), Op.mult)
+        tt(v("postf", nq, nq + 32), v("postp"), v("we"), Op.subtract)
+        for k in range(t + 1, RO):
+            tt(v("cs1"), v("ce%d" % k), v("wv"), Op.subtract)
+            tt(v("cu"), v("cs1"), v("rwf"), Op.mult)
+            tt(v("cmf%d" % k, nq, nq + 32), v("cu"), v("cp%d" % k), Op.add)
+            cp(v("cmu%d" % k, nq, nq + 32), v("cmf%d" % k, nq, nq + 32))
+        if last:
+            for k in range(0, 96, 32):
+                tt(v("eq", k, k + 32), v("atab%d" % t, k, k + 32), v("wv"), Op.is_equal)
+        else:
+            mms([(p1(32 * k, 32 * k + 32), v("identf"), v("wv"), True, True) for k in range(3)])
+            tt(v("eq"), v("atab%d" % t), p1(0, 96), Op.is_equal)
+        tt(v("eh"), v("eq"), v("hd"), Op.mult)
         if not last:
             tt(v("live", nq, nq + 32), v("go"), v("rwf"), Op.add)
             cp(v("post16", nq, nq + 32), v("postf", nq, nq + 32))

import numpy as np
from concourse.bass import DstId, RemoteDMATransfer
from concourse.mybir import AluOpType as Op, AxisListType as Ax, ActivationFunctionType as Fn

R0, P0, SP, RO = 6144, 416, 32, 3
R = R0 + 96 * RO
PD = 512
MD = 544
WP = 672
XW = 16 * WP
TS = 544
BIG = 262144.0
MAGIC = 1.5 * 2 ** 27
HOME = "vsvsssv"
COMP = "sssvsss"
SLOT = ["sssvsss", "ssvvvvvv", "sssvsvvv"]
NEAR = ["svsvsss", "sssssss", "svssssss"]
HELP = [7, 12]
EARLY = 6
FOLD = [0, 0, 3, 0]
XSQ = "vss"
MAB = ["vvv", "vss"]
LOADS = "post rec0 homes rec1 rec2 ab0 near xd0 xd1 xd2 ab ctr"
TBQ = "vv"
RELU, BTQ, TQQ = "ssvv", "ssvv", "vvsv"
FULLQ = "svs"
MISC = "vvvvv"
CONST = "ssssvssvvvvvsv"
PARTS = [[[0, 1], [2, 3]]] * 3
ORDER = ("moves list rows split tab first0 bt0 first1 bt1 first2 bt2 first3 bt3 dist0 offer0 dist1 offer1 dist2 offer2 "
         "dist3 offer3 book").split()
URGENT = ("moves", "list", "split", "rows", "tab", "first0", "first1", "bt0", "bt1", "offer1")
CYCLE, GATHER, SCATTER = np.array([[0.00095, 1.6, 3.7], [0.0012, 1.15, 4.5], [0.00087, 2.0, 3.0]]).T
SLOW = dict(zip("pgrd", np.array([[1.0, 1.1, 1.0, 1.15], [1.0, 1.2, 1.25, 1.0], [1.3, 1.1, 0.85, 1.6]]).T))
WAKE, LOOK = 0.18, 0.3
FIXED = {"v": 0.0, "s": 0.15, "p": 0.0, "g": 0.15}
START, RATE, ISSUE = 1.8, 3e5, 0.6
HOP = {"rp": 5.7, "rb": 4.7, "rm": 4.2}
FRATE, FLAG = 1.2e5, 8.0
QUEUES, TRIES, SEED, SLACK = "vspgydfr", 3500, 1, 2e-5

SCRATCH = {}
ALIAS = {}
ORDERS = {}
OWN = ("plr", "pls", "bw", "mf", "arr", "p0", "p1", "p2", "p3", "p4", "p5", "p6", "p7")


def _b(names, w, dt="bfloat16", where="sbuf"):
    for name in names.split():
        if w > 256 or name.startswith(OWN):
            SCRATCH[name] = (where, [128, w], dt)
        else:
            pool = "small_" + dt
            o = SCRATCH.get(pool, ("", [0, 0]))[1][1]
            ALIAS[name] = (pool, o, w)
            SCRATCH[pool] = ("sbuf", [128, o + (w + 15) // 16 * 16], dt)


F, I, U = "float32", "int32", "uint16"
_b("x1 x2", R)
_b("hh", R + 512)
_b("xd", R0)
_b("xg", XW)
_b("ng mc md", 16 * 480)
_b("nm", 2048)
_b("e16 rmp rmn rx hm em zi cw1 cw2", 144)
_b("postI nearI nsh", P0, I)
_b("abI", 1152, I)
_b("ab16", 768, U)
_b("abh", 1536)
_b("post16 near16 cmu1 cmu2 w16", 512, U)
_b("postf nearf cmf1 cmf2", WP, F)
_b("slot pm h16", P0, F)
_b("ctr live gone0 gone1", WP)
for _t in range(RO):
    _b("tab%d" % _t, 4 * TS)
    _b("plr%d" % _t, 6, U)
    _b("pls%d" % _t, 2, U)
    _b("lst%d" % _t, 10, U)
    _b("bw%d" % _t, 144)
    _b("mf%d" % _t, 128)
    _b("arr%d" % _t, 96)
    _b("atab%d" % _t, 96, F)
    _b("vst%d" % _t, 512)
_b("full scan sd1 junk0 junk1", TS)
_b("cnt", 480)
_b("cm0 cm1", 130, F)
_b("ident ibig d14 d15 bo bo14p bo14n px dcp cg n15 ck w128 wa128 wb128 wc128 bou nsp vm oh lgt dat away lval", 128)
_b("bo64k nident", 128)
_b("bof bofn pg pgc pgm identf d384 dneg rlf fa", 128, F)
_b("lg", 1024)
_b("ones n15r cka ckb rst", 256)
_b("kt", 512, F)
_b("wt ff xs ma mb vhi vlo bt tb0 tb1 tq0", 512)
_b("tq1", 528)
_b("fc kn", 32, F)
_b("cidx i32k i32 tr whi postp nearp ktk kts spa spb spc wv wd we rwt cp1 cp2 ce1 ce2 cd cs1 cu", 32, F)
_b("wc", 64, F)
_b("sd2 sd3 lp oa obt ob go nog rw rwf ac hw stay own", 32)
_b("g8 rgp rgn kd", 8)
_b("pcol", 2, I)
_b("r16 wk wl", 16, F)
_b("k5", 5, F)
_b("h4", 4, F)
_b("i8 ms lsf lqf lmf", 8, F)
_b("acc", 2, F)
_b("lac lbc lrc", 2, U)
_b("ps16 cps16 spl16 tgl", 32, U)
_b("ls16 lm16 rl16", 8, U)
_b("eq eh hd", 96)
_b("ya1 ya2 ya3", 288)
for _i in range(8):
    _b("p%d" % _i, *((1024, "bfloat16") if _i in (2, 3, 7) else (512, F)), "psum")


def runs(places, most):
    out = []
    for i in places:
        if out and out[-1][-1] == i - 1 and len(out[-1]) < most:
            out[-1].append(i)
        else:
            out.append([i])
    return out


def folds():
    out = []
    for t in range(RO):
        if t and FOLD[2 * t - 1]:
            ne = P0 + SP * (t - 1)
            out += [("xg", 1024 * x[0], min(16 * ne, 1024 * x[-1] + 1024))
                    for x in runs([i for i in range(7) if SLOT[t][i] == "s"], FOLD[2 * t - 1])]
        if t < 2 and FOLD[2 * t]:
            out += [("x%d" % (t + 1), 512 * x[0], 512 * x[-1] + 512) for x in runs(range(12 - HELP[t], EARLY if t else 12), FOLD[2 * t])]
    return out


NDMA = 28
SEMAPHORES = ["qv", "qs", "qp", "qg", "sent"] + ["f%d" % i for i in range(30)] + ["d%d" % i for i in range(NDMA)] + \
    ["%s%d" % (a, t) for a in ("rp", "rb", "rm") for t in range(RO)]


def helper(core, T, topo):
    return [c for c in topo.cores_of(core) if c != core and topo.die(c) == topo.die(core) and T.rank_of(c) is None][-1]


def hand_back(g, core, T, topo):
    for to in T.cores:
        if helper(to, T, topo) == core and folds():
            rid, pid, _ = topo.addr(to)
            n = len(topo.engines(core, to))
            for i, (b, c0, c1) in enumerate(folds()):
                g.wait_ge(T.sem["f%d" % i], n // 2)
                g.remote_dma(T[b][:, c0:c1], T[b][:, c0:c1], T.sem["f%d" % i], T.sem["sent"], pid, rid, topo.mask(core, to))
            g.wait_ge(T.sem["sent"], n * len(folds()))


def edges(ops, far=1.0):
    before = [[(d, ops[d]["lag"] * (far if o["q"] == "r" else 1.0) if o["q"] in "dfr" and w else WAKE if w else 0.0)
               for d, w in o["dep"].items()] for o in ops]
    behind = [[] for _ in ops]
    for i, b in enumerate(before):
        for d, gap in b:
            behind[d].append((i, gap))
    return before, behind


def lay(time, queue, turn, follows, end=None, fixed=0):
    end = list(end) if end else [0.0] * len(time)
    busy = {q: ([], []) for q in QUEUES}
    for i in turn[:fixed]:
        busy[queue[i]][0].append(end[i] - time[i])
        busy[queue[i]][1].append(end[i])
    for i in turn[fixed:]:
        at = 0.0
        for d, gap in follows[i]:
            if end[d] + gap > at:
                at = end[d] + gap
        s, e = busy[queue[i]]
        lo = len(e)
        while lo and e[lo - 1] > at:
            lo -= 1
        while lo < len(s) and s[lo] < at + time[i]:
            at = max(at, e[lo])
            lo += 1
        s.insert(lo, at)
        e.insert(lo, at + time[i])
        end[i] = at + time[i]
    return end


def play(time, queue, turn, follows):
    end, why, prev = [0.0] * len(time), [-1] * len(time), [-1] * len(time)
    last = dict.fromkeys(QUEUES, -1)
    for i in turn:
        w = prev[i] = last[queue[i]]
        at = end[w] if w >= 0 else 0.0
        for d, gap in follows[i]:
            if end[d] + gap > at:
                at, w = end[d] + gap, d
        end[i], why[i], last[queue[i]] = at + time[i], w, i
    return end, why, prev


def arrange(ops):
    n = len(ops)
    before, behind = edges(ops)
    times = np.array([o["time"] * np.ones(len(CYCLE)) for o in ops]).T.tolist()
    time, queue = times[0], [o["q"] for o in ops]
    key = [999] * n
    for i in range(n - 1, -1, -1):
        step, t = ops[i]["at"]
        key[i] = min([100 * t + (ORDER.index(step) if step in ORDER else 99)] + [key[j] for j, gap in behind[i]])
    left = [len(b) for b in before]
    ready = [0.0] * n
    free = {q: 0.0 for q in QUEUES}
    cand = {q: [i for i in range(n) if queue[i] == q and not left[i]] for q in free}
    soon = [LOOK if o["at"][0] in URGENT else 0.0 for o in ops]
    turn = []
    while len(turn) < n:
        t0, q = min((max(free[q], min(ready[i] for i in c)), q) for q, c in cand.items() if c)
        i = min((key[i], i) for i in cand[q] if ready[i] <= t0 + soon[i])[1]
        cand[q].remove(i)
        turn.append(i)
        free[q] = max(t0, ready[i]) + time[i]
        for j, gap in behind[i]:
            ready[j] = max(ready[j], free[q] + gap)
            left[j] -= 1
            if not left[j]:
                cand[queue[j]].append(j)

    def settle(turn, back, end=None, fixed=0):
        end = lay(time, queue, turn, before, end, fixed)
        turn = sorted(turn, key=lambda i: end[i] - time[i])
        if back:
            late = lay(time, queue, sorted(turn[::-1], key=lambda i: -end[i]), behind)
            return settle(sorted(turn, key=lambda i: -late[i]), False)
        return turn, end

    def value(turn):
        out = [play(x, queue, turn, b) for x, b in zip(times, befores)]
        return sum(max(o[0]) / z for o, z in zip(out, scale)), out

    befores = [edges(ops, float(x))[0] for x in SLOW["r"]]
    turn, end = settle(turn, True)
    scale = [sum(x[i] for i in range(n) if queue[i] in "vs") for x in times]
    best, out = value(turn)
    seed = [SEED]

    def draw(k):
        seed[0] = (seed[0] * 1103515245 + 12345) % 2 ** 31
        return (seed[0] >> 8) % k

    for k in range(TRIES):
        e, why, prev = out[draw(len(out))]
        chain = [max(range(n), key=lambda i: e[i])]
        while why[chain[-1]] >= 0:
            chain.append(why[chain[-1]])
        a, by = draw(len(chain)), (0.3, 1, 2, 4, 8)[draw(5)]
        kind = draw(4)
        some = chain[a:a + (1, 1, 3, 10, 30)[draw(5)]]
        if kind % 2:
            some, by = [prev[i] for i in some if prev[i] == why[i] >= 0], -by
        if kind > 1 and some:
            some = [i for i in range(n) if ops[i]["at"] == ops[some[0]]["at"] and queue[i] == queue[some[0]]]
        if not some:
            continue
        key = [end[i] - time[i] for i in range(n)]
        first = min(key[i] for i in some)
        for i in some:
            key[i] -= by
        for i in (turn[::-1] if by > 0 else turn):
            for j, gap in (before if by > 0 else behind)[i]:
                if (key[j] - key[i]) * by >= 0:
                    key[j] = key[i] - 1e-6 * by
                    first = min(first, end[j] - time[j])
        first -= max(by, 0) + 0.01
        fixed = 0
        while end[turn[fixed]] - time[turn[fixed]] < first:
            fixed += 1
        new, en = settle(turn[:fixed] + sorted(turn[fixed:], key=lambda i: key[i]), draw(3) == 0, end, fixed)
        val, o = value(new)
        if val <= best + SLACK * draw(100) * (1 - k / TRIES):
            turn, end, best, out = new, en, val, o
    return turn, max(end)


def rank_program(g, core, T, topo):
    r = T.rank_of(core)
    if r is None:
        return hand_back(g, core, T, topo)
    Q = {"v": g.vector, "s": g.scalar, "p": g.tensor, "g": g, "y": g.sync}
    ops = []
    acc = {}
    dn = [0]
    line = {}
    put_off = {}
    mark = [0]
    stage = ["", 0]

    def meet(a, b):
        if a[0] >= b[1] or b[0] >= a[1]:
            return False
        return a[2] == 1 or a[2] != b[2] or (a[0] - b[0]) % a[2] == 0

    def note(q, fn, time, lag, reads, writes, adds=False, after=(), sem=None, mine=0):
        me = len(ops)
        dep = {d: True for d in after}
        for is_w, regs in ((False, reads), (True, writes)):
            for reg in regs:
                ps = SCRATCH[reg[0]][0] == "psum"
                for (o, w2, d, adds2) in acc.get(reg[0], ()):
                    if ps:
                        if ops[d]["q"] != q:
                            dep[d] = True
                        elif q == "p":
                            if not (adds and adds2):
                                dep.setdefault(d, False)
                        elif is_w or w2:
                            dep[d] = True
                    elif (is_w or w2) and meet(reg[1:], o):
                        dep[d] = True
        ops.append({"q": q, "fn": fn, "time": time, "lag": lag, "dep": dep, "sem": sem, "at": tuple(stage)})
        for reg in writes:
            ps = SCRATCH[reg[0]][0] == "psum"
            old = acc.get(reg[0], [])
            if not adds:
                old = [o for o in old if not (ps or (reg[3] == 1 and reg[1] <= o[0][0] and o[0][1] <= reg[2]) or reg[1:] == o[0])]
            acc[reg[0]] = old + [(reg[1:], True, me + mine, adds)]
        for reg in reads:
            acc.setdefault(reg[0], []).append((reg[1:], False, me + mine, False))
        return me

    def run(q, fn, cycles, reads, writes, adds=False):
        note(q, fn, (cycles * CYCLE + FIXED[q]) * SLOW.get(q, 1.0), 0.0, reads, writes, adds)

    def in_turn(*kind):
        if kind in line:
            ops[-1]["dep"].setdefault(line[kind], False)
        line[kind] = len(ops) - 1

    def together(first):
        some = ops[first:]
        del ops[first:]
        dep = {}
        for o in some:
            for d, w in o["dep"].items():
                if d < first:
                    dep[d] = dep.get(d, False) or w
        ops.append(dict(some[0], fn=lambda: [o["fn"]() for o in some], time=sum(o["time"] for o in some), dep=dep))
        for b in acc:
            acc[b] = [x if x[2] < first else x[:2] + (first,) + x[3:] for x in acc[b]]

    def dma(q, out, in_, nbytes, next_=False):
        sem = "d%d" % dn[0]
        dn[0] += 1
        me = note(q, lambda: Q[q].dma_start(out[0], in_[0]).then_inc(T.sem[sem], 16), 0.1, START, in_[1], out[1], sem=(sem, 0), mine=1)
        note("d", None, nbytes / RATE * SLOW.get("d", 1.0), 0.0, [], [], after=[me], sem=(sem, 16))
        if next_:
            ops[me]["dep"][me - 2] = False
            ops[me + 1]["dep"][me - 1] = False

    def emit():
        cnt = {}
        known = {q: {} for q in Q}
        tok = {}
        form = tuple((o["q"], o["at"], tuple(sorted(o["dep"].items()))) for o in ops)
        if form not in ORDERS:
            ORDERS[form] = arrange(ops)[0]
        for i in ORDERS[form]:
            o = ops[i]
            q = o["q"]
            if q == "f":
                continue
            if q in "dr":
                tok[i] = (o["sem"][0], o["sem"][1], {})
                cnt[o["sem"][0]] = o["sem"][1]
                continue
            need = {}
            for d, w in o["dep"].items():
                if w and known[q].get(tok[d][0], 0) < tok[d][1] and need.get(tok[d][0], ("", 0))[1] < tok[d][1]:
                    need[tok[d][0]] = tok[d]
            for tk in need.values():
                if not any(x is not tk and x[2].get(tk[0], 0) >= tk[1] for x in need.values()):
                    Q[q].wait_ge(T.sem[tk[0]], tk[1])
            for tk in need.values():
                for s2, v2 in list(tk[2].items()) + [tk[:2]]:
                    known[q][s2] = max(known[q].get(s2, 0), v2)
            if o["sem"] is None:
                sem = "q" + q
                made = o["fn"]()
                for x in made if isinstance(made, list) else [made]:
                    x.then_inc(T.sem[sem], 1)
                    cnt[sem] = cnt.get(sem, 0) + 1
            else:
                o["fn"]()
                sem = o["sem"][0]
                cnt[sem] = cnt.get(sem, 0) + o["sem"][1]
            tok[i] = (sem, cnt[sem], dict(known[q]))
        for sem, val in cnt.items():
            g.wait_ge(T.sem[sem], val)

    def v(b, c0=0, c1=None, s=1, n=128):
        if b in ALIAS:
            b, o, w = ALIAS[b]
            c0, c1 = o + c0, o + (w if c1 is None else c1)
        c1 = SCRATCH[b][1][1] if c1 is None else c1
        kind = "two" if SCRATCH[b][2] in (U, "bfloat16") else "four"
        return (T[b][0:n, c0:c1] if s == 1 else T[b][0:n, c0:c1:s], [(b, c0, c1, s)], len(range(c0, c1, s)), kind)

    def ind(win, off):
        return (win[0].indirect(off[0]), win[1] + off[1], 16 * off[2], "ind")

    def col(i):
        return v("fc", i, i + 1)

    def fam(b, m):
        return v(b, 15 - m, 143 - m)

    def blk(b, m):
        return v(b, 128 * m, 128 * m + 128)

    def cyc(out, a):
        return 60 + a[2] * GATHER if a[3] == "ind" else max(64, a[2] * (0.5 if out[3] == a[3] == "two" else 1))

    def tt(out, a, b, op):
        psum = any(SCRATCH[x[1][0][0]][0] == "psum" for x in (a, b))
        c = cyc(out, a) if a[3] == "ind" else max(64, a[2] * (1 if psum else 2) * (0.5 if out[3] == a[3] == b[3] == "two" else 1))
        run("v", lambda: g.vector.tensor_tensor(out[0], a[0], b[0], op), c, a[1] + b[1], out[1])

    def ts(out, a, s1, o1, s2=None, o2=None):
        regs = list(a[1])
        x1, x2 = s1, s2
        if isinstance(s1, tuple):
            regs += s1[1]
            x1 = s1[0]
        if isinstance(s2, tuple):
            regs += s2[1]
            x2 = s2[0]
        if o2 is None:
            run("v", lambda: g.vector.tensor_scalar(out[0], a[0], x1, None, o1), cyc(out, a), regs, out[1])
        else:
            run("v", lambda: g.vector.tensor_scalar(out[0], a[0], x1, x2, o1, o2), cyc(out, a), regs, out[1])

    def cp(out, a):
        run("v", lambda: g.vector.tensor_copy(out[0], a[0]), cyc(out, a), a[1], out[1])

    def scat(win, off, a):
        run("v", lambda: g.vector.tensor_copy(win[0].indirect(off[0]), a[0]), np.maximum(64, SCATTER * a[2]), a[1] + off[1], win[1])

    def red(out, a, op, ab=False):
        kw = {"apply_absolute_value": True} if ab else {}
        run("v", lambda: g.vector.tensor_reduce(out[0], a[0], Ax.X, op, **kw), max(64, a[2]), a[1], out[1])

    def scan(out, a, b, init, o0, o1):
        regs = a[1] + b[1] + (init[1] if isinstance(init, tuple) else [])
        x = init[0] if isinstance(init, tuple) else init
        run("v", lambda: g.vector.tensor_tensor_scan(out[0], a[0], b[0], x, o0, o1), cyc(out, b), regs, out[1])

    def tr(out, a):
        run("v", lambda: g.vector.transpose(out[0], a[0]), 64, a[1], out[1])

    def fill(out, c):
        run("v", lambda: g.vector.memset(out[0], c), cyc(out, out), [], out[1])

    def act(out, a, fn=Fn.Copy, bias=None, scale=None, accum=None):
        kw = {}
        regs = list(a[1])
        w = list(out[1])
        if bias is not None:
            kw["bias"] = bias[0]
            regs += bias[1]
        if isinstance(scale, tuple):
            kw["scale"] = scale[0]
            regs += scale[1]
        elif scale is not None:
            kw["scale"] = scale
        if accum is not None:
            kw["accum_out"] = accum[0]
            w += accum[1]
        run("s", lambda: g.scalar.activation(out[0], a[0], fn, **kw), a[2] * GATHER - 100 if a[3] == "ind" else a[2], regs, w)

    def times(q, out, a, w):
        if q == "v":
            ts(out, a, w, Op.mult)
        else:
            act(out, a, scale=w)

    def relu(q, out, a):
        if q == "v":
            ts(out, a, 0.0, Op.max)
        else:
            act(out, a, Fn.Relu)

    def copy(q, out, a):
        (cp if q == "v" else act)(out, a)

    def mms(calls):
        c = sum(max(min(64, a[2]), b[2]) * (2 if b[3] == "four" else 0.5) for o, a, b, s, e in calls)
        run("p", lambda: [g.tensor.matmul(o[0], a[0], b[0], s, e) for o, a, b, s, e in calls], c,
            [reg for x in calls for reg in x[1][1] + x[2][1]], [reg for x in calls for reg in x[0][1]],
            not any(x[3] or x[4] for x in calls))

    def mm(*call):
        mms([call])

    def turn(out, a, ident):
        run("p", lambda: g.tensor.transpose(out[0], a[0], ident[0]), 0.5 * max(64, out[2]), a[1] + ident[1], out[1])

    def iota(out, pat, base=0, cm=0, flag=True):
        kw = {"allow_small_or_imprecise_dtypes": True} if flag else {}
        run("g", lambda: g.iota(out[0], pat, base, cm, **kw), 2 * out[2], [], out[1])
        if stage[0] == "const":
            in_turn("small")
        else:
            ops[-1]["dep"].setdefault(line[("small",)], False)

    def keep(out, pat, base, cm):
        run("g", lambda: g.affine_select(out[0], out[0], pat, Op.is_ge, 0.0, base, cm), 2 * out[2], out[1], out[1])

    others = [q for q in range(len(T.cores)) if q != r]
    NE = 2

    def send(bufs, dsts, lands, sem):
        trs = []
        for i, q in enumerate(others):
            rid, pid, _ = topo.addr(T.cores[q])
            eng = topo.engines(core, T.cores[q])[NE * i:NE * i + NE]
            trs.append(RemoteDMATransfer(dst_ids=[DstId(rid=rid, pnc=pid)], dma_engine_mask=sum(1 << e for e in eng),
                                         remote_sem=T.sem[sem], srcs=[bufs[i][0]], dsts=[dsts[i][0]]))
        n = NE * len(others)
        me = note("g", lambda: g.remote_dma_fused(trs, local_sem=T.sem["sent"]), ISSUE + (2.0 if sem == "rp0" else 0.0),
                  HOP[sem[:2]], [reg for b in bufs for reg in b[1]], [], sem=("sent", n))
        note("r", None, 0.001, 0.0, [], [reg for x in lands for reg in x[1]], after=[me], sem=(sem, n))
        line[sem] = me
        for i in put_off.get(sem, ()):
            ops[i]["dep"][me] = False

    todo = list(enumerate(folds()))

    def fold(other):
        i, piece = todo.pop(0)
        out, a = v(*piece), v(other, *piece[1:])
        to = helper(core, T, topo)
        rid, pid, _ = topo.addr(to)
        eng = topo.engines(core, to)
        one = RemoteDMATransfer(dst_ids=[DstId(rid=rid, pnc=pid)], dma_engine_mask=sum(1 << e for e in eng[len(eng) // 2:]),
                                remote_sem=T.sem["f%d" % i], srcs=[out[0], a[0]], dsts=[out[0]], alu_op=2)
        me = note("g", lambda: g.remote_dma_fused([one], local_sem=T.sem["sent"]), ISSUE, START, a[1], out[1],
                  sem=("sent", len(eng) // 2), mine=2)
        in_turn("fold")
        ops[me]["dep"].setdefault(line["rb%d" % stage[1]], False)
        note("f", None, 256 * out[2] / FRATE, FLAG + (0.0 if i else 3.0), [], [], after=[me])
        in_turn("bytes")
        note("r", None, 0.001, 0.0, [], [], after=[me + 1], sem=("f%d" % i, len(eng)))
        in_turn("back")

    def place(q):
        return r - (1 if r > q else 0)

    third = R0 // 3
    stage[0] = "home"
    fill(v("x2", 0, 768), 0.0)
    fill(v("x2", 768, 4608), 0.0)
    for a in (4608, 5376):
        act(v("x2", a, a + 768), v("x2", 0, 768))
    stage[0] = ""
    loads = {"post": [(v("postI"), T.post[:, :], 2e5)], "near": [(v("nearI"), T.near[:, :], 2e5)],
             "ab0": [(v("abI", 0, 384), T.absorb[:, 0:384], 2e5)], "ab": [(v("abI", 384, 1152), T.absorb[:, 384:1152], 4e5)],
             "ctr": [(v("ctr", 0, P0), T.cen[:, :], 1e5)],
             "homes": [((T["x2"][i:128:16, 0:R0], [("x2", i - 14, R0, 2)]), T.rec[i:128:16, :], 1e5) for i in (14, 15)]}
    for i in range(3):
        a, b = third * i, third * i + third
        loads["rec%d" % i] = [(v("hh", a, b), T.rec[:, a:b], 5e5)]
        b = min(b, R0 - 512 * HELP[0])
        loads["xd%d" % i] = [(v("xd", a, b), T.rec[:, a:b], 256 * (b - a))] if b > a else []
    for i, (out, in_, size) in enumerate(x for name in LOADS.split() for x in loads[name]):
        dma("y", out, (in_, []), size, i > 0)

    pI, p15 = v("pcol", 0, 1), v("pcol", 1, 2)
    PF, MF_, PB = col(0), col(1), col(2)
    stage[0] = "const"
    iota(pI, [[0, 1]], 0, 1, False)
    iota(PF, [[0, 1]], 0, 1)
    iota(v("i32"), [[1, 32]])
    iota(v("k5"), [[-16, 5]], 32)
    iota(v("h4"), [[512, 2], [16, 2]])
    iota(v("i8"), [[16, 8]])
    iota(v("zi"), [[1, 144]], -15)
    iota(v("cg"), [[16, 8], [0, 16]])
    iota(v("dcp"), [[1, 128]], 0, -1)
    iota(v("n15"), [[0, 8], [1, 16]])
    iota(v("cidx"), [[1, 32]], PD + 1)
    iota(v("w128"), [[-1, 128]], 128)
    iota(v("whi"), [[128, 4], [0, 8]])
    iota(v("i32k"), [[16, 32]])
    iota(v("n15r"), [[0, 16], [-1, 16]], 15)
    iota(v("slot"), [[16, P0]])
    stage[0] = ""
    for b, a, e in (("hh", R0, R), ("live", P0, WP), ("full", P0, TS), ("wk", 0, 16)):
        iota(v(b, a, e), [[0, e - a]])
    iota(v("ones"), [[0, 256]], 1)
    iota(col(31), [[0, 1]], -13)
    for i, w in ((0, 32768), (1, 1), (2, -256), (3, -16), (4, -32768 * 128), (5, -16), (7, 2 ** 23), (12, 32768), (14, 16)):
        iota(v("wk", i, i + 1), [[0, 1]], w)
    for b in ("postf", "cmf1", "cmf2"):
        iota(v(b, MD, WP), [[1, 128]], R)
        iota(v(b, PD, MD), [[0, 32]])
    iota(v("lg"), [[16, 8], [0, 8], [1, 16]])
    iota(v("vhi"), [[1, 2], [0, 256]], 26)
    iota(v("vlo"), [[0, 2], [1, 256]])
    for k in range(RO):
        first = len(ops)
        iota(v("bw%d" % k, 128, 144), [[0, 16]], 8192)
        for q in range(4):
            iota(v("tab%d" % k, TS * q, TS * q + TS), [[0, TS]])
        put_off.setdefault("rb%d" % (k - 1), []).extend(range(first, len(ops)))
        first = len(ops)
        iota(v("atab%d" % k), [[-1, 96]], -R0 - 96 * k)
        if k < RO - 1:
            iota(v("gone%d" % k), [[0, WP]])
        put_off.setdefault("rb%d" % k, []).extend(range(first, len(ops)))
    iota(v("vm"), [[0, 128]], 255)
    iota(v("sd1", 0, PD), [[0, PD]])
    iota(v("wt"), [[0, 512]])
    for k in (4, 5):
        iota(v("wt", k, 512, 16), [[0, 32]], 1)
    iota(v("xg", 16 * MD, XW, 16), [[0, 128]], -8192)
    for b, a, e in (("x1", R0, R), ("x2", R0, R), ("ff", P0, 512), ("nearf", P0, WP), ("ctr", P0, WP)):
        iota(v(b, a, e), [[0, e - a]])
    stage[0] = "const"
    ts(p15, pI, 15, Op.bitwise_and)
    cp(MF_, p15)
    tt(PB, PF, MF_, Op.subtract)
    ts(v("r16"), v("i32", 0, 16), MF_, Op.is_equal)

    def row(i):
        return v("r16", i, i + 1)

    C14, C15, N14, CF, N255 = row(14), row(15), col(3), col(4), col(5)
    ts(CF, MF_, 13.5, Op.is_le)
    ts(N14, MF_, 13.5, Op.is_gt)
    ts(N255, MF_, 13.5, Op.is_gt, 255.0, Op.mult)
    ts(col(6), C14, 256.0, Op.mult, C15, Op.add)
    ts(v("fc", 8, 13), v("k5"), CF, Op.mult)
    K32, K16c, KN16, KN32 = col(8), col(9), col(11), col(12)
    ts(v("fc", 16, 20), v("h4"), MF_, Op.add, 0.5, Op.add)
    HB = (col(16), col(17))
    ts(v("e16"), v("zi"), PB, Op.is_equal)
    ts(v("hm"), v("zi"), PB, Op.is_equal, col(6), Op.mult)
    for b, w in (("em", MF_), ("rx", KN16), ("rmp", K32), ("rmn", KN32)):
        act(v(b), v("e16"), scale=w)
    cp(v("post16", 0, P0), v("postI"))
    cp(v("postf", 0, P0), v("postI"))
    act(v("slot"), v("slot"), Fn.Identity, bias=MF_)
    ts(col(20), row(1), -256.0, Op.mult, row(0), Op.add)
    ts(col(21), row(1), -256.0, Op.mult)
    ts(v("bo"), v("cg"), PB, Op.is_equal)
    for q, b, w in zip(CONST, ("nsp", "bo14p", "bo14n", "bof", "bofn"), (col(21), K16c, KN16, 1.0, -1.0)):
        times(q, v(b), v("bo"), w)
    ts(v("g8"), v("i8"), PB, Op.is_equal)
    ts(v("bo64k"), v("bo"), 65536.0, Op.mult)
    ts(v("nident"), v("dcp"), 0.0, Op.is_equal, -1.0, Op.mult)
    for b, w in (("rgp", K32), ("rgn", KN32)):
        ts(v(b), v("i8"), PB, Op.is_equal, w, Op.mult)
    ts(v("wc128"), v("n15"), row(0), Op.add)
    tt(v("bou"), v("wc128"), v("bo"), Op.mult)
    for j in range(16):
        ts(blk("nm", j), v("bou"), float(j), Op.is_gt, col(20), Op.mult)
        if j % 4 == 3:
            together(len(ops) - 4)
    for h in range(2):
        tt(v("wl", 8 * h, 8 * h + 8), v("wk", 8 * h, 8 * h + 8), v("r16", 0, 8), Op.mult)
        red(col(22 + h), v("wl", 8 * h, 8 * h + 8), Op.add)
    stage[0] = "late"
    ts(v("lg"), v("lg"), col(23), Op.mult, col(22), Op.add)
    keep(v("lg"), [[0, 8], [-16, 8], [0, 16]], 0, 1)
    keep(v("lg"), [[0, 8], [16, 8], [0, 16]], 15, -1)
    stage[0] = "const"
    ts(v("sd2"), v("cidx"), col(18), Op.is_ge, 16.0, Op.mult)
    ts(v("sd3"), v("cidx"), col(19), Op.is_ge, 84.0, Op.mult)
    tt(v("sd1", PD, TS), v("sd2"), v("sd3"), Op.add)
    for b, w in (("ident", 1.0), ("ibig", BIG)):
        ts(v(b), v("dcp"), 0.0, Op.is_equal, w, Op.mult)
    for q, b, w in zip(CONST[5:], ("d14", "d15", "identf", "d384", "dneg"), (C14, C15, 1.0, 384.0, -6143 / 16)):
        times(q, v(b), v("ident"), w)
    ts(v("wa128"), v("dcp"), 0.0, Op.is_gt, -32.0, Op.mult)
    tt(v("wb128"), v("wa128"), v("bo"), Op.mult)
    tt(v("px"), v("wb128"), v("ident"), Op.add)
    ts(v("away"), v("n15"), MF_, Op.not_equal, -BIG, Op.mult)
    ts(v("kd", 0, 2), v("h4", 0, 2), MF_, Op.add, 16.0, Op.mult)
    ts(v("dat"), v("w128"), row(0), Op.mult, row(1), Op.add)
    ts(v("ckb"), v("n15r"), -7.5, Op.add, v("ident", 1, 2), Op.mult)
    ts(v("cka"), v("ones", 0, 256), v("ibig", 0, 1), Op.mult, -1.0, Op.mult)
    ts(v("ck"), v("n15r", 0, 128), v("ident", 1, 2), Op.mult, v("ibig", 0, 1), Op.subtract)
    ts(v("rst"), v("n15r"), 15.0, Op.is_equal, -2.0 ** 22, Op.mult)
    ts(v("nsh"), v("nearI"), 4, Op.arith_shift_right, 96, Op.bitwise_and)
    tt(v("nearf", 0, P0), v("nsh"), v("nearI"), Op.add)
    cp(v("near16", 0, P0), v("nearf", 0, P0))
    ts(v("wt", 2, 512, 16), v("whi"), PB, Op.add, 1 / 16, Op.mult)
    ts(v("wt", 3, 512, 16), v("whi"), 0.0, Op.mult, MF_, Op.add)
    ts(col(13), row(5), -8.5 / 16, Op.mult, row(6), Op.add)
    for a in sorted({128 * p[-1][0] + 15 for p in PARTS}):
        ts(v("tq1", a, a + 1), row(2), -34.0, Op.mult, col(13), Op.add)
    ts(v("tr"), v("i32k"), MF_, Op.add, float(R), Op.add)
    stage[0] = ""
    for t in range(RO - 1):
        cp(v("ab16", 384 * t, 384 * t + 384), v("abI", 384 * t, 384 * t + 384))
    stage[0] = "late"
    mm(v("p1"), v("d14"), v("vhi"), True, False)
    mm(v("p1"), v("d15"), v("vlo"), False, True)
    act(v("vst0"), v("p1"))
    for t in range(1, RO):
        ts(col(24 + t), C14, 2.0 * t, Op.mult)
        if CONST[11] == "v":
            ts(v("vst%d" % t), v("vst0"), col(24 + t), Op.add)
        else:
            act(v("vst%d" % t), v("vst0"), Fn.Identity, bias=col(24 + t))

    stage[0] = "home"
    for i, q in enumerate(HOME):
        a, b = 64 * i, min(P0, 64 * i + 64)
        copy(q, v("xg", 16 * a, 16 * b), ind(v("x2", 0, R0), v("post16", a, b)))
        in_turn("home", q)
    for c in range(4):
        a, b = 128 * c, min(P0, 128 * c + 128)
        mms([(v("p%d" % (4 + c % 3), a, b), fam("hm", m), v("xg", 16 * a + m, 16 * b, 16), m == 0, m == 15) for m in range(16)])
        tt(v("live", a, b), v("slot", a, b), v("p%d" % (4 + c % 3), a, b), Op.is_equal)

    stage[0] = "prep"
    for k in range(2):
        whole = v("abI", 384 * k + 384, 384 * k + 768)
        cp(v("abh", 768 * k, 768 * k + 384), whole)
        tt(v("abh", 768 * k + 384, 768 * k + 768), whole, v("abh", 768 * k, 768 * k + 384), Op.subtract)
        ts(col(27 + k), row(2 * k), 1.0, Op.mult, row(2 * k + 1), Op.add)
        times(CONST[10], v("cw%d" % (k + 1)), v("e16"), col(27 + k))
    for k in range(4):
        dma("y", (T["x2"][k:128:16, 0:R0], [("x2", k, R0, 4)]), v("abh", 384 * k, 384 * k + 384), 1e5)
    fill(col(29), -7.5)
    act(v("pm"), v("postf", 0, P0), Fn.Identity, bias=col(29))
    ts(v("h16"), v("pm"), MAGIC, Op.add, MAGIC, Op.subtract)
    mm(v("p5", 0, P0), v("d384"), v("postf", 0, P0), True, False)
    mm(v("p5", 0, P0), v("dneg"), v("h16"), False, True)
    cp(v("w16", 0, P0), v("p5", 0, P0))
    stage[0] = "home"

    def count_full(n, k):
        scan(v("scan", 0, n), v("full", 0, n), v("sd1", 0, n), 0.0, Op.add, Op.max)
        for h in range(2):
            if FULLQ[k] == "v" and h:
                ts(v("junk1", 0, n), v("scan", 0, n), HB[h], Op.is_le, 2.0, Op.mult)
                red(col(30), v("junk1", 0, n), Op.add)
                ts(v("cm1", 0, 1), col(30), float(-n), Op.add)
            else:
                act(v("junk%d" % h, 0, n), v("scan", 0, n), Fn.Sign, bias=HB[h], scale=-1.0, accum=v("cm%d" % h, 0, 1))

    def p0(a, b):
        return v("p0", a, b)

    def p1(a, b):
        return v("p1", a, b)

    def above(q, out, a):
        if q == "v":
            mms([(v("p6", m, 512, 16), v("ident"), a, True, True) for m in range(16)])
            tt(v(out), v("xs"), v("p6"), Op.max)
        else:
            mms([(v("p6"), v("ident"), v("xs"), True, False)] + [(v("p6", m, 512, 16), v("nident"), a, False, m == 15) for m in range(16)])
            act(v(out), v("p6"), Fn.Relu)

    def row_list(out, one):
        mm(p0(0, 2), v("ident"), v("kd", 0, 2), True, False)
        mms([(p0(0, 2), fam("em", j), v(one, j, 32, 16), False, j == 15) for j in range(16)])
        cp(v(out), p0(0, 2))

    mm(v("p0", 0, P0), v("bo"), v("live", 0, P0), True, True)
    ts(v("full", 0, P0), v("p0", 0, P0), 13.5, Op.is_ge)
    count_full(P0, 0)
    for t in range(RO):
        nq = P0 + SP * t
        ne = max(P0, nq - SP)
        last = t == RO - 1
        xa = ["hh", "x1", "x2"][t]
        xb = ["x1", "x2", "x2"][t]
        Xa = v(xa, 0, R)
        Xb = v(xb, 0, R)
        tab, plr, pls, lst, bw, mf, arr = [n + str(t) for n in ("tab", "plr", "pls", "lst", "bw", "mf", "arr")]
        pl16, lq16 = v(lst, 8, 10), v(lst, 0, 8)
        bs = v(bw, 32 * r, 32 * r + 32)
        chunks = [(128 * c, min(nq, 128 * c + 128)) for c in range(4)]
        halves = [(0, 0, 256, chunks[0:2]), (1, 256, nq, chunks[2:4])]
        parts = [(h, chunks[p[0]][0], chunks[p[-1]][1], [chunks[c] for c in p]) for h, p in enumerate(PARTS[t])]

        def absorb():
            stage[0] = "absorb"
            own = R0 - 512 * HELP[t]
            for a in range(0, R0, 512):
                which = ind(Xa, v("ab16", 384 * t + a // 16, 384 * t + a // 16 + 32))
                if a < own:
                    tt(v(xb, a, a + 512), which, v("xd", a, a + 512), Op.max)
                else:
                    act(v(xb, a, a + 512), which)
                    in_turn("absorb", t)
                    if t and a >= 512 * EARLY:
                        ops[-1]["dep"].setdefault(mark[0], False)
                    elif t and FOLD[2 * t]:
                        ops[near[0][1]]["dep"][len(ops) - 1] = False
                    if not FOLD[2 * t] or (t and a >= 512 * EARLY):
                        tt(v(xb, a, a + 512), v(xb, a, a + 512), v(xa, a, a + 512), Op.max)
                    elif todo[0][1][2] == a + 512:
                        fold(xa)
            if t == 0 and HELP[1] < 12:
                dma("y", v("xd", 0, R0 - 512 * HELP[1]), v(xb, 0, R0 - 512 * HELP[1]), 131072 * (12 - HELP[1]))

        stage[:] = ["list", t]
        scan(v("scan", ne, TS), v("full", ne, TS), v("sd1", ne, TS), v("scan", ne - 1, ne), Op.add, Op.max)
        for h in range(2):
            ts(v("cm%d" % h, 1, 1 + TS - ne), v("scan", ne, TS), HB[h], Op.is_le, 2.0, Op.mult)
            red(v("acc", h, h + 1), v("cm%d" % h, 0, 1 + TS - ne), Op.add)
        ts(v(pls), v("acc"), 0.5, Op.mult, ne / 2 + TS * r, Op.add)
        send([v(pls)] * len(others), [v(plr, 2 * place(q), 2 * place(q) + 2) for q in others], [v(plr)], "rp%d" % t)
        ts(pl16, v("acc"), 0.5, Op.mult, ne / 2, Op.add)
        scat(v(tab), v(pls), v("dat", 32 * r, 32 * r + 32))
        stage[0] = "rows"
        copy(MISC[0], v("lp"), ind(v("live"), pl16))
        copy(MISC[1], v("postp"), ind(v("postf"), pl16))
        cp(v("ps16"), v("postp"))
        if t:
            copy(MISC[2], v("cp%d" % t), ind(v("cmf%d" % t), pl16))
            cp(v("cps16"), v("cp%d" % t))
        mm(p0(0, 32), v("px"), v("lp"), True, True)
        ts(v("oa"), p0(0, 32), 0.0, Op.max)
        row_list("lac", "oa")
        if t == 0:
            absorb()
        stage[0] = "tab"
        near = []
        cut = min(max(r, 1), 2)
        for c0, c1 in ((0, cut), (cut, 3)):
            scat(v(tab), v(plr, 2 * c0, 2 * c1), v("dat", 32 * others[c0], 32 * others[c1 - 1] + 32))
        for i, q in enumerate(NEAR[t]):
            stage[0] = "near%d" % i
            step = 32 if q == "v" else 64
            for a in range(64 * i, min(nq, 64 * i + 64), step):
                b = min(nq, a + step)
                copy(q, v("ng", 16 * a, 16 * b), ind(v(tab), v("near16", a, b)))
                in_turn("near", t, q)
                if q == "s":
                    near.append((b, len(ops) - 1))
        stage[0] = "split"
        XS = v("xs")
        if t == 0:
            copy(XSQ[t], XS, ind(Xb, v("ps16")))
        else:
            copy(XSQ[t], XS, ind(Xa, v("ps16")))
            tt(XS, ind(Xa, v("cps16")), XS, Op.max)
        if not last:
            dma("y", v("xg", 16 * nq, 16 * nq + 512), XS, 131072)
        cp(v("ac"), ind(XS, v("lac")))
        above(MAB[0][t], "ma", v("ac"))
        mm(p0(0, 32), v("ck"), v("ones", 0, 32), True, False)
        mm(p0(0, 32), v("ibig"), v("lp"), False, False)
        mms([(p0(0, 32), fam("rx", m), v("xs", m, 512, 16), False, False) for m in range(16)])
        mms([(p0(0, 32), fam("rmp", m), v("ma", m, 512, 16), False, m == 15) for m in range(16)])
        tr(v("ktk"), p0(0, 32))
        scan(v("kts"), v("rst", 0, 32), v("ktk"), 0.0, Op.add, Op.max)
        for h in range(2):
            ts(v("obt", 16 * h, 16 * h + 16), v("ktk", 16 * h, 16 * h + 16), v("kts", 16 * h + 15, 16 * h + 16), Op.is_equal)
        tr(v("ob"), v("obt"))
        row_list("lbc", "ob")
        cp(bs, ind(XS, v("lbc")))
        send([bs] * len(others), [bs] * len(others), [v(bw, 32 * q, 32 * q + 32) for q in others], "rb%d" % t)

        for i, q in enumerate(SLOT[t]):
            stage[0] = "slot%d" % i
            step = 32 if q == "v" else 64
            lo, hi = (ne, nq) if i == 7 else (64 * i, min(ne, 64 * i + 64))
            for a in range(lo, hi, step):
                b = min(hi, a + step)
                XG = v("xg", 16 * a, 16 * b)
                if t == 0:
                    copy(q, XG, ind(Xb, v("post16", a, b)))
                    in_turn("slot", t, q)
                    continue
                which = ind(Xa, v("cmu%d" % t, a, b))
                if q == "v" or i == 7:
                    tt(XG, which, XG, Op.max)
                    in_turn("slot", t, "v")
                else:
                    act(v("mc", 16 * a, 16 * b), which)
                    in_turn("slot", t, q)
                    if not FOLD[2 * t - 1]:
                        for e in range(16 * a, 16 * b, 512):
                            tt(v("xg", e, e + 512), v("mc", e, e + 512), v("xg", e, e + 512), Op.max)
                    elif todo[0][1][2] == 16 * b:
                        fold("mc")

        for h, qa, qb, cs in parts:
            stage[0] = "first%d" % h
            for a, b in cs:
                mm(p1(a - qa, b - qa), v("nsp"), v(tab, TS * r + a, TS * r + b), True, False)
                mms([(p1(a - qa, b - qa), blk("nm", j), v("ng", 16 * a + j, 16 * b, 16), False, j == 15) for j in range(16)])
            relu(RELU[h], v("ff", qa, qb), p1(0, qb - qa))
            later = [i for b, i in near if b > qb]
            for i in later[1:2] if RELU[h] == "s" else ():
                ops[i]["dep"][len(ops) - 1] = False
            nl = (qb - qa) // 16
            mms([(p1(0, nl), fam("e16", k), v("ff", qa + k, qb, 16), k == 0, k == 15) for k in range(16)] +
                [(p1(32 + 8 * i, 40 + 8 * i), v("ff", a, a + 128), v("g8"), True, True) for i, (a, b) in enumerate(cs)])
            ts(v("tgl", qa // 16, qa // 16 + nl), p1(0, nl), -1.0, Op.mult, 128.0, Op.add)
            cp(v("wt", qa, qa + 128 * len(cs), 16), p1(32, 32 + 8 * len(cs)))
            stage[0] = "bt%d" % h
            copy(BTQ[h], v("bt", qa, qb), ind(v(bw), v("tgl", qa // 16, qa // 16 + nl)))
            mark[0] = len(ops) - 1
            for i in later[2:3] if BTQ[h] == "s" else ():
                ops[i]["dep"][len(ops) - 1] = False

        stage[0] = "go"
        above(MAB[1][t], "mb", bs)
        mm(p0(0, 32), v("ck"), v("ones", 0, 32), True, False)
        mm(p0(0, 32), v("ibig"), v("lp"), False, False)
        mms([(p0(0, 32), fam("rmp", m), v("ma", m, 512, 16), False, False) for m in range(16)])
        mms([(p0(0, 32), fam("rmn", m), v("mb", m, 512, 16), False, False) for m in range(16)])
        mm(p0(0, 32), v("bo14p" if MAB[1][t] == "v" else "bo14n"), bs, False, False)
        mm(p0(0, 32), v("bo14n" if MAB[0][t] == "v" else "bo14p"), v("ac"), False, True)
        ts(v("go"), p0(0, 32), 15.5, Op.is_ge)
        ts(v("nog"), p0(0, 32), 15.5, Op.is_lt)
        mm(p0(0, 32), v("px"), v("nog"), True, True)
        if not last:
            tt(v("stay"), v("lp"), v("go"), Op.subtract)
        ts(v("rw"), p0(0, 32), 0.0, Op.max)
        ts(v("rwt"), v("rw"), -8001.0, Op.mult, 1.0, Op.add)
        mm(p0(0, 32), fam("em", 15), v("rw"), True, True)
        tt(v("hw"), v("vst%d" % t, 0, 512, 16), p0(0, 32), Op.add)
        if not last:
            row_list("lrc", "rw")
        stage[0] = "homes"
        tt(v("spa"), v("postp"), v("tr"), Op.subtract)
        tt(v("spb"), v("spa"), v("go"), Op.mult)
        tt(v("spc"), v("spb"), v("tr"), Op.add)
        cp(v("spl16"), v("spc"))
        for a in range(0, 32, 8):
            scat(v("hh"), v("spl16", a, a + 8), v("vst%d" % t, 16 * a, 16 * a + 128))
        cp(v("vm", 32 * r, 32 * r + 32), v("hw"))
        if not last:
            act(v("nearp"), ind(v("nearf"), pl16))
            cp(v("near16", nq, nq + 32), v("nearp"))
            cp(v("nearf", nq, nq + 32), v("nearp"))

        def maxima(q, other, tb, ph, dst, qa, qb, cs):
            w = qb - qa
            for a, b in cs:
                turn(v("p7", a - qa, a - qa + 128, 1, b - a), v(other, a, b), v("ident"))
            for a, b, e in ([(qa, qa + 128, w)] if w % 128 == 0 else [c + (128,) for c in cs]):
                copy(q, v(tb, a, a + e, 1, b - a), v("p7", a - qa, a - qa + e, 1, b - a))
            for a, b in cs:
                turn(v(ph[0], ph[1] + a - qa, ph[1] + b - qa), v(tb, a, a + 128, 1, b - a), v("ident", 0, b - a, 1, b - a))
            for m0 in range(0, 16, 4):
                first = len(ops)
                for m in range(m0, m0 + 4):
                    o = 16 * qa + m * w
                    tt(v(dst, o, o + w), v("xg", 16 * qa + m, 16 * qb, 16), v(ph[0], ph[1], ph[1] + w), Op.max)
                together(first)
                yield range(m0, m0 + 4)

        def sums(pb, qa, m, dst, da, db, a, b, by):
            o = 16 * da + m * (db - da) - da
            return (v(pb, a - qa + m, a - qa + 128, 16, b - a), v(dst, o + a, o + b), v(by), False, False)

        for h, qa, qb, cs in halves:
            stage[0] = "centre%d" % h
            list(maxima(TBQ[0], "ctr", "tb0", ("p2", qa), "mc", qa, qb, cs))
        for h, qa, qb, cs in parts:
            w, wide = qb - qa, 128 * len(cs)
            ph, pb = ("p%d" % (3 - h % 2), 512), "p%d" % (4 + h % 2)
            stage[0] = "dist%d" % h
            mms([(v(pb, 0, wide), v("ones", 0, 128), v("cka", 0, wide), True, False)] +
                [(v(pb, a - qa, a - qa + 128), v("live", a, a + 128), v("ibig"), False, False) for a, b in cs] +
                [(v(pb, a - qa, a - qa + 128, 1, b - a), v("ctr", a, b), v("bo14n"), False, False) for a, b in cs] +
                [sums(pb, qa, m, "mc", *halves[a // 256][1:3], a, b, "rgp") for a, b in cs for m in range(16)])
            mms([(v(pb, a - qa, a - qa + 128, 1, b - a), v("bt", a, b), v("bo14p"), False, False) for a, b in cs])
            for rows in maxima(TBQ[1], "bt", "tb1", ph, "md", qa, qb, cs):
                mms([sums(pb, qa, m, "md", qa, qb, a, b, "rgn") for m in rows for a, b in cs])
            mm(v(pb, 0, wide), v("ones", 0, 128), v("ckb", 0, wide), False, True)

            stage[0] = "offer%d" % h
            best = v("kt", qa + 15, qa + wide, 16)
            kn = v("kn", qa // 16, (qa + wide) // 16)
            scan(v("kt", qa, qa + wide), v("rst", 0, wide), v(pb, 0, wide), 0.0, Op.add, Op.max)
            ts(kn, best, MAGIC, Op.add, MAGIC, Op.subtract)
            ts(v("wt", qa + 7, qa + wide, 16), best, 8.0, Op.is_lt)
            tt(v("wt", qa + 1, qa + wide, 16), best, kn, Op.subtract)
            for a, b in cs:
                turn(v(ph[0], 512 + a - qa, 512 + b - qa), v("wt", a, a + 128, 1, b - a), v("ident", 0, b - a, 1, b - a))
            end = h == len(parts) - 1
            o = qa + 16 * end
            copy(TQQ[h], v("tq%d" % end, o, o + w), v(ph[0], 512, 512 + w))
            keys = v("tq%d" % end, o - end, o + w)
            each = 4 if keys[2] <= 128 else 2
            ms = "lsf" if h == 0 else "ms"
            for k in range(0, 8, each):
                kb = ("p6", pb)[k // each % 2]
                mms([(v(kb, keys[2] * e, keys[2] * (e + 1)), blk("lg", k + e), keys, True, True) for e in range(each)])
                first = len(ops)
                for e in range(each):
                    red(v(ms, k + e, k + e + 1), v(kb, keys[2] * e, keys[2] * (e + 1)), Op.min, True)
                together(first)
            if h:
                tt(v("lsf"), v("lsf"), v("ms"), Op.min)
        if not last:
            stage[0] = "count"
            scat(v("live"), pl16, v("stay"))
            mm(p1(0, nq), v("bo"), v("live", 0, nq), True, True)
            act(v("cnt", 0, nq), p1(0, nq), Fn.Identity, bias=col(31))
            scat(v("ctr"), pl16, v("ac"))
            cp(v("ctr", nq, nq + 32), bs)
        stage[0] = "offer%d" % (len(parts) - 1)
        ts(v("ls16"), v("lsf"), -8.5, Op.add)
        copy(MISC[3], v(mf), ind(v("xg"), v("ls16")))
        send([v(mf, 32 * q, 32 * q + 32) for q in others],
             [v(arr, 32 * place(q), 32 * place(q) + 32) for q in others], [v(arr)], "rm%d" % t)

        stage[0] = "book"
        ts(v("lqf"), v("lsf"), MAGIC, Op.add, MAGIC, Op.subtract)
        ts(lq16, v("lqf"), 1 / 16, Op.mult, -1.0, Op.add)
        if not last:
            scat(v("gone%d" % t), lq16, v("ones", 0, 128))
            tt(v("full", 0, nq), v("cnt", 0, nq), v("gone%d" % t, 0, nq), Op.is_gt)
            count_full(nq, t + 1)
        stage[0] = "live"
        tt(v("lmf"), v("lsf"), v("lqf"), Op.subtract)
        ts(v("lm16"), v("lmf"), 7.5, Op.add)
        act(v("oh"), ind(v("r16"), v("lm16")))
        if not last:
            act(v("lgt"), ind(v("live"), lq16))
            tt(v("lval"), v("lgt"), v("oh"), Op.subtract)
            scat(v("live"), lq16, v("lval"))
            relu("v", v("own"), v(mf, 32 * r, 32 * r + 32))
            scat(v("xg", 16 * nq, 16 * nq + 512), v("lrc"), v("own"))
        stage[0] = "copy"
        act(v("pg"), ind(v("postf"), lq16))
        tt(v("pgm"), v("pg"), v("oh"), Op.mult)
        mm(p1(0, 32), v("bofn"), v("pgm", 32 * r, 32 * r + 32), True, True)
        mms([(p1(128, 256), v("bof"), v("pgm"), True, False), (p1(128, 256), v("ident"), v("away"), False, True)])
        tt(v("fa", 96, 128), v(mf, 32 * r, 32 * r + 32), p1(0, 32), Op.min)
        scan(v("rlf"), v("rst", 0, 128), p1(128, 256), 0.0, Op.add, Op.max)
        cp(v("rl16"), v("rlf", 15, 128, 16))
        scat(v("hh"), v("rl16"), v("vm"))
        mms([(p1(32 * k, 32 * k + 32), v("ident"), v("hw"), True, True) for k in range(3)])
        ts(v("hd"), p1(0, 96), -255.0, Op.add, N14, Op.mult)
        if t == 0:
            stage[0] = "comp"
            for i, q in enumerate(COMP):
                a, b = 64 * i, min(P0, 64 * i + 64)
                copy(q, v("ng", 16 * a, 16 * b), ind(v("x2", 0, R0), v("w16", a, b)))
                ops[-1]["dep"].setdefault(mark[0], False)
                in_turn("comp", q)
            for k in (1, 2):
                for c in range(4):
                    a, b = 128 * c, min(P0, 128 * c + 128)
                    pb = v("p%d" % (4 + (c + k) % 3), a, b)
                    mms([(pb, fam("cw%d" % k, m), v("ng", 16 * a + m, 16 * b, 16), m == 0, m == 15) for m in range(16)])
                    copy(CONST[11 + k], v("cmf%d" % k, a, b), pb)
                    cp(v("cmu%d" % k, a, b), v("cmf%d" % k, a, b))
        if t == 1:
            absorb()
        stage[0] = "copy"
        for k in range(t + 1, RO):
            act(v("cp%d" % k), ind(v("cmf%d" % k), pl16))
            act(v("pgc", 0, 32), ind(v("cmf%d" % k), v(lst, 2 * r, 2 * r + 2)))
            tt(v("cd"), v("pgc", 0, 32), v("pg", 32 * r, 32 * r + 32), Op.subtract)
            tt(v("cd"), v("cd"), v("oh", 32 * r, 32 * r + 32), Op.mult)
            mm(p1(0, 32), v("bof"), v("cd"), True, True)
            tt(v("ce%d" % k), p1(0, 32), v("cp%d" % k), Op.subtract)
        if last:
            dma("y", (T.yh[0:16:2, :], []), (T["hh"][14:128:16, 0:R0], [("hh", 0, R0, 1)]), 1e5)
            dma("s", (T.yh[1:16:2, :], []), (T["hh"][15:128:16, 0:R0], [("hh", 0, R0, 1)]), 1e5)
            dma("y", (T.ypost[:, 0:nq], []), v("postf", 0, nq), 2.5e5)
            times("s", v("ya1", 0, 192), v("x2", R0, R0 + 192), CF)
            times("s", v("ya2", 0, 192), v("hh", R0, R0 + 192), N14)
            tt(v("ya3", 0, 192), v("ya1", 0, 192), v("ya2", 0, 192), Op.add)
            dma("s", (T.ya[:, 0:192], []), v("ya3", 0, 192), 5e4)

        stage[0] = "moves"
        if not last:
            mms([(p0(0, 32), v("bo64k"), v("go"), True, False), (p0(0, 32), v("ident"), v(mf, 32 * r, 32 * r + 32), False, False)])
            mms([(p0(0, 32), v("ident"), v(arr, 32 * k, 32 * k + 32), False, k == 2) for k in range(3)])
            ts(v("full", nq, nq + 32), p0(0, 32), 13 * 65536.0 - 28000, Op.is_ge)
            for b in ("x1", "x2")[t:]:
                relu(MISC[4], v(b, R0 + 96 * t, R0 + 96 * t + 96), v(arr))
        tt(v("fa", 0, 96), v(arr), v("atab%d" % t), Op.min)
        tt(v("wc"), v("fa", 0, 64), v("fa", 64, 128), Op.max)
        tt(v("wv"), v("wc", 0, 32), v("wc", 32, 64), Op.max)
        stage[0] = "win"
        tt(v("rwf"), v("wv"), v("rwt"), Op.is_ge)
        tt(v("wd"), v("wv"), v("postp"), Op.add)
        tt(v("we"), v("wd"), v("rwf"), Op.mult)
        tt(v("postf", nq, nq + 32), v("postp"), v("we"), Op.subtract)
        for k in range(t + 1, RO):
            tt(v("cs1"), v("ce%d" % k), v("wv"), Op.subtract)
            tt(v("cu"), v("cs1"), v("rwf"), Op.mult)
            tt(v("cmf%d" % k, nq, nq + 32), v("cu"), v("cp%d" % k), Op.add)
            cp(v("cmu%d" % k, nq, nq + 32), v("cmf%d" % k, nq, nq + 32))
        if last:
            for k in range(0, 96, 32):
                tt(v("eq", k, k + 32), v("atab%d" % t, k, k + 32), v("wv"), Op.is_equal)
        else:
            mms([(p1(32 * k, 32 * k + 32), v("identf"), v("wv"), True, True) for k in range(3)])
            tt(v("eq"), v("atab%d" % t), p1(0, 96), Op.is_equal)
        tt(v("eh"), v("eq"), v("hd"), Op.mult)
        if not last:
            tt(v("live", nq, nq + 32), v("go"), v("rwf"), Op.add)
            cp(v("post16", nq, nq + 32), v("postf", nq, nq + 32))
            ts(v("hh", R0 + 96 * t, R0 + 96 * t + 96), v("eh"), 255.0, Op.add)
        else:
            dma("y", (T.ypost[:, nq:512], []), v("postf", nq, 512), 2e4)
            ts(v("ya1", 192, 288), v(arr), N255, Op.max)
            tt(v("ya3", 192, 288), v("ya1", 192, 288), v("eh"), Op.add)
            dma("s", (T.ya[:, 192:288], []), v("ya3", 192, 288), 3e4)
    emit()
